import numpy as np
import ml_dtypes


def mxq(x, axis, fmt="e4m3"):
    dtype, down = {"e4m3": (ml_dtypes.float8_e4m3fn, 7), "e5m2": (ml_dtypes.float8_e5m2, 14)}[fmt]
    v = np.moveaxis(np.asarray(x, np.float32).astype(ml_dtypes.bfloat16).astype(np.float64), axis, -1)
    blocks = v.reshape(v.shape[:-1] + (-1, 32))
    amax = np.abs(blocks).max(-1, keepdims=True)
    byte = np.maximum(np.where(amax > 0, np.frexp(amax)[1] - 1 + 127, 0) - down, 1)
    scale = np.exp2(byte - 127.0)
    codes = (blocks / scale).astype(np.float32).astype(dtype).astype(np.float64)
    return np.moveaxis((codes * scale).reshape(v.shape), -1, axis)


WIDE = False


def mx_kscale(k):
    if not WIDE:
        return np.ones(k)
    levels = np.array([10, -10, 5, -5, 0])
    if k % 512:
        return np.exp2(np.random.permutation(np.resize(levels, k // 32))).repeat(32)
    a = np.empty((k // 512, 16))
    for p in range(k // 512):
        a[p, :8] = np.random.permutation(np.resize(levels, 8))
        for g in range(8):
            far = levels[np.abs(levels - a[p, g]) >= 10]
            a[p, g + 8] = far[np.random.randint(len(far))]
    return np.exp2(a.ravel()).repeat(32)


def f64(x):
    return np.asarray(x).astype(np.float64)


def striped(idx):
    return np.tile(idx.reshape(-1, 16).T, (8, 1)).astype(np.uint16)


def unstriped(offs):
    return offs[:16].T.reshape(-1).astype(np.int64)


def gelu(v):
    return 0.5 * v * (1.0 + np.tanh(np.sqrt(2.0 / np.pi) * (v + 0.044715 * v**3)))


K, T, E, C, H, N = 1024, 1536, 4, 256, 512, 256


def by_expert(wq, xq):
    return np.concatenate([wq[e].T @ xq[:, e * C:(e + 1) * C] for e in range(E)], axis=1)


def setup_inputs():
    n = np.random.standard_normal
    s = mx_kscale(K)[:, None]
    u = mx_kscale(H)
    return {
        "xT": (n((K, T)) * s).astype(np.float32),
        "xr": n((N, T)).astype(np.float32),
        "w1": (n((E, K, H)) / np.sqrt(K) / s[None]).astype(np.float32),
        "w3": (n((E, K, H)) / np.sqrt(K) / s[None] * u[None, None, :]).astype(np.float32),
        "w2": (n((E, H, N)) / np.sqrt(H) / u[None, :, None]).astype(np.float32),
        "gate": np.tile(np.random.uniform(0.2, 1.0, E * C), (N, 1)).astype(np.float32),
        "offs": striped(np.random.permutation(T)[:E * C]),
    }


def reference(xT, xr, w1, w3, w2, gate, offs):
    idx = unstriped(offs)
    xq = mxq(f64(xT)[:, idx], 0, "e4m3")
    h = gelu(by_expert(mxq(f64(w1), 1, "e4m3"), xq))
    h = h * by_expert(mxq(f64(w3), 1, "e4m3"), xq)
    y = by_expert(mxq(f64(w2), 1, "e4m3"), mxq(h, 0, "e4m3"))
    out = f64(xr).copy()
    out[:, idx] += f64(gate) * y
    return out

@@ -1,0 +1,290 @@
+import concourse.mybir as mybir
+
+K, T, E, C, H, N = 1024, 1536, 4, 256, 512, 256
+FLOPS = 2 * E * C * (2 * K * H + H * N)
+BYTES = 4 * (K * T + N * T + 2 * E * K * H + E * H * N + E * C + N * T) + 2 * 128 * E * C // 16
+
+F32 = mybir.dt.float32
+BF16 = mybir.dt.bfloat16
+U32 = mybir.dt.uint32
+U16 = mybir.dt.uint16
+U8 = mybir.dt.uint8
+FP8X4 = mybir.dt.float8_e4m3fn_x4
+MULT, ADD = mybir.AluOpType.mult, mybir.AluOpType.add
+GELU = mybir.ActivationFunctionType.Gelu_apprx_tanh
+
+P = 128
+PASSES = K // 512
+TC = 512
+V_SHARE = {("w1", 0, 1): 40, ("w3", 0, 1): 40, ("w1", 1, 1): 40, ("w3", 1, 1): 40, ("w1", 2, 1): 40, ("w3", 2, 1): 40, ("w1", 3, 1): 40, ("w3", 3, 1): 64}
+SINGLE = (("w3", 3),)
+LOOKAHEAD = 8
+
+
+def tile_moe_res_glu_gelu_kernel(tc, xT, xr, w1, w3, w2, gate, offs, out):
+    nc = tc.nc
+    with (
+        tc.tile_pool(name="held", bufs=1) as held,
+        tc.tile_pool(name="rawp", bufs=11) as rawp,
+        tc.tile_pool(name="grp", bufs=3) as grp,
+        tc.tile_pool(name="codes", bufs=2) as codes,
+        tc.tile_pool(name="work", bufs=2) as work,
+        tc.psum_pool(name="psum", bufs=1) as psum,
+    ):
+        offsets = held.tile([P, E * C // 16], U16, name="offsets")
+        warm = held.tile([P, 8], F32, name="warm")
+        tok_words = [held.tile([P, T], U32, name=f"tok_words{s}", align_bytes=64) for s in range(PASSES)]
+        tok_bytes = held.tile([P, T], U8, name="tok_bytes", align_bytes=64)
+        win = [held.tile([P, T], F32, name=f"win{b}") for b in range(2)]
+        late = {}
+        out_sb = [held.tile([P, T], F32, name=f"out_sb{b}") for b in range(2)]
+
+        chunks = [("x", 0, s, c) for s in range(PASSES) for c in range(T // TC)]
+        for e in range(E):
+            chunks += [("w1", e, 0, 0), ("w1", e, 1, 0), ("w3", e, 0, 0)]
+            chunks += [("w2", e, 0, 0), ("w3", e, 1, 0)] if e < E - 1 else [("w3", e, 1, 0), ("w2", e, 0, 0)]
+        raws, groups, weights = {}, {}, {}
+        first_layer_in = {"w1": w1, "w3": w3}
+
+        def load(i):
+            kind, e, s, c = chunks[i]
+            if kind == "x":
+                raw = rawp.tile([P, 4, TC], F32, name="raw")
+                nc.sync.dma_start(raw[:], xT[s * 512 : (s + 1) * 512, c * TC : (c + 1) * TC].rearrange("(p j) t -> p j t", j=4))
+            elif kind == "w2":
+                raw = rawp.tile([P, 4, N], F32, name="raw2", tag="raw")
+                nc.sync.dma_start(raw[:], w2[e].rearrange("(p j) n -> p j n", j=4))
+            else:
+                raw = rawp.tile([P, 4, H], F32, name="raw")
+                nc.sync.dma_start(raw[:], first_layer_in[kind][e, s * 512 : (s + 1) * 512, :].rearrange("(p j) c -> p j c", j=4))
+            raws[i] = raw
+            if i == 0:
+                nc.sync.dma_start(offsets[:], offs)
+            if chunks[i] == ("w3", 1, 0, 0):
+                late["gate"] = grp.tile([P, E * C], F32, name="gate_sb", tag="tok_grouped", align_bytes=64)
+                nc.sync.dma_start(late["gate"][:], gate[0:P, :])
+            if i == len(chunks) - 1:
+                for b in range(2):
+                    late[b] = rawp.tile([P, T], F32, name=f"xr_sb{b}", tag="raw")
+                    nc.sync.dma_start(late[b][:], xr[b * P : (b + 1) * P, :])
+
+        def share(dst, src, cut, whole):
+            if cut:
+                nc.vector.tensor_copy(dst[:, :cut], src[:, :cut])
+            if cut < whole:
+                nc.scalar.copy(dst[:, cut:], src[:, cut:])
+
+        def interleave(i):
+            kind, e, s, c = chunks[i]
+            raw = raws.pop(i)
+            if kind == "x":
+                grouped = grp.tile([P, TC, 4], BF16, name="tok_grouped", align_bytes=64)
+                share(grouped[:].rearrange("p (c i) j -> p c j i", i=4), raw[:].rearrange("p j (c i) -> p c j i", i=4), 128 // 4, TC // 4)
+            elif kind == "w2":
+                grouped = grp.tile([P, N, 4], BF16, name="w2_grouped", bufs=2, align_bytes=64)
+                share(grouped[:].rearrange("p (c i) j -> p c j i", i=4), raw[:].rearrange("p j (c i) -> p c j i", i=4), 256 // 4, N // 4)
+            else:
+                if s == 0:
+                    groups[kind, e] = grp.tile([P, 2, 4, 128, 4], BF16, name="w_grouped", align_bytes=64)
+                grouped = groups[kind, e][:, s]
+                m_v = V_SHARE.get(chunks[i][:3], 0)
+                share(grouped.rearrange("p t m j -> p m j t"), raw[:].rearrange("p j (m t) -> p m j t", t=4), m_v, 128)
+            groups[i] = grouped
+
+        def quantize(i):
+            kind, e, s, c = chunks[i]
+            grouped = groups.pop(i)
+            if kind == "x":
+                nc.vector.quantize_mx(
+                    out=tok_words[s][:, c * TC : (c + 1) * TC].bitcast(FP8X4),
+                    scales=tok_bytes[4 * s : P, c * TC : (c + 1) * TC],
+                    in_=grouped[:].rearrange("p t j -> p (t j)"),
+                )
+                return
+            if kind == "w2":
+                words = codes.tile([P, N], U32, name="w2_words", align_bytes=64)
+                scales = codes.tile([P, N], U8, name="w2_scales", align_bytes=64)
+                flat = grouped[:].rearrange("p n j -> p (n j)")
+            else:
+                if (kind, e) not in weights:
+                    words = codes.tile([P, PASSES * H], U32, name=f"{kind}_words", align_bytes=64)
+                    scales = codes.tile([P, PASSES * H], U8, name=f"{kind}_scales", align_bytes=64)
+                    weights[kind, e] = (words, scales)
+                both = groups[kind, e]
+                if (kind, e) in SINGLE:
+                    words, scales = (t[:, s * H : (s + 1) * H] for t in weights[kind, e])
+                    nc.vector.quantize_mx(out=words.bitcast(FP8X4), scales=scales, in_=both[:, s].rearrange("p t m j -> p (t m j)"))
+                else:
+                    words, scales = weights[kind, e]
+                    nc.vector.quantize_mx(out=words[:].bitcast(FP8X4), scales=scales[:], in_=both[:].rearrange("p s t m j -> p (s t m j)"))
+                return
+            nc.vector.quantize_mx(out=words[:].bitcast(FP8X4), scales=scales[:], in_=flat)
+            weights[kind, e] = (words, scales)
+
+        gathered, banks, gelus, hidden, ys, ygs = {}, {}, {}, {}, {}, {}
+
+        def idx(e, n=1):
+            return offsets[:, e * 16 : (e + n) * 16]
+
+        def gather_words(es, s):
+            gw = work.tile([P, len(es) * C], U32, name=f"g_words{s}_{es[0]}", bufs=1, align_bytes=64)
+            nc.vector.tensor_copy(gw[:], tok_words[s][:].indirect(idx(es[0], len(es))))
+            for q, e in enumerate(es):
+                gathered[e, s] = gw, q * C
+
+        def gather_bytes(es):
+            gb = work.tile([P, len(es) * C], U8, name=f"g_bytes_{es[0]}", bufs=1, align_bytes=64)
+            nc.vector.tensor_copy(gb[:], tok_bytes[:].indirect(idx(es[0], len(es))))
+            for q, e in enumerate(es):
+                gathered[e, "bytes"] = gb
+
+        def first_layer(kind, e, half):
+            bank = psum.tile([P, 4, 128], F32, name=f"bank_{kind}", bufs=3)
+            for t in range(4):
+                for s in range(PASSES):
+                    words, scales = weights[kind, e]
+                    m_cols = slice(s * H + t * 128, s * H + (t + 1) * 128)
+                    gw, first = gathered[e, s]
+                    cols = slice(first + half * 128, first + (half + 1) * 128)
+                    nc.tensor.matmul_mx(
+                        out=bank[:, t, :],
+                        lhsT=words[:, m_cols].bitcast(FP8X4),
+                        lhsT_scale=scales[:, m_cols],
+                        rhs=gw[:, cols].bitcast(FP8X4),
+                        rhs_scale=gathered[e, "bytes"][4 * s : P, cols],
+                        start=s == 0,
+                        stop=s == PASSES - 1,
+                    )
+            banks[kind, half] = bank
+
+        def gelu(half):
+            ga = work.tile([P, 128, 4], F32, name="ga", bufs=3)
+            nc.scalar.activation(ga[:], banks["w1", half][:].rearrange("p t n -> p n t"), GELU)
+            gelus[half] = ga
+
+        def product(half):
+            if half == 0:
+                hidden["h"] = work.tile([P, C, 4], BF16, name="h", align_bytes=64)
+            nc.vector.tensor_tensor(
+                hidden["h"][:, half * 128 : (half + 1) * 128, :], banks["w3", half][:].rearrange("p t n -> p n t"), gelus[half][:], MULT
+            )
+
+        def second_layer(e, first, n):
+            if first == 0:
+                hidden["q"] = (
+                    work.tile([P, C], U32, name="h_words", align_bytes=64),
+                    work.tile([P, C], U8, name="h_scales", align_bytes=64),
+                )
+                ys[e] = psum.tile([P, 2, C], F32, name="y", bufs=2)
+            cols = slice(first, first + n)
+            h_words, h_scales = hidden["q"]
+            nc.vector.quantize_mx(out=h_words[:, cols].bitcast(FP8X4), scales=h_scales[:, cols], in_=hidden["h"][:, cols, :].rearrange("p n t -> p (n t)"))
+            words, scales = weights["w2", e]
+            for b in range(2):
+                nc.tensor.matmul_mx(
+                    out=ys[e][:, b, cols],
+                    lhsT=words[:, b * 128 : (b + 1) * 128].bitcast(FP8X4),
+                    lhsT_scale=scales[:, b * 128 : (b + 1) * 128],
+                    rhs=h_words[:, cols].bitcast(FP8X4),
+                    rhs_scale=h_scales[:, cols],
+                    start=True,
+                    stop=True,
+                )
+
+        def weigh(e, blocks):
+            for b in blocks:
+                yg = work.tile([P, C], F32, name=f"yg{b}")
+                nc.vector.tensor_tensor(yg[:], ys[e][:, b, :], late["gate"][:, e * C : (e + 1) * C], MULT)
+                ygs[e, b] = yg
+
+        def scatter(e, b):
+            nc.vector.tensor_copy(win[b][:].indirect(idx(e)), ygs[e, b][:])
+
+        def finish(b, engines):
+            cuts = (0, 1024, 1536)
+            for engine, c0, c1 in zip(engines, cuts[:-1], cuts[1:]):
+                cols = slice(c0, c1)
+                engine.tensor_tensor(out_sb[b][:, cols], win[b][:, cols], late[b][:, cols], ADD)
+                nc.sync.dma_start(out[b * P : (b + 1) * P, cols], out_sb[b][:, cols])
+
+        for i in range(LOOKAHEAD):
+            load(i)
+        nc.gpsimd.memset(tok_bytes[:], 0)
+        nc.vector.memset(warm[:], 0.0)
+        for b in range(2):
+            nc.vector.memset(win[b][:], 0.0)
+        nc.scalar.activation(warm[:], warm[:], GELU)
+
+        pos = {c: i for i, c in enumerate(chunks)}
+
+        def X(kind, e, s=0, c=0):
+            i = pos[kind, e, s, c]
+            interleave(i)
+            if i + LOOKAHEAD < len(chunks):
+                load(i + LOOKAHEAD)
+
+        def Q(kind, e, s=1, c=0):
+            quantize(pos[kind, e, s, c])
+
+        for i in range(6):
+            X("x", 0, i // 3, i % 3)
+            if i > 0:
+                Q("x", 0, (i - 1) // 3, (i - 1) % 3)
+            if i == 4:
+                gather_words((0,), 0)
+        X("w1", 0, 0)
+        Q("x", 0, 1, 2)
+        gather_words((0,), 1)
+        gather_bytes((0,))
+        X("w1", 0, 1)
+        gather_words((1, 2, 3), 0)
+        Q("w1", 0)
+        first_layer("w1", 0, 0)
+        first_layer("w1", 0, 1)
+        X("w3", 0, 0)
+        gather_words((1, 2, 3), 1)
+        X("w2", 0)
+        X("w3", 0, 1)
+        gelu(0)
+        gelu(1)
+        Q("w3", 0)
+        first_layer("w3", 0, 0)
+        first_layer("w3", 0, 1)
+        gather_bytes((1, 2, 3))
+        for e in range(1, E):
+            last = e == E - 1
+            X("w1", e, 0)
+            if e > 1:
+                scatter(e - 2, 1)
+            product(0)
+            product(1)
+            Q("w2", e - 1, 0)
+            second_layer(e - 1, 0, C)
+            X("w1", e, 1)
+            Q("w1", e)
+            first_layer("w1", e, 0)
+            first_layer("w1", e, 1)
+            X("w3", e, 0)
+            weigh(e - 1, (0, 1))
+            if e < E - 1:
+                X("w2", e)
+            scatter(e - 1, 0)
+            if ("w3", e) in SINGLE:
+                Q("w3", e, 0)
+            X("w3", e, 1)
+            gelu(0)
+            gelu(1)
+            Q("w3", e)
+            first_layer("w3", e, 0)
+            first_layer("w3", e, 1)
+        X("w2", E - 1)
+        scatter(E - 2, 1)
+        product(0)
+        product(1)
+        Q("w2", E - 1, 0)
+        second_layer(E - 1, 0, C)
+        weigh(E - 1, (0, 1))
+        for b in range(2):
+            scatter(E - 1, b)
+        finish(0, (nc.vector, nc.vector))
+        finish(1, (nc.vector, nc.vector))

@@ -16,8 +16,9 @@ GELU = mybir.ActivationFunctionType.Gelu_apprx_tanh
 P = 128
 PASSES = K // 512
 TC = 512
-V_SHARE = {("w1", 0, 1): 40, ("w3", 0, 1): 40, ("w1", 1, 1): 40, ("w3", 1, 1): 40, ("w1", 2, 1): 40, ("w3", 2, 1): 40, ("w1", 3, 1): 40, ("w3", 3, 1): 64}
-SINGLE = (("w3", 3),)
+V_TOKENS = 20
+V_FIRST = 16
+V_LAST = 42
 LOOKAHEAD = 8
 
 
@@ -26,7 +27,7 @@ def tile_moe_res_glu_gelu_kernel(tc, xT, xr, w1, w3, w2, gate, offs, out):
     with (
         tc.tile_pool(name="held", bufs=1) as held,
         tc.tile_pool(name="rawp", bufs=11) as rawp,
-        tc.tile_pool(name="grp", bufs=3) as grp,
+        tc.tile_pool(name="grp", bufs=6) as grp,
         tc.tile_pool(name="codes", bufs=2) as codes,
         tc.tile_pool(name="work", bufs=2) as work,
         tc.psum_pool(name="psum", bufs=1) as psum,
@@ -35,14 +36,15 @@ def tile_moe_res_glu_gelu_kernel(tc, xT, xr, w1, w3, w2, gate, offs, out):
         warm = held.tile([P, 8], F32, name="warm")
         tok_words = [held.tile([P, T], U32, name=f"tok_words{s}", align_bytes=64) for s in range(PASSES)]
         tok_bytes = held.tile([P, T], U8, name="tok_bytes", align_bytes=64)
+        slot_words = [held.tile([P, E * C], U32, name=f"slot_words{s}", align_bytes=64) for s in range(PASSES)]
+        slot_bytes = held.tile([P, E * C], U8, name="slot_bytes", align_bytes=64)
+        gate_sb = held.tile([P, E * C], F32, name="gate_sb")
         win = [held.tile([P, T], F32, name=f"win{b}") for b in range(2)]
-        late = {}
-        out_sb = [held.tile([P, T], F32, name=f"out_sb{b}") for b in range(2)]
 
         chunks = [("x", 0, s, c) for s in range(PASSES) for c in range(T // TC)]
         for e in range(E):
-            chunks += [("w1", e, 0, 0), ("w1", e, 1, 0), ("w3", e, 0, 0)]
-            chunks += [("w2", e, 0, 0), ("w3", e, 1, 0)] if e < E - 1 else [("w3", e, 1, 0), ("w2", e, 0, 0)]
+            chunks += [("w1", e, 0, 0), ("w1", e, 1, 0), ("w3", e, 0, 0), ("w3", e, 1, 0), ("w2", e, 0, 0)]
+        chunks += [("xr", 0, 0, 0), ("xr", 0, 1, 0)]
         raws, groups, weights = {}, {}, {}
         first_layer_in = {"w1": w1, "w3": w3}
 
@@ -53,159 +55,132 @@ def tile_moe_res_glu_gelu_kernel(tc, xT, xr, w1, w3, w2, gate, offs, out):
                 nc.sync.dma_start(raw[:], xT[s * 512 : (s + 1) * 512, c * TC : (c + 1) * TC].rearrange("(p j) t -> p j t", j=4))
             elif kind == "w2":
                 raw = rawp.tile([P, 4, N], F32, name="raw2", tag="raw")
-                nc.sync.dma_start(raw[:], w2[e].rearrange("(p j) n -> p j n", j=4))
+                rows = w2[e].rearrange("(q t b) n -> b q t n", t=4, b=2)
+                for b in range(2):
+                    nc.sync.dma_start(raw[b:P:2], rows[b])
+            elif kind == "xr":
+                raw = rawp.tile([P, T], F32, name="xr_sb", tag="raw")
+                nc.sync.dma_start(raw[:], xr[s * P : (s + 1) * P, :])
             else:
                 raw = rawp.tile([P, 4, H], F32, name="raw")
                 nc.sync.dma_start(raw[:], first_layer_in[kind][e, s * 512 : (s + 1) * 512, :].rearrange("(p j) c -> p j c", j=4))
             raws[i] = raw
             if i == 0:
                 nc.sync.dma_start(offsets[:], offs)
-            if chunks[i] == ("w3", 1, 0, 0):
-                late["gate"] = grp.tile([P, E * C], F32, name="gate_sb", tag="tok_grouped", align_bytes=64)
-                nc.sync.dma_start(late["gate"][:], gate[0:P, :])
-            if i == len(chunks) - 1:
-                for b in range(2):
-                    late[b] = rawp.tile([P, T], F32, name=f"xr_sb{b}", tag="raw")
-                    nc.sync.dma_start(late[b][:], xr[b * P : (b + 1) * P, :])
+            if i == LOOKAHEAD - 1:
+                nc.sync.dma_start(gate_sb[:], gate[0:P, :])
 
-        def share(dst, src, cut, whole):
+        def share(dst, src, part):
+            cut = dst.shape[1] * part // 64
             if cut:
                 nc.vector.tensor_copy(dst[:, :cut], src[:, :cut])
-            if cut < whole:
+            if part < 64:
                 nc.scalar.copy(dst[:, cut:], src[:, cut:])
 
         def interleave(i):
             kind, e, s, c = chunks[i]
             raw = raws.pop(i)
             if kind == "x":
-                grouped = grp.tile([P, TC, 4], BF16, name="tok_grouped", align_bytes=64)
-                share(grouped[:].rearrange("p (c i) j -> p c j i", i=4), raw[:].rearrange("p j (c i) -> p c j i", i=4), 128 // 4, TC // 4)
+                grouped = grp.tile([P, TC * 4], BF16, name="grouped", align_bytes=64)
+                share(grouped[:].rearrange("p (c b j) -> p c j b", b=2, j=4), raw[:].rearrange("p j (c b) -> p c j b", b=2), V_TOKENS)
             elif kind == "w2":
-                grouped = grp.tile([P, N, 4], BF16, name="w2_grouped", bufs=2, align_bytes=64)
-                share(grouped[:].rearrange("p (c i) j -> p c j i", i=4), raw[:].rearrange("p j (c i) -> p c j i", i=4), 256 // 4, N // 4)
+                grouped = groups.pop("spent")[:, : N * 4]
+                share(grouped.rearrange("p (c b j) -> p c j b", b=2, j=4), raw[:].rearrange("p j (c b) -> p c j b", b=2), 64)
             else:
-                if s == 0:
-                    groups[kind, e] = grp.tile([P, 2, 4, 128, 4], BF16, name="w_grouped", align_bytes=64)
-                grouped = groups[kind, e][:, s]
-                m_v = V_SHARE.get(chunks[i][:3], 0)
-                share(grouped.rearrange("p t m j -> p m j t"), raw[:].rearrange("p j (m t) -> p m j t", t=4), m_v, 128)
+                grouped = grp.tile([P, H * 4], BF16, name="grouped", align_bytes=64)
+                part = V_LAST if chunks[i] == ("w3", E - 1, 1, 0) else V_FIRST if (kind, s) == ("w1", 0) else 0
+                if (kind, s) == ("w3", 1):
+                    groups["spent"] = grouped
+                    raws["spent"] = raw
+                share(
+                    grouped[:].rearrange("p (t q b j) -> p q t j b", t=4, b=2, j=4),
+                    raw[:].rearrange("p j (q t b) -> p q t j b", t=4, b=2),
+                    part,
+                )
             groups[i] = grouped
 
         def quantize(i):
             kind, e, s, c = chunks[i]
             grouped = groups.pop(i)
             if kind == "x":
-                nc.vector.quantize_mx(
-                    out=tok_words[s][:, c * TC : (c + 1) * TC].bitcast(FP8X4),
-                    scales=tok_bytes[4 * s : P, c * TC : (c + 1) * TC],
-                    in_=grouped[:].rearrange("p t j -> p (t j)"),
-                )
-                return
-            if kind == "w2":
-                words = codes.tile([P, N], U32, name="w2_words", align_bytes=64)
-                scales = codes.tile([P, N], U8, name="w2_scales", align_bytes=64)
-                flat = grouped[:].rearrange("p n j -> p (n j)")
+                words, scales = tok_words[s][:, c * TC : (c + 1) * TC], tok_bytes[4 * s : P, c * TC : (c + 1) * TC]
             else:
-                if (kind, e) not in weights:
-                    words = codes.tile([P, PASSES * H], U32, name=f"{kind}_words", align_bytes=64)
-                    scales = codes.tile([P, PASSES * H], U8, name=f"{kind}_scales", align_bytes=64)
-                    weights[kind, e] = (words, scales)
-                both = groups[kind, e]
-                if (kind, e) in SINGLE:
-                    words, scales = (t[:, s * H : (s + 1) * H] for t in weights[kind, e])
-                    nc.vector.quantize_mx(out=words.bitcast(FP8X4), scales=scales, in_=both[:, s].rearrange("p t m j -> p (t m j)"))
-                else:
-                    words, scales = weights[kind, e]
-                    nc.vector.quantize_mx(out=words[:].bitcast(FP8X4), scales=scales[:], in_=both[:].rearrange("p s t m j -> p (s t m j)"))
-                return
-            nc.vector.quantize_mx(out=words[:].bitcast(FP8X4), scales=scales[:], in_=flat)
-            weights[kind, e] = (words, scales)
+                width = N if kind == "w2" else H
+                words = codes.tile([P, width], U32, name=f"{kind}_words{s}", align_bytes=64)[:]
+                scales = codes.tile([P, width], U8, name=f"{kind}_scales{s}", align_bytes=64)[:]
+                weights[kind, e, s] = (words, scales)
+            nc.vector.quantize_mx(out=words.bitcast(FP8X4), scales=scales, in_=grouped[:])
 
-        gathered, banks, gelus, hidden, ys, ygs = {}, {}, {}, {}, {}, {}
+        banks, gelus, hidden, ys = {}, {}, {}, {}
 
-        def idx(e, n=1):
-            return offsets[:, e * 16 : (e + n) * 16]
+        def gather_words(s):
+            nc.vector.tensor_copy(slot_words[s][:], tok_words[s][:].indirect(offsets[:]))
 
-        def gather_words(es, s):
-            gw = work.tile([P, len(es) * C], U32, name=f"g_words{s}_{es[0]}", bufs=1, align_bytes=64)
-            nc.vector.tensor_copy(gw[:], tok_words[s][:].indirect(idx(es[0], len(es))))
-            for q, e in enumerate(es):
-                gathered[e, s] = gw, q * C
-
-        def gather_bytes(es):
-            gb = work.tile([P, len(es) * C], U8, name=f"g_bytes_{es[0]}", bufs=1, align_bytes=64)
-            nc.vector.tensor_copy(gb[:], tok_bytes[:].indirect(idx(es[0], len(es))))
-            for q, e in enumerate(es):
-                gathered[e, "bytes"] = gb
+        def gather_bytes():
+            nc.vector.tensor_copy(slot_bytes[:], tok_bytes[:].indirect(offsets[:]))
 
         def first_layer(kind, e, half):
             bank = psum.tile([P, 4, 128], F32, name=f"bank_{kind}", bufs=3)
+            cols = slice(e * C + half * 128, e * C + (half + 1) * 128)
             for t in range(4):
+                m_cols = slice(t * 128, (t + 1) * 128)
                 for s in range(PASSES):
-                    words, scales = weights[kind, e]
-                    m_cols = slice(s * H + t * 128, s * H + (t + 1) * 128)
-                    gw, first = gathered[e, s]
-                    cols = slice(first + half * 128, first + (half + 1) * 128)
+                    words, scales = weights[kind, e, s]
                     nc.tensor.matmul_mx(
                         out=bank[:, t, :],
                         lhsT=words[:, m_cols].bitcast(FP8X4),
                         lhsT_scale=scales[:, m_cols],
-                        rhs=gw[:, cols].bitcast(FP8X4),
-                        rhs_scale=gathered[e, "bytes"][4 * s : P, cols],
+                        rhs=slot_words[s][:, cols].bitcast(FP8X4),
+                        rhs_scale=slot_bytes[4 * s : P, cols],
                         start=s == 0,
                         stop=s == PASSES - 1,
                     )
             banks[kind, half] = bank
 
         def gelu(half):
-            ga = work.tile([P, 128, 4], F32, name="ga", bufs=3)
-            nc.scalar.activation(ga[:], banks["w1", half][:].rearrange("p t n -> p n t"), GELU)
+            ga = raws["spent"][:, half, :].rearrange("p (n t) -> p n t", t=4)
+            nc.scalar.activation(ga, banks["w1", half][:].rearrange("p t n -> p n t"), GELU)
             gelus[half] = ga
 
         def product(half):
             if half == 0:
                 hidden["h"] = work.tile([P, C, 4], BF16, name="h", align_bytes=64)
             nc.vector.tensor_tensor(
-                hidden["h"][:, half * 128 : (half + 1) * 128, :], banks["w3", half][:].rearrange("p t n -> p n t"), gelus[half][:], MULT
+                hidden["h"][:, half * 128 : (half + 1) * 128, :], banks["w3", half][:].rearrange("p t n -> p n t"), gelus[half], MULT
             )
 
-        def second_layer(e, first, n):
-            if first == 0:
-                hidden["q"] = (
-                    work.tile([P, C], U32, name="h_words", align_bytes=64),
-                    work.tile([P, C], U8, name="h_scales", align_bytes=64),
-                )
-                ys[e] = psum.tile([P, 2, C], F32, name="y", bufs=2)
-            cols = slice(first, first + n)
-            h_words, h_scales = hidden["q"]
-            nc.vector.quantize_mx(out=h_words[:, cols].bitcast(FP8X4), scales=h_scales[:, cols], in_=hidden["h"][:, cols, :].rearrange("p n t -> p (n t)"))
-            words, scales = weights["w2", e]
+        def second_layer(e):
+            h_words = work.tile([P, C], U32, name="h_words", align_bytes=64)
+            h_scales = work.tile([P, C], U8, name="h_scales", align_bytes=64)
+            y = psum.tile([P, 2, C], F32, name="y", bufs=2)
+            nc.vector.quantize_mx(out=h_words[:].bitcast(FP8X4), scales=h_scales[:], in_=hidden["h"][:].rearrange("p n t -> p (n t)"))
+            words, scales = weights["w2", e, 0]
             for b in range(2):
                 nc.tensor.matmul_mx(
-                    out=ys[e][:, b, cols],
+                    out=y[:, b, :],
                     lhsT=words[:, b * 128 : (b + 1) * 128].bitcast(FP8X4),
                     lhsT_scale=scales[:, b * 128 : (b + 1) * 128],
-                    rhs=h_words[:, cols].bitcast(FP8X4),
-                    rhs_scale=h_scales[:, cols],
+                    rhs=h_words[:].bitcast(FP8X4),
+                    rhs_scale=h_scales[:],
                     start=True,
                     stop=True,
                 )
-
-        def weigh(e, blocks):
-            for b in blocks:
-                yg = work.tile([P, C], F32, name=f"yg{b}")
-                nc.vector.tensor_tensor(yg[:], ys[e][:, b, :], late["gate"][:, e * C : (e + 1) * C], MULT)
-                ygs[e, b] = yg
+            ys[e] = y
 
         def scatter(e, b):
-            nc.vector.tensor_copy(win[b][:].indirect(idx(e)), ygs[e, b][:])
+            nc.vector.tensor_copy(win[b][:].indirect(offsets[:, e * 16 : (e + 1) * 16]), ys[e, b][:])
 
-        def finish(b, engines):
-            cuts = (0, 1024, 1536)
-            for engine, c0, c1 in zip(engines, cuts[:-1], cuts[1:]):
+        def weigh(e, b):
+            yg = work.tile([P, C], F32, name=f"yg{b}")
+            nc.vector.tensor_tensor(yg[:], ys[e][:, b, :], gate_sb[:, e * C : (e + 1) * C], MULT)
+            ys[e, b] = yg
+
+        def finish(b):
+            xr_sb = raws.pop(pos["xr", 0, b, 0])
+            for c0, c1 in ((0, 1024), (1024, T)):
                 cols = slice(c0, c1)
-                engine.tensor_tensor(out_sb[b][:, cols], win[b][:, cols], late[b][:, cols], ADD)
-                nc.sync.dma_start(out[b * P : (b + 1) * P, cols], out_sb[b][:, cols])
+                nc.vector.tensor_tensor(xr_sb[:, cols], win[b][:, cols], xr_sb[:, cols], ADD)
+                nc.sync.dma_start(out[b * P : (b + 1) * P, cols], xr_sb[:, cols])
 
         for i in range(LOOKAHEAD):
             load(i)
@@ -217,74 +192,38 @@ def tile_moe_res_glu_gelu_kernel(tc, xT, xr, w1, w3, w2, gate, offs, out):
 
         pos = {c: i for i, c in enumerate(chunks)}
 
-        def X(kind, e, s=0, c=0):
+        def prepare(kind, e, s=0, c=0):
             i = pos[kind, e, s, c]
             interleave(i)
             if i + LOOKAHEAD < len(chunks):
                 load(i + LOOKAHEAD)
+            quantize(i)
 
-        def Q(kind, e, s=1, c=0):
-            quantize(pos[kind, e, s, c])
-
-        for i in range(6):
-            X("x", 0, i // 3, i % 3)
-            if i > 0:
-                Q("x", 0, (i - 1) // 3, (i - 1) % 3)
-            if i == 4:
-                gather_words((0,), 0)
-        X("w1", 0, 0)
-        Q("x", 0, 1, 2)
-        gather_words((0,), 1)
-        gather_bytes((0,))
-        X("w1", 0, 1)
-        gather_words((1, 2, 3), 0)
-        Q("w1", 0)
-        first_layer("w1", 0, 0)
-        first_layer("w1", 0, 1)
-        X("w3", 0, 0)
-        gather_words((1, 2, 3), 1)
-        X("w2", 0)
-        X("w3", 0, 1)
-        gelu(0)
-        gelu(1)
-        Q("w3", 0)
-        first_layer("w3", 0, 0)
-        first_layer("w3", 0, 1)
-        gather_bytes((1, 2, 3))
-        for e in range(1, E):
-            last = e == E - 1
-            X("w1", e, 0)
-            if e > 1:
-                scatter(e - 2, 1)
-            product(0)
-            product(1)
-            Q("w2", e - 1, 0)
-            second_layer(e - 1, 0, C)
-            X("w1", e, 1)
-            Q("w1", e)
-            first_layer("w1", e, 0)
-            first_layer("w1", e, 1)
-            X("w3", e, 0)
-            weigh(e - 1, (0, 1))
-            if e < E - 1:
-                X("w2", e)
-            scatter(e - 1, 0)
-            if ("w3", e) in SINGLE:
-                Q("w3", e, 0)
-            X("w3", e, 1)
-            gelu(0)
-            gelu(1)
-            Q("w3", e)
-            first_layer("w3", e, 0)
-            first_layer("w3", e, 1)
-        X("w2", E - 1)
-        scatter(E - 2, 1)
-        product(0)
-        product(1)
-        Q("w2", E - 1, 0)
-        second_layer(E - 1, 0, C)
-        weigh(E - 1, (0, 1))
+        for s in range(PASSES):
+            for c in range(T // TC):
+                prepare("x", 0, s, c)
+            gather_words(s)
+        gather_bytes()
+        for e in range(E):
+            prepare("w1", e, 0)
+            prepare("w1", e, 1)
+            for half in range(2):
+                first_layer("w1", e, half)
+            if e > 0:
+                scatter(e - 1, 0)
+            prepare("w3", e, 0)
+            if e > 0:
+                scatter(e - 1, 1)
+            prepare("w3", e, 1)
+            for half in range(2):
+                gelu(half)
+            prepare("w2", e)
+            for half in range(2):
+                first_layer("w3", e, half)
+                product(half)
+            second_layer(e)
+            for b in range(2):
+                weigh(e, b)
         for b in range(2):
             scatter(E - 1, b)
-        finish(0, (nc.vector, nc.vector))
-        finish(1, (nc.vector, nc.vector))
+            finish(b)

@@ -1,4 +1,5 @@
 import concourse.mybir as mybir
+from concourse.masks import make_identity
 
 K, T, E, C, H, N = 1024, 1536, 4, 256, 512, 256
 FLOPS = 2 * E * C * (2 * K * H + H * N)
@@ -16,9 +17,12 @@ GELU = mybir.ActivationFunctionType.Gelu_apprx_tanh
 P = 128
 PASSES = K // 512
 TC = 512
-V_TOKENS = 20
-V_FIRST = 16
-V_LAST = 42
+V_TOKENS = 28
+V_SHARE = 40
+V_FIRST = (16, 32)
+V_LAST = 40
+EARLY = 2
+TOKEN_LOADS = ((0, 0, T), (1, 0, 2 * TC), (1, 2 * TC, T))
 LOOKAHEAD = 8
 
 
@@ -26,7 +30,7 @@ def tile_moe_res_glu_gelu_kernel(tc, xT, xr, w1, w3, w2, gate, offs, out):
     nc = tc.nc
     with (
         tc.tile_pool(name="held", bufs=1) as held,
-        tc.tile_pool(name="rawp", bufs=11) as rawp,
+        tc.tile_pool(name="rawp", bufs=10) as rawp,
         tc.tile_pool(name="grp", bufs=6) as grp,
         tc.tile_pool(name="codes", bufs=2) as codes,
         tc.tile_pool(name="work", bufs=2) as work,
@@ -36,24 +40,21 @@ def tile_moe_res_glu_gelu_kernel(tc, xT, xr, w1, w3, w2, gate, offs, out):
         warm = held.tile([P, 8], F32, name="warm")
         tok_words = [held.tile([P, T], U32, name=f"tok_words{s}", align_bytes=64) for s in range(PASSES)]
         tok_bytes = held.tile([P, T], U8, name="tok_bytes", align_bytes=64)
-        slot_words = [held.tile([P, E * C], U32, name=f"slot_words{s}", align_bytes=64) for s in range(PASSES)]
-        slot_bytes = held.tile([P, E * C], U8, name="slot_bytes", align_bytes=64)
         gate_sb = held.tile([P, E * C], F32, name="gate_sb")
+        gate_col = held.tile([P, 8], F32, name="gate_col")
+        identity = held.tile([P, P], F32, name="identity")
         win = [held.tile([P, T], F32, name=f"win{b}") for b in range(2)]
 
-        chunks = [("x", 0, s, c) for s in range(PASSES) for c in range(T // TC)]
+        chunks = []
         for e in range(E):
             chunks += [("w1", e, 0, 0), ("w1", e, 1, 0), ("w3", e, 0, 0), ("w3", e, 1, 0), ("w2", e, 0, 0)]
         chunks += [("xr", 0, 0, 0), ("xr", 0, 1, 0)]
-        raws, groups, weights = {}, {}, {}
+        raws, groups, weights, spent, slots = {}, {}, {}, {}, {}
         first_layer_in = {"w1": w1, "w3": w3}
 
         def load(i):
             kind, e, s, c = chunks[i]
-            if kind == "x":
-                raw = rawp.tile([P, 4, TC], F32, name="raw")
-                nc.sync.dma_start(raw[:], xT[s * 512 : (s + 1) * 512, c * TC : (c + 1) * TC].rearrange("(p j) t -> p j t", j=4))
-            elif kind == "w2":
+            if kind == "w2":
                 raw = rawp.tile([P, 4, N], F32, name="raw2", tag="raw")
                 rows = w2[e].rearrange("(q t b) n -> b q t n", t=4, b=2)
                 for b in range(2):
@@ -65,10 +66,6 @@ def tile_moe_res_glu_gelu_kernel(tc, xT, xr, w1, w3, w2, gate, offs, out):
                 raw = rawp.tile([P, 4, H], F32, name="raw")
                 nc.sync.dma_start(raw[:], first_layer_in[kind][e, s * 512 : (s + 1) * 512, :].rearrange("(p j) c -> p j c", j=4))
             raws[i] = raw
-            if i == 0:
-                nc.sync.dma_start(offsets[:], offs)
-            if i == LOOKAHEAD - 1:
-                nc.sync.dma_start(gate_sb[:], gate[0:P, :])
 
         def share(dst, src, part):
             cut = dst.shape[1] * part // 64
@@ -80,18 +77,22 @@ def tile_moe_res_glu_gelu_kernel(tc, xT, xr, w1, w3, w2, gate, offs, out):
         def interleave(i):
             kind, e, s, c = chunks[i]
             raw = raws.pop(i)
-            if kind == "x":
-                grouped = grp.tile([P, TC * 4], BF16, name="grouped", align_bytes=64)
-                share(grouped[:].rearrange("p (c b j) -> p c j b", b=2, j=4), raw[:].rearrange("p j (c b) -> p c j b", b=2), V_TOKENS)
-            elif kind == "w2":
-                grouped = groups.pop("spent")[:, : N * 4]
-                share(grouped.rearrange("p (c b j) -> p c j b", b=2, j=4), raw[:].rearrange("p j (c b) -> p c j b", b=2), 64)
+            if kind == "w2":
+                grouped = grp.tile([P, N * 4], BF16, name="w2_grouped", bufs=2, align_bytes=64)[:]
+                share(grouped.rearrange("p (c b j) -> p c j b", b=2, j=4), raw[:].rearrange("p j (c b) -> p c j b", b=2), 64 if e < E - 1 else 0)
             else:
-                grouped = grp.tile([P, H * 4], BF16, name="grouped", align_bytes=64)
-                part = V_LAST if chunks[i] == ("w3", E - 1, 1, 0) else V_FIRST if (kind, s) == ("w1", 0) else 0
-                if (kind, s) == ("w3", 1):
-                    groups["spent"] = grouped
-                    raws["spent"] = raw
+                if (kind, e, s) == ("w1", 0, 1):
+                    grouped = work.tile([P, H * 4], BF16, name="grouped_once", tag="late_words", bufs=1, align_bytes=64)
+                else:
+                    grouped = grp.tile([P, H * 4], BF16, name="grouped", align_bytes=64)
+                part = 0
+                if (kind, s) == ("w1", 0) and e > 0:
+                    part = V_SHARE
+                if (kind, e) == ("w3", 0):
+                    part = V_FIRST[s]
+                if (kind, e, s) == ("w3", E - 1, 1):
+                    part = V_LAST
+                spent[kind, s] = raw
                 share(
                     grouped[:].rearrange("p (t q b j) -> p q t j b", t=4, b=2, j=4),
                     raw[:].rearrange("p j (q t b) -> p q t j b", t=4, b=2),
@@ -102,26 +103,47 @@ def tile_moe_res_glu_gelu_kernel(tc, xT, xr, w1, w3, w2, gate, offs, out):
         def quantize(i):
             kind, e, s, c = chunks[i]
             grouped = groups.pop(i)
-            if kind == "x":
-                words, scales = tok_words[s][:, c * TC : (c + 1) * TC], tok_bytes[4 * s : P, c * TC : (c + 1) * TC]
-            else:
-                width = N if kind == "w2" else H
-                words = codes.tile([P, width], U32, name=f"{kind}_words{s}", align_bytes=64)[:]
-                scales = codes.tile([P, width], U8, name=f"{kind}_scales{s}", align_bytes=64)[:]
-                weights[kind, e, s] = (words, scales)
+            width = N if kind == "w2" else H
+            words = codes.tile([P, width], U32, name=f"{kind}_words{s}", align_bytes=64)[:]
+            scales = codes.tile([P, width], U8, name=f"{kind}_scales{s}", align_bytes=64)[:]
+            weights[kind, e, s] = (words, scales)
             nc.vector.quantize_mx(out=words.bitcast(FP8X4), scales=scales, in_=grouped[:])
+
+        def load_tokens(s, t0, t1):
+            raw = held.tile([P, 4, t1 - t0], F32, name=f"tok_raw{s}_{t0}")
+            nc.sync.dma_start(raw[:], xT[s * 512 : (s + 1) * 512, t0:t1].rearrange("(p j) t -> p j t", j=4))
+            return raw
+
+        def quantize_tokens(raw, s, t0, t1):
+            for c0 in range(t0, t1, TC):
+                grouped = grp.tile([P, TC * 4], BF16, name="grouped", align_bytes=64)
+                share(
+                    grouped[:].rearrange("p (c b j) -> p c j b", b=2, j=4),
+                    raw[:, :, c0 - t0 : c0 - t0 + TC].rearrange("p j (c b) -> p c j b", b=2),
+                    V_TOKENS,
+                )
+                nc.vector.quantize_mx(out=tok_words[s][:, c0 : c0 + TC].bitcast(FP8X4), scales=tok_bytes[4 * s : P, c0 : c0 + TC], in_=grouped[:])
+
+        def spread_gate():
+            make_identity(nc, identity[:])
+            for half in range(2):
+                bank = psum.tile([P, 4, 128], F32, name="gate_bank", tag="y", bufs=2)
+                for c in range(4):
+                    col = 4 * half + c
+                    nc.tensor.transpose(bank[:, c, :], gate_col[:, col : col + 1].to_broadcast([P, P]), identity[:])
+                nc.scalar.copy(gate_sb[:].rearrange("p (n c) -> p n c", c=8)[:, :, 4 * half : 4 * half + 4], bank[:].rearrange("p c n -> p n c"))
 
         banks, gelus, hidden, ys = {}, {}, {}, {}
 
-        def gather_words(s):
-            nc.vector.tensor_copy(slot_words[s][:], tok_words[s][:].indirect(offsets[:]))
-
-        def gather_bytes():
-            nc.vector.tensor_copy(slot_bytes[:], tok_bytes[:].indirect(offsets[:]))
+        def gather(what, window, dtype, e0, e1, tag):
+            got = work.tile([P, (e1 - e0) * C], dtype, name=f"slot_{what}_{e0}", tag=tag, bufs=1, align_bytes=64)
+            nc.vector.tensor_copy(got[:], window[:].indirect(offsets[:, e0 * 16 : e1 * 16]))
+            for e in range(e0, e1):
+                slots[what, e] = got[:, (e - e0) * C : (e - e0 + 1) * C]
 
         def first_layer(kind, e, half):
             bank = psum.tile([P, 4, 128], F32, name=f"bank_{kind}", bufs=3)
-            cols = slice(e * C + half * 128, e * C + (half + 1) * 128)
+            cols = slice(half * 128, (half + 1) * 128)
             for t in range(4):
                 m_cols = slice(t * 128, (t + 1) * 128)
                 for s in range(PASSES):
@@ -130,19 +152,19 @@ def tile_moe_res_glu_gelu_kernel(tc, xT, xr, w1, w3, w2, gate, offs, out):
                         out=bank[:, t, :],
                         lhsT=words[:, m_cols].bitcast(FP8X4),
                         lhsT_scale=scales[:, m_cols],
-                        rhs=slot_words[s][:, cols].bitcast(FP8X4),
-                        rhs_scale=slot_bytes[4 * s : P, cols],
+                        rhs=slots[s, e][:, cols].bitcast(FP8X4),
+                        rhs_scale=slots["bytes", e][4 * s : P, cols],
                         start=s == 0,
                         stop=s == PASSES - 1,
                     )
             banks[kind, half] = bank
 
         def gelu(half):
-            ga = raws["spent"][:, half, :].rearrange("p (n t) -> p n t", t=4)
+            ga = spent["w3", 1][:, half, :].rearrange("p (n t) -> p n t", t=4)
             nc.scalar.activation(ga, banks["w1", half][:].rearrange("p t n -> p n t"), GELU)
             gelus[half] = ga
 
-        def product(half):
+        def product(e, half):
             if half == 0:
                 hidden["h"] = work.tile([P, C, 4], BF16, name="h", align_bytes=64)
             nc.vector.tensor_tensor(
@@ -151,7 +173,10 @@ def tile_moe_res_glu_gelu_kernel(tc, xT, xr, w1, w3, w2, gate, offs, out):
 
         def second_layer(e):
             h_words = work.tile([P, C], U32, name="h_words", align_bytes=64)
-            h_scales = work.tile([P, C], U8, name="h_scales", align_bytes=64)
+            if e == 0:
+                h_scales = work.tile([P, C], U8, name="h_scales_first", tag="late_bytes", bufs=1, align_bytes=64)
+            else:
+                h_scales = work.tile([P, C], U8, name="h_scales", align_bytes=64)
             y = psum.tile([P, 2, C], F32, name="y", bufs=2)
             nc.vector.quantize_mx(out=h_words[:].bitcast(FP8X4), scales=h_scales[:], in_=hidden["h"][:].rearrange("p n t -> p (n t)"))
             words, scales = weights["w2", e, 0]
@@ -168,20 +193,22 @@ def tile_moe_res_glu_gelu_kernel(tc, xT, xr, w1, w3, w2, gate, offs, out):
             ys[e] = y
 
         def scatter(e, b):
-            nc.vector.tensor_copy(win[b][:].indirect(offsets[:, e * 16 : (e + 1) * 16]), ys[e, b][:])
+            nc.vector.tensor_tensor(win[b][:].indirect(offsets[:, e * 16 : (e + 1) * 16]), ys[e, b], gate_sb[:, e * C : (e + 1) * C], MULT)
 
-        def weigh(e, b):
-            yg = work.tile([P, C], F32, name=f"yg{b}")
-            nc.vector.tensor_tensor(yg[:], ys[e][:, b, :], gate_sb[:, e * C : (e + 1) * C], MULT)
-            ys[e, b] = yg
+        def fetch_y(e, b, y_sb):
+            nc.scalar.copy(y_sb, ys[e][:, b, :])
+            ys[e, b] = y_sb
 
         def finish(b):
             xr_sb = raws.pop(pos["xr", 0, b, 0])
-            for c0, c1 in ((0, 1024), (1024, T)):
+            for c0, c1 in ((0, 640), (640, 1280), (1280, T)):
                 cols = slice(c0, c1)
                 nc.vector.tensor_tensor(xr_sb[:, cols], win[b][:, cols], xr_sb[:, cols], ADD)
                 nc.sync.dma_start(out[b * P : (b + 1) * P, cols], xr_sb[:, cols])
 
+        nc.sync.dma_start(gate_col[:], gate[0].rearrange("(p c) -> p c", c=8))
+        tok_raws = [load_tokens(*piece) for piece in TOKEN_LOADS]
+        nc.sync.dma_start(offsets[:], offs)
         for i in range(LOOKAHEAD):
             load(i)
         nc.gpsimd.memset(tok_bytes[:], 0)
@@ -199,31 +226,49 @@ def tile_moe_res_glu_gelu_kernel(tc, xT, xr, w1, w3, w2, gate, offs, out):
                 load(i + LOOKAHEAD)
             quantize(i)
 
-        for s in range(PASSES):
-            for c in range(T // TC):
-                prepare("x", 0, s, c)
-            gather_words(s)
-        gather_bytes()
+        spread_gate()
+        for raw, (s, t0, t1) in zip(tok_raws, TOKEN_LOADS):
+            quantize_tokens(raw, s, t0, t1)
+            if (s, t1) == (0, T):
+                gather(0, tok_words[0], U32, 0, E, "words0")
+        gather(1, tok_words[1], U32, 0, EARLY, "words1")
+        gather("bytes", tok_bytes, U8, 0, EARLY, "bytes")
         for e in range(E):
             prepare("w1", e, 0)
             prepare("w1", e, 1)
             for half in range(2):
                 first_layer("w1", e, half)
-            if e > 0:
-                scatter(e - 1, 0)
+            if e == 0:
+                gather(1, tok_words[1], U32, EARLY, E, "late_words")
+            if e == 1:
+                fetch_y(0, 0, spent["w1", 1][:, 0, :C])
+                scatter(0, 0)
             prepare("w3", e, 0)
-            if e > 0:
-                scatter(e - 1, 1)
+            if e == 2:
+                fetch_y(1, 0, spent["w3", 0][:, 0, :C])
+                scatter(1, 0)
             prepare("w3", e, 1)
-            for half in range(2):
-                gelu(half)
+            if e > 2:
+                fetch_y(e - 1, 0, spent["w3", 1][:, 2, :C])
+            if 0 < e < E - 1:
+                fetch_y(e - 1, 1, spent["w3", 1][:, 3, :C])
+            gelu(0)
+            gelu(1)
             prepare("w2", e)
+            if e > 2:
+                scatter(e - 1, 0)
             for half in range(2):
                 first_layer("w3", e, half)
-                product(half)
+                product(e, half)
             second_layer(e)
-            for b in range(2):
-                weigh(e, b)
+            if e == E - 1:
+                fetch_y(e - 1, 1, spent["w3", 1][:, 1, :C])
+            if e > 0:
+                scatter(e - 1, 1)
+            if e == 0:
+                gather("bytes", tok_bytes, U8, EARLY, E, "late_bytes")
+        for b in range(2):
+            fetch_y(E - 1, b, spent["w1", 1][:, b, :C])
         for b in range(2):
             scatter(E - 1, b)
             finish(b)

@@ -37,7 +37,6 @@ def tile_moe_res_glu_gelu_kernel(tc, xT, xr, w1, w3, w2, gate, offs, out):
         tc.psum_pool(name="psum", bufs=1) as psum,
     ):
         offsets = held.tile([P, E * C // 16], U16, name="offsets")
-        warm = held.tile([P, 8], F32, name="warm")
         tok_words = [held.tile([P, T], U32, name=f"tok_words{s}", align_bytes=64) for s in range(PASSES)]
         tok_bytes = held.tile([P, T], U8, name="tok_bytes", align_bytes=64)
         gate_sb = held.tile([P, E * C], F32, name="gate_sb")
@@ -212,10 +211,8 @@ def tile_moe_res_glu_gelu_kernel(tc, xT, xr, w1, w3, w2, gate, offs, out):
         for i in range(LOOKAHEAD):
             load(i)
         nc.gpsimd.memset(tok_bytes[:], 0)
-        nc.vector.memset(warm[:], 0.0)
         for b in range(2):
             nc.vector.memset(win[b][:], 0.0)
-        nc.scalar.activation(warm[:], warm[:], GELU)
 
         pos = {c: i for i, c in enumerate(chunks)}
 

@@ -17,12 +17,13 @@ GELU = mybir.ActivationFunctionType.Gelu_apprx_tanh
 P = 128
 PASSES = K // 512
 TC = 512
-V_TOKENS = 28
+V_TOKENS = 40
 V_SHARE = 40
-V_FIRST = (16, 32)
+V_FIRST = (0, 32)
 V_LAST = 40
 EARLY = 2
-TOKEN_LOADS = ((0, 0, T), (1, 0, 2 * TC), (1, 2 * TC, T))
+TOKEN_LOADS = ((0, 0, T), (1, 0, T))
+CUTS = ((0, 320, 704, 1088, T), (0, 512, 1024, T))
 LOOKAHEAD = 8
 
 
@@ -55,9 +56,9 @@ def tile_moe_res_glu_gelu_kernel(tc, xT, xr, w1, w3, w2, gate, offs, out):
             kind, e, s, c = chunks[i]
             if kind == "w2":
                 raw = rawp.tile([P, 4, N], F32, name="raw2", tag="raw")
-                rows = w2[e].rearrange("(q t b) n -> b q t n", t=4, b=2)
+                rows = w2[e].rearrange("(q u b v) n -> b q u (v n)", u=2, b=2, v=2)
                 for b in range(2):
-                    nc.sync.dma_start(raw[b:P:2], rows[b])
+                    nc.sync.dma_start(raw[b:P:2].rearrange("p (u v) n -> p u (v n)", u=2), rows[b])
             elif kind == "xr":
                 raw = rawp.tile([P, T], F32, name="xr_sb", tag="raw")
                 nc.sync.dma_start(raw[:], xr[s * P : (s + 1) * P, :])
@@ -92,11 +93,10 @@ def tile_moe_res_glu_gelu_kernel(tc, xT, xr, w1, w3, w2, gate, offs, out):
                 if (kind, e, s) == ("w3", E - 1, 1):
                     part = V_LAST
                 spent[kind, s] = raw
-                share(
-                    grouped[:].rearrange("p (t q b j) -> p q t j b", t=4, b=2, j=4),
-                    raw[:].rearrange("p j (q t b) -> p q t j b", t=4, b=2),
-                    part,
-                )
+                dst = grouped[:].rearrange("p (u v q b j) -> p u q j b v", u=2, v=2, b=2, j=4)
+                src = raw[:].rearrange("p j (q u b v) -> p u q j b v", u=2, b=2, v=2)
+                for u in range(2):
+                    share(dst[:, u], src[:, u], min(max(2 * part - 64 * u, 0), 64))
             groups[i] = grouped
 
         def quantize(i):
@@ -200,14 +200,14 @@ def tile_moe_res_glu_gelu_kernel(tc, xT, xr, w1, w3, w2, gate, offs, out):
 
         def finish(b):
             xr_sb = raws.pop(pos["xr", 0, b, 0])
-            for c0, c1 in ((0, 640), (640, 1280), (1280, T)):
-                cols = slice(c0, c1)
+            for k in range(len(CUTS[b]) - 1):
+                cols = slice(CUTS[b][k], CUTS[b][k + 1])
                 nc.vector.tensor_tensor(xr_sb[:, cols], win[b][:, cols], xr_sb[:, cols], ADD)
                 nc.sync.dma_start(out[b * P : (b + 1) * P, cols], xr_sb[:, cols])
 
+        nc.sync.dma_start(offsets[:], offs)
         nc.sync.dma_start(gate_col[:], gate[0].rearrange("(p c) -> p c", c=8))
         tok_raws = [load_tokens(*piece) for piece in TOKEN_LOADS]
-        nc.sync.dma_start(offsets[:], offs)
         for i in range(LOOKAHEAD):
             load(i)
         nc.gpsimd.memset(tok_bytes[:], 0)

@@ -18,12 +18,12 @@ P = 128
 PASSES = K // 512
 TC = 512
 V_TOKENS = 40
-V_SHARE = 40
+V_SHARE = 32
 V_FIRST = (0, 32)
 V_LAST = 40
 EARLY = 2
 TOKEN_LOADS = ((0, 0, T), (1, 0, T))
-CUTS = ((0, 320, 704, 1088, T), (0, 512, 1024, T))
+CUTS = ((0, 256, 512, 1024, T), (0, 512, 1024, T))
 LOOKAHEAD = 8
 
 
@@ -106,7 +106,10 @@ def tile_moe_res_glu_gelu_kernel(tc, xT, xr, w1, w3, w2, gate, offs, out):
             words = codes.tile([P, width], U32, name=f"{kind}_words{s}", align_bytes=64)[:]
             scales = codes.tile([P, width], U8, name=f"{kind}_scales{s}", align_bytes=64)[:]
             weights[kind, e, s] = (words, scales)
-            nc.vector.quantize_mx(out=words.bitcast(FP8X4), scales=scales, in_=grouped[:])
+            pieces = 2 if (kind, e, s) == ("w3", E - 1, 1) else 1
+            for u in range(pieces):
+                c0, c1 = u * width // pieces, (u + 1) * width // pieces
+                nc.vector.quantize_mx(out=words[:, c0:c1].bitcast(FP8X4), scales=scales[:, c0:c1], in_=grouped[:, 4 * c0 : 4 * c1])
 
         def load_tokens(s, t0, t1):
             raw = held.tile([P, 4, t1 - t0], F32, name=f"tok_raw{s}_{t0}")

@@ -18,7 +18,7 @@ P = 128
 PASSES = K // 512
 TC = 512
 V_TOKENS = 40
-V_SHARE = 32
+V_SHARE = 40
 V_FIRST = (0, 32)
 V_LAST = 40
 EARLY = 2
@@ -41,6 +41,7 @@ def tile_moe_res_glu_gelu_kernel(tc, xT, xr, w1, w3, w2, gate, offs, out):
         tok_words = [held.tile([P, T], U32, name=f"tok_words{s}", align_bytes=64) for s in range(PASSES)]
         tok_bytes = held.tile([P, T], U8, name="tok_bytes", align_bytes=64)
         gate_sb = held.tile([P, E * C], F32, name="gate_sb")
+        gate_rows = held.tile([P, P], F32, name="gate_rows")
         gate_col = held.tile([P, 8], F32, name="gate_col")
         identity = held.tile([P, P], F32, name="identity")
         win = [held.tile([P, T], F32, name=f"win{b}") for b in range(2)]
@@ -128,12 +129,15 @@ def tile_moe_res_glu_gelu_kernel(tc, xT, xr, w1, w3, w2, gate, offs, out):
 
         def spread_gate():
             make_identity(nc, identity[:])
+            turned = psum.tile([P, P], F32, name="gate_turned", tag="y", bufs=2)
+            nc.tensor.transpose(turned[:], gate_rows[:], identity[:])
+            nc.scalar.copy(gate_col[:], turned[:, :8])
             for half in range(2):
                 bank = psum.tile([P, 4, 128], F32, name="gate_bank", tag="y", bufs=2)
                 for c in range(4):
                     col = 4 * half + c
                     nc.tensor.transpose(bank[:, c, :], gate_col[:, col : col + 1].to_broadcast([P, P]), identity[:])
-                nc.scalar.copy(gate_sb[:].rearrange("p (n c) -> p n c", c=8)[:, :, 4 * half : 4 * half + 4], bank[:].rearrange("p c n -> p n c"))
+                nc.scalar.copy(gate_sb[:, half * 512 : (half + 1) * 512], bank[:].rearrange("p c n -> p (c n)"))
 
         banks, gelus, hidden, ys = {}, {}, {}, {}
 
@@ -209,8 +213,10 @@ def tile_moe_res_glu_gelu_kernel(tc, xT, xr, w1, w3, w2, gate, offs, out):
                 nc.sync.dma_start(out[b * P : (b + 1) * P, cols], xr_sb[:, cols])
 
         nc.sync.dma_start(offsets[:], offs)
-        nc.sync.dma_start(gate_col[:], gate[0].rearrange("(p c) -> p c", c=8))
-        tok_raws = [load_tokens(*piece) for piece in TOKEN_LOADS]
+        nc.vector.memset(gate_rows[:], 0.0)
+        tok_raws = [load_tokens(*TOKEN_LOADS[0])]
+        nc.sync.dma_start(gate_rows[0:8, :], gate[0].rearrange("(c n) -> c n", c=8))
+        tok_raws.append(load_tokens(*TOKEN_LOADS[1]))
         for i in range(LOOKAHEAD):
             load(i)
         nc.gpsimd.memset(tok_bytes[:], 0)
@@ -254,6 +260,8 @@ def tile_moe_res_glu_gelu_kernel(tc, xT, xr, w1, w3, w2, gate, offs, out):
                 fetch_y(e - 1, 1, spent["w3", 1][:, 3, :C])
             gelu(0)
             gelu(1)
+            if 0 < e < E - 1:
+                scatter(e - 1, 1)
             prepare("w2", e)
             if e > 2:
                 scatter(e - 1, 0)
@@ -263,7 +271,6 @@ def tile_moe_res_glu_gelu_kernel(tc, xT, xr, w1, w3, w2, gate, offs, out):
             second_layer(e)
             if e == E - 1:
                 fetch_y(e - 1, 1, spent["w3", 1][:, 1, :C])
-            if e > 0:
                 scatter(e - 1, 1)
             if e == 0:
                 gather("bytes", tok_bytes, U8, EARLY, E, "late_bytes")

@@ -23,7 +23,6 @@ V_FIRST = (0, 32)
 V_LAST = 40
 EARLY = 2
 TOKEN_LOADS = ((0, 0, T), (1, 0, T))
-CUTS = ((0, 256, 512, 1024, T), (0, 512, 1024, T))
 LOOKAHEAD = 8
 
 
@@ -205,12 +204,10 @@ def tile_moe_res_glu_gelu_kernel(tc, xT, xr, w1, w3, w2, gate, offs, out):
             nc.scalar.copy(y_sb, ys[e][:, b, :])
             ys[e, b] = y_sb
 
-        def finish(b):
-            xr_sb = raws.pop(pos["xr", 0, b, 0])
-            for k in range(len(CUTS[b]) - 1):
-                cols = slice(CUTS[b][k], CUTS[b][k + 1])
-                nc.vector.tensor_tensor(xr_sb[:, cols], win[b][:, cols], xr_sb[:, cols], ADD)
-                nc.sync.dma_start(out[b * P : (b + 1) * P, cols], xr_sb[:, cols])
+        def finish(engine, b, c0, c1):
+            xr_sb = raws[pos["xr", 0, b, 0]]
+            engine.tensor_tensor(xr_sb[:, c0:c1], win[b][:, c0:c1], xr_sb[:, c0:c1], ADD)
+            nc.sync.dma_start(out[b * P : (b + 1) * P, c0:c1], xr_sb[:, c0:c1])
 
         nc.sync.dma_start(offsets[:], offs)
         nc.vector.memset(gate_rows[:], 0.0)
@@ -274,8 +271,13 @@ def tile_moe_res_glu_gelu_kernel(tc, xT, xr, w1, w3, w2, gate, offs, out):
                 scatter(e - 1, 1)
             if e == 0:
                 gather("bytes", tok_bytes, U8, EARLY, E, "late_bytes")
-        for b in range(2):
-            fetch_y(E - 1, b, spent["w1", 1][:, b, :C])
-        for b in range(2):
-            scatter(E - 1, b)
-            finish(b)
+        last = slice((E - 1) * 16, E * 16)
+        fetch_y(E - 1, 0, spent["w1", 1][:, 0, :C])
+        gated = spent["w1", 1][:, 1, :C]
+        nc.vector.tensor_tensor(gated, ys[E - 1][:, 1, :], gate_sb[:, (E - 1) * C :], MULT)
+        scatter(E - 1, 0)
+        nc.vector.tensor_copy(win[1][:].indirect(offsets[:, last]), gated)
+        for c0 in (0, 256):
+            finish(nc.gpsimd, 0, c0, c0 + 256)
+        for b, c0 in ((0, 512), (0, 1024), (1, 0), (1, 512), (1, 1024)):
+            finish(nc.vector, b, c0, c0 + 512)

@@ -15,181 +15,203 @@ MULT, ADD = mybir.AluOpType.mult, mybir.AluOpType.add
 GELU = mybir.ActivationFunctionType.Gelu_apprx_tanh
 
 P = 128
-PASSES = K // 512
-TC = 512
+PASS_K = 512
+PASSES = K // PASS_K
+BLOCKS = N // P
+SLOT_HALF = 128
+LIST_COLS = C // 16
+LAST = E - 1
+TOKEN_CHUNK = 512
+Q = 64
 V_TOKENS = 40
-V_SHARE = 40
-V_FIRST = (0, 32)
-V_LAST = 40
+V_CLOSING = 48
 EARLY = 2
-TOKEN_LOADS = ((0, 0, T), (1, 0, T))
+CUTS = ((0, 256, 512, 1024, T), (0, 512, 1024, T))
 LOOKAHEAD = 8
+RAW_BUFS = LOOKAHEAD + 2
+GROUPED_BUFS = 6
+BANK_BUFS = 3
 
 
 def tile_moe_res_glu_gelu_kernel(tc, xT, xr, w1, w3, w2, gate, offs, out):
     nc = tc.nc
     with (
         tc.tile_pool(name="held", bufs=1) as held,
-        tc.tile_pool(name="rawp", bufs=10) as rawp,
-        tc.tile_pool(name="grp", bufs=6) as grp,
+        tc.tile_pool(name="rawp", bufs=RAW_BUFS) as rawp,
+        tc.tile_pool(name="grp", bufs=GROUPED_BUFS) as grp,
         tc.tile_pool(name="codes", bufs=2) as codes,
         tc.tile_pool(name="work", bufs=2) as work,
         tc.psum_pool(name="psum", bufs=1) as psum,
     ):
-        offsets = held.tile([P, E * C // 16], U16, name="offsets")
+        offsets = held.tile([P, E * LIST_COLS], U16, name="offsets")
         tok_words = [held.tile([P, T], U32, name=f"tok_words{s}", align_bytes=64) for s in range(PASSES)]
         tok_bytes = held.tile([P, T], U8, name="tok_bytes", align_bytes=64)
         gate_sb = held.tile([P, E * C], F32, name="gate_sb")
         gate_rows = held.tile([P, P], F32, name="gate_rows")
         gate_col = held.tile([P, 8], F32, name="gate_col")
         identity = held.tile([P, P], F32, name="identity")
-        win = [held.tile([P, T], F32, name=f"win{b}") for b in range(2)]
+        win = [held.tile([P, T], F32, name=f"win{b}") for b in range(BLOCKS)]
 
         chunks = []
         for e in range(E):
-            chunks += [("w1", e, 0, 0), ("w1", e, 1, 0), ("w3", e, 0, 0), ("w3", e, 1, 0), ("w2", e, 0, 0)]
-        chunks += [("xr", 0, 0, 0), ("xr", 0, 1, 0)]
-        raws, groups, weights, spent, slots = {}, {}, {}, {}, {}
+            chunks += [("w1", e, 0), ("w1", e, 1), ("w3", e, 0), ("w3", e, 1), ("w2", e, 0)]
+        chunks += [("xr", 0, b) for b in range(BLOCKS)]
+        pos = {chunk: i for i, chunk in enumerate(chunks)}
+        raws, weights, banks, gelus, ys, slots = {}, {}, {}, {}, {}, {}
         first_layer_in = {"w1": w1, "w3": w3}
 
         def load(i):
-            kind, e, s, c = chunks[i]
+            kind, e, s = chunks[i]
             if kind == "w2":
                 raw = rawp.tile([P, 4, N], F32, name="raw2", tag="raw")
-                rows = w2[e].rearrange("(q u b v) n -> b q u (v n)", u=2, b=2, v=2)
-                for b in range(2):
-                    nc.sync.dma_start(raw[b:P:2].rearrange("p (u v) n -> p u (v n)", u=2), rows[b])
+                rows = w2[e].rearrange("(q u r v) n -> r q u (v n)", u=2, r=2, v=2)
+                for r in range(2):
+                    nc.sync.dma_start(raw[r:P:2].rearrange("p (u v) n -> p u (v n)", u=2), rows[r])
             elif kind == "xr":
                 raw = rawp.tile([P, T], F32, name="xr_sb", tag="raw")
                 nc.sync.dma_start(raw[:], xr[s * P : (s + 1) * P, :])
             else:
                 raw = rawp.tile([P, 4, H], F32, name="raw")
-                nc.sync.dma_start(raw[:], first_layer_in[kind][e, s * 512 : (s + 1) * 512, :].rearrange("(p j) c -> p j c", j=4))
-            raws[i] = raw
+                rows = first_layer_in[kind][e, s * PASS_K : (s + 1) * PASS_K, :]
+                nc.sync.dma_start(raw[:], rows.rearrange("(p j) i -> p j i", j=4))
+            raws[chunks[i]] = raw
 
-        def share(dst, src, part):
-            cut = dst.shape[1] * part // 64
-            if cut:
-                nc.vector.tensor_copy(dst[:, :cut], src[:, :cut])
-            if part < 64:
-                nc.scalar.copy(dst[:, cut:], src[:, cut:])
+        def load_ahead(chunk):
+            if pos[chunk] + LOOKAHEAD < len(chunks):
+                load(pos[chunk] + LOOKAHEAD)
 
-        def interleave(i):
-            kind, e, s, c = chunks[i]
-            raw = raws.pop(i)
-            if kind == "w2":
-                grouped = grp.tile([P, N * 4], BF16, name="w2_grouped", bufs=2, align_bytes=64)[:]
-                share(grouped.rearrange("p (c b j) -> p c j b", b=2, j=4), raw[:].rearrange("p j (c b) -> p c j b", b=2), 64 if e < E - 1 else 0)
-            else:
-                if (kind, e, s) == ("w1", 0, 1):
-                    grouped = work.tile([P, H * 4], BF16, name="grouped_once", tag="late_words", bufs=1, align_bytes=64)
-                else:
-                    grouped = grp.tile([P, H * 4], BF16, name="grouped", align_bytes=64)
-                part = 0
-                if (kind, s) == ("w1", 0) and e > 0:
-                    part = V_SHARE
-                if (kind, e) == ("w3", 0):
-                    part = V_FIRST[s]
-                if (kind, e, s) == ("w3", E - 1, 1):
-                    part = V_LAST
-                spent[kind, s] = raw
-                dst = grouped[:].rearrange("p (u v q b j) -> p u q j b v", u=2, v=2, b=2, j=4)
-                src = raw[:].rearrange("p j (q u b v) -> p u q j b v", u=2, b=2, v=2)
-                for u in range(2):
-                    share(dst[:, u], src[:, u], min(max(2 * part - 64 * u, 0), 64))
-            groups[i] = grouped
-
-        def quantize(i):
-            kind, e, s, c = chunks[i]
-            grouped = groups.pop(i)
-            width = N if kind == "w2" else H
+        def new_codes(chunk, width):
+            kind, e, s = chunk
             words = codes.tile([P, width], U32, name=f"{kind}_words{s}", align_bytes=64)[:]
             scales = codes.tile([P, width], U8, name=f"{kind}_scales{s}", align_bytes=64)[:]
-            weights[kind, e, s] = (words, scales)
-            pieces = 2 if (kind, e, s) == ("w3", E - 1, 1) else 1
-            for u in range(pieces):
-                c0, c1 = u * width // pieces, (u + 1) * width // pieces
-                nc.vector.quantize_mx(out=words[:, c0:c1].bitcast(FP8X4), scales=scales[:, c0:c1], in_=grouped[:, 4 * c0 : 4 * c1])
+            weights[chunk] = (words, scales)
 
-        def load_tokens(s, t0, t1):
-            raw = held.tile([P, 4, t1 - t0], F32, name=f"tok_raw{s}_{t0}")
-            nc.sync.dma_start(raw[:], xT[s * 512 : (s + 1) * 512, t0:t1].rearrange("(p j) t -> p j t", j=4))
+        def interleave(chunk, by_u, vector_q):
+            src = raws[chunk][:].rearrange("p j (q u r v) -> p u q j r v", u=2, r=2, v=2)
+            dst = [part.rearrange("p (v q r j) -> p q j r v", v=2, r=2, j=4) for part in by_u]
+            nc.scalar.copy(dst[0], src[:, 0])
+            if vector_q:
+                nc.vector.tensor_copy(dst[1][:, :vector_q], src[:, 1, :vector_q])
+            if vector_q < Q:
+                nc.scalar.copy(dst[1][:, vector_q:], src[:, 1, vector_q:])
+
+        def quantize(chunk, first_col, grouped):
+            words, scales = weights[chunk]
+            made = slice(first_col, first_col + grouped.shape[1] // 4)
+            nc.vector.quantize_mx(out=words[:, made].bitcast(FP8X4), scales=scales[:, made], in_=grouped)
+
+        def multiply(chunk, tiles, closing):
+            kind, e, s = chunk
+            words, scales = weights[chunk]
+            for half in range(2):
+                if s == 0:
+                    banks[kind, half] = psum.tile([P, 4, SLOT_HALF], F32, name=f"bank_{kind}", bufs=BANK_BUFS)
+                moving = slice(half * SLOT_HALF, (half + 1) * SLOT_HALF)
+                for t in tiles:
+                    stationary = slice(t * P, (t + 1) * P)
+                    nc.tensor.matmul_mx(
+                        out=banks[kind, half][:, t, :],
+                        lhsT=words[:, stationary].bitcast(FP8X4),
+                        lhsT_scale=scales[:, stationary],
+                        rhs=slots[s, e][:, moving].bitcast(FP8X4),
+                        rhs_scale=slots["bytes", e][4 * s : P, moving],
+                        start=(s, t) == (0, 0),
+                        stop=closing and (s, t) == (PASSES - 1, tiles[-1]),
+                    )
+
+        def prepare(chunk):
+            grouped = grp.tile([P, 4 * H], BF16, name="grouped", align_bytes=64)
+            interleave(chunk, (grouped[:, : 2 * H], grouped[:, 2 * H :]), 0)
+            load_ahead(chunk)
+            new_codes(chunk, H)
+            quantize(chunk, 0, grouped[:])
+            multiply(chunk, range(4), True)
+
+        def prepare_last(e):
+            chunk = ("w3", e, PASSES - 1)
+            by_u = [work.tile([P, 2 * H], BF16, name=f"last{u}", tag=f"last{u}", bufs=1, align_bytes=64)[:] for u in range(2)]
+            interleave(chunk, by_u, V_CLOSING if e == LAST else Q)
+            load_ahead(chunk)
+            new_codes(chunk, H)
+            order = (0, 1) if e == LAST else (1, 0)
+            for u in order:
+                quantize(chunk, u * H // 2, by_u[u])
+                multiply(chunk, (2 * u, 2 * u + 1), u == order[1])
+
+        def load_tokens(s):
+            raw = held.tile([P, 4, T], F32, name=f"tok_raw{s}")
+            nc.sync.dma_start(raw[:], xT[s * PASS_K : (s + 1) * PASS_K, :].rearrange("(p j) x -> p j x", j=4))
             return raw
 
-        def quantize_tokens(raw, s, t0, t1):
-            for c0 in range(t0, t1, TC):
-                grouped = grp.tile([P, TC * 4], BF16, name="grouped", align_bytes=64)
-                share(
-                    grouped[:].rearrange("p (c b j) -> p c j b", b=2, j=4),
-                    raw[:, :, c0 - t0 : c0 - t0 + TC].rearrange("p j (c b) -> p c j b", b=2),
-                    V_TOKENS,
-                )
-                nc.vector.quantize_mx(out=tok_words[s][:, c0 : c0 + TC].bitcast(FP8X4), scales=tok_bytes[4 * s : P, c0 : c0 + TC], in_=grouped[:])
+        def quantize_tokens(raw, s):
+            for x0 in range(0, T, TOKEN_CHUNK):
+                tokens = slice(x0, x0 + TOKEN_CHUNK)
+                grouped = grp.tile([P, TOKEN_CHUNK * 4], BF16, name="grouped", align_bytes=64)
+                dst = grouped[:].rearrange("p (x pair j) -> p x j pair", pair=2, j=4)
+                src = raw[:, :, tokens].rearrange("p j (x pair) -> p x j pair", pair=2)
+                cut = dst.shape[1] * V_TOKENS // 64
+                nc.vector.tensor_copy(dst[:, :cut], src[:, :cut])
+                nc.scalar.copy(dst[:, cut:], src[:, cut:])
+                nc.vector.quantize_mx(out=tok_words[s][:, tokens].bitcast(FP8X4), scales=tok_bytes[4 * s : P, tokens], in_=grouped[:])
+
+        def gather(what, source, dtype, e0, e1, tag):
+            got = work.tile([P, (e1 - e0) * C], dtype, name=f"slot_{what}_{e0}", tag=tag, bufs=1, align_bytes=64)
+            nc.vector.tensor_copy(got[:], source[:].indirect(offsets[:, e0 * LIST_COLS : e1 * LIST_COLS]))
+            for e in range(e0, e1):
+                slots[what, e] = got[:, (e - e0) * C : (e - e0 + 1) * C]
 
         def spread_gate():
             make_identity(nc, identity[:])
             turned = psum.tile([P, P], F32, name="gate_turned", tag="y", bufs=2)
             nc.tensor.transpose(turned[:], gate_rows[:], identity[:])
             nc.scalar.copy(gate_col[:], turned[:, :8])
-            for half in range(2):
-                bank = psum.tile([P, 4, 128], F32, name="gate_bank", tag="y", bufs=2)
-                for c in range(4):
-                    col = 4 * half + c
-                    nc.tensor.transpose(bank[:, c, :], gate_col[:, col : col + 1].to_broadcast([P, P]), identity[:])
-                nc.scalar.copy(gate_sb[:, half * 512 : (half + 1) * 512], bank[:].rearrange("p c n -> p (c n)"))
-
-        banks, gelus, hidden, ys = {}, {}, {}, {}
-
-        def gather(what, window, dtype, e0, e1, tag):
-            got = work.tile([P, (e1 - e0) * C], dtype, name=f"slot_{what}_{e0}", tag=tag, bufs=1, align_bytes=64)
-            nc.vector.tensor_copy(got[:], window[:].indirect(offsets[:, e0 * 16 : e1 * 16]))
-            for e in range(e0, e1):
-                slots[what, e] = got[:, (e - e0) * C : (e - e0 + 1) * C]
-
-        def first_layer(kind, e, half):
-            bank = psum.tile([P, 4, 128], F32, name=f"bank_{kind}", bufs=3)
-            cols = slice(half * 128, (half + 1) * 128)
-            for t in range(4):
-                m_cols = slice(t * 128, (t + 1) * 128)
-                for s in range(PASSES):
-                    words, scales = weights[kind, e, s]
-                    nc.tensor.matmul_mx(
-                        out=bank[:, t, :],
-                        lhsT=words[:, m_cols].bitcast(FP8X4),
-                        lhsT_scale=scales[:, m_cols],
-                        rhs=slots[s, e][:, cols].bitcast(FP8X4),
-                        rhs_scale=slots["bytes", e][4 * s : P, cols],
-                        start=s == 0,
-                        stop=s == PASSES - 1,
-                    )
-            banks[kind, half] = bank
-
-        def gelu(half):
-            ga = spent["w3", 1][:, half, :].rearrange("p (n t) -> p n t", t=4)
-            nc.scalar.activation(ga, banks["w1", half][:].rearrange("p t n -> p n t"), GELU)
-            gelus[half] = ga
-
-        def product(e, half):
-            if half == 0:
-                hidden["h"] = work.tile([P, C, 4], BF16, name="h", align_bytes=64)
-            nc.vector.tensor_tensor(
-                hidden["h"][:, half * 128 : (half + 1) * 128, :], banks["w3", half][:].rearrange("p t n -> p n t"), gelus[half], MULT
-            )
+            for c0 in (0, 4):
+                bank = psum.tile([P, 4, P], F32, name="gate_bank", tag="y", bufs=2)
+                for c in range(c0, c0 + 4):
+                    nc.tensor.transpose(bank[:, c - c0, :], gate_col[:, c : c + 1].to_broadcast([P, P]), identity[:])
+                nc.scalar.copy(gate_sb[:, c0 * P : (c0 + 4) * P], bank[:].rearrange("p c n -> p (c n)"))
 
         def second_layer(e):
+            spent = raws["w3", e, PASSES - 1]
+            gelus[0] = spent[:, 0:2, :].rearrange("p j (q u t) -> p j q u t", u=2, t=4)[:, :, :, 0, :]
+            gelus[1] = spent[:, 2, :].rearrange("p (j q t) -> p j q t", j=2, t=4)
+            for half in range(2):
+                nc.scalar.activation(gelus[half], banks["w1", half][:].rearrange("p t (j q) -> p j q t", j=2), GELU)
+            chunk = ("w2", e, 0)
+            grouped = work.tile([P, 4 * N], BF16, name="w2_grouped", tag="last1", bufs=1, align_bytes=64)[:]
+            dst = grouped.rearrange("p (n pair j) -> p n j pair", pair=2, j=4)
+            src = raws[chunk][:].rearrange("p j (n pair) -> p n j pair", pair=2)
+            cut = N // 4 if e == LAST else N // 2
+            nc.vector.tensor_copy(dst[:, :cut], src[:, :cut])
+            if e == LAST:
+                nc.scalar.copy(dst[:, cut:], src[:, cut:])
+            load_ahead(chunk)
+            if e == 0:
+                h = work.tile([P, C, 4], BF16, name="h_first", tag="late_words", bufs=1, align_bytes=64)
+            else:
+                h = work.tile([P, C, 4], BF16, name="h", align_bytes=64)
+            for half in range(2):
+                nc.vector.tensor_tensor(
+                    h[:, half * SLOT_HALF : (half + 1) * SLOT_HALF, :].rearrange("p (j q) t -> p j q t", j=2),
+                    banks["w3", half][:].rearrange("p t (j q) -> p j q t", j=2),
+                    gelus[half],
+                    MULT,
+                )
+            new_codes(chunk, N)
+            quantize(chunk, 0, grouped)
             h_words = work.tile([P, C], U32, name="h_words", align_bytes=64)
             if e == 0:
                 h_scales = work.tile([P, C], U8, name="h_scales_first", tag="late_bytes", bufs=1, align_bytes=64)
             else:
                 h_scales = work.tile([P, C], U8, name="h_scales", align_bytes=64)
-            y = psum.tile([P, 2, C], F32, name="y", bufs=2)
-            nc.vector.quantize_mx(out=h_words[:].bitcast(FP8X4), scales=h_scales[:], in_=hidden["h"][:].rearrange("p n t -> p (n t)"))
-            words, scales = weights["w2", e, 0]
-            for b in range(2):
+            nc.vector.quantize_mx(out=h_words[:].bitcast(FP8X4), scales=h_scales[:], in_=h[:].rearrange("p c t -> p (c t)"))
+            words, scales = weights[chunk]
+            y = psum.tile([P, BLOCKS, C], F32, name="y", bufs=2)
+            for b in range(BLOCKS):
                 nc.tensor.matmul_mx(
                     out=y[:, b, :],
-                    lhsT=words[:, b * 128 : (b + 1) * 128].bitcast(FP8X4),
-                    lhsT_scale=scales[:, b * 128 : (b + 1) * 128],
+                    lhsT=words[:, b * P : (b + 1) * P].bitcast(FP8X4),
+                    lhsT_scale=scales[:, b * P : (b + 1) * P],
                     rhs=h_words[:].bitcast(FP8X4),
                     rhs_scale=h_scales[:],
                     start=True,
@@ -197,87 +219,48 @@ def tile_moe_res_glu_gelu_kernel(tc, xT, xr, w1, w3, w2, gate, offs, out):
                 )
             ys[e] = y
 
-        def scatter(e, b):
-            nc.vector.tensor_tensor(win[b][:].indirect(offsets[:, e * 16 : (e + 1) * 16]), ys[e, b], gate_sb[:, e * C : (e + 1) * C], MULT)
+        def put_back(e, b, staged):
+            nc.scalar.copy(staged, ys[e][:, b, :])
+            window = win[b][:].indirect(offsets[:, e * LIST_COLS : (e + 1) * LIST_COLS])
+            nc.vector.tensor_tensor(window, staged, gate_sb[:, e * C : (e + 1) * C], MULT)
 
-        def fetch_y(e, b, y_sb):
-            nc.scalar.copy(y_sb, ys[e][:, b, :])
-            ys[e, b] = y_sb
+        def finish(b):
+            xr_sb = raws["xr", 0, b]
+            for x0, x1 in zip(CUTS[b], CUTS[b][1:]):
+                nc.vector.tensor_tensor(xr_sb[:, x0:x1], win[b][:, x0:x1], xr_sb[:, x0:x1], ADD)
+                nc.sync.dma_start(out[b * P : (b + 1) * P, x0:x1], xr_sb[:, x0:x1])
 
-        def finish(engine, b, c0, c1):
-            xr_sb = raws[pos["xr", 0, b, 0]]
-            engine.tensor_tensor(xr_sb[:, c0:c1], win[b][:, c0:c1], xr_sb[:, c0:c1], ADD)
-            nc.sync.dma_start(out[b * P : (b + 1) * P, c0:c1], xr_sb[:, c0:c1])
-
-        nc.sync.dma_start(offsets[:], offs)
         nc.vector.memset(gate_rows[:], 0.0)
-        tok_raws = [load_tokens(*TOKEN_LOADS[0])]
+        tok_raws = [load_tokens(0)]
+        nc.sync.dma_start(offsets[:], offs)
         nc.sync.dma_start(gate_rows[0:8, :], gate[0].rearrange("(c n) -> c n", c=8))
-        tok_raws.append(load_tokens(*TOKEN_LOADS[1]))
+        tok_raws.append(load_tokens(1))
         for i in range(LOOKAHEAD):
             load(i)
         nc.gpsimd.memset(tok_bytes[:], 0)
-        for b in range(2):
+        for b in range(BLOCKS):
             nc.vector.memset(win[b][:], 0.0)
 
-        pos = {c: i for i, c in enumerate(chunks)}
-
-        def prepare(kind, e, s=0, c=0):
-            i = pos[kind, e, s, c]
-            interleave(i)
-            if i + LOOKAHEAD < len(chunks):
-                load(i + LOOKAHEAD)
-            quantize(i)
-
         spread_gate()
-        for raw, (s, t0, t1) in zip(tok_raws, TOKEN_LOADS):
-            quantize_tokens(raw, s, t0, t1)
-            if (s, t1) == (0, T):
-                gather(0, tok_words[0], U32, 0, E, "words0")
+        quantize_tokens(tok_raws[0], 0)
+        gather(0, tok_words[0], U32, 0, E, "words0")
+        quantize_tokens(tok_raws[1], 1)
         gather(1, tok_words[1], U32, 0, EARLY, "words1")
         gather("bytes", tok_bytes, U8, 0, EARLY, "bytes")
         for e in range(E):
-            prepare("w1", e, 0)
-            prepare("w1", e, 1)
-            for half in range(2):
-                first_layer("w1", e, half)
+            prepare(("w1", e, 0))
+            prepare(("w1", e, 1))
+            if e > 0:
+                put_back(e - 1, 0, raws["w1", e, 1][:, 0, :C])
+            prepare(("w3", e, 0))
+            prepare_last(e)
+            second_layer(e)
             if e == 0:
                 gather(1, tok_words[1], U32, EARLY, E, "late_words")
-            if e == 1:
-                fetch_y(0, 0, spent["w1", 1][:, 0, :C])
-                scatter(0, 0)
-            prepare("w3", e, 0)
-            if e == 2:
-                fetch_y(1, 0, spent["w3", 0][:, 0, :C])
-                scatter(1, 0)
-            prepare("w3", e, 1)
-            if e > 2:
-                fetch_y(e - 1, 0, spent["w3", 1][:, 2, :C])
-            if 0 < e < E - 1:
-                fetch_y(e - 1, 1, spent["w3", 1][:, 3, :C])
-            gelu(0)
-            gelu(1)
-            if 0 < e < E - 1:
-                scatter(e - 1, 1)
-            prepare("w2", e)
-            if e > 2:
-                scatter(e - 1, 0)
-            for half in range(2):
-                first_layer("w3", e, half)
-                product(e, half)
-            second_layer(e)
-            if e == E - 1:
-                fetch_y(e - 1, 1, spent["w3", 1][:, 1, :C])
-                scatter(e - 1, 1)
-            if e == 0:
                 gather("bytes", tok_bytes, U8, EARLY, E, "late_bytes")
-        last = slice((E - 1) * 16, E * 16)
-        fetch_y(E - 1, 0, spent["w1", 1][:, 0, :C])
-        gated = spent["w1", 1][:, 1, :C]
-        nc.vector.tensor_tensor(gated, ys[E - 1][:, 1, :], gate_sb[:, (E - 1) * C :], MULT)
-        scatter(E - 1, 0)
-        nc.vector.tensor_copy(win[1][:].indirect(offsets[:, last]), gated)
-        for c0 in (0, 256):
-            finish(nc.gpsimd, 0, c0, c0 + 256)
-        for b, c0 in ((0, 512), (0, 1024), (1, 0), (1, 512), (1, 1024)):
-            finish(nc.vector, b, c0, c0 + 512)
+            else:
+                put_back(e - 1, 1, raws["w3", e, PASSES - 1][:, 2 if e == LAST else 3, :C])
+        for b in range(BLOCKS):
+            put_back(LAST, b, raws["w1", LAST, 0][:, b, :C])
+        for b in range(BLOCKS):
+            finish(b)

@@ -13,6 +13,7 @@ U8 = mybir.dt.uint8
 FP8X4 = mybir.dt.float8_e4m3fn_x4
 MULT, ADD = mybir.AluOpType.mult, mybir.AluOpType.add
 GELU = mybir.ActivationFunctionType.Gelu_apprx_tanh
+COPY = mybir.ActivationFunctionType.Copy
 
 P = 128
 PASS_K = 512
@@ -22,15 +23,14 @@ SLOT_HALF = 128
 LIST_COLS = C // 16
 LAST = E - 1
 TOKEN_CHUNK = 512
-Q = 64
 V_TOKENS = 40
-V_CLOSING = 48
-EARLY = 2
-CUTS = ((0, 256, 512, 1024, T), (0, 512, 1024, T))
+CUTS = ((0, 128, 512, 1024, T), (0, 512, 1024, T))
 LOOKAHEAD = 8
 RAW_BUFS = LOOKAHEAD + 2
 GROUPED_BUFS = 6
-BANK_BUFS = 3
+BANK_BUFS = {"w1": 2, "w3": 3}
+EARLY = 2
+V_SHARES = ((0, 0, 64), (0, 32, 64), (128, 24, 48))
 
 
 def tile_moe_res_glu_gelu_kernel(tc, xT, xr, w1, w3, w2, gate, offs, out):
@@ -41,7 +41,7 @@ def tile_moe_res_glu_gelu_kernel(tc, xT, xr, w1, w3, w2, gate, offs, out):
         tc.tile_pool(name="grp", bufs=GROUPED_BUFS) as grp,
         tc.tile_pool(name="codes", bufs=2) as codes,
         tc.tile_pool(name="work", bufs=2) as work,
-        tc.psum_pool(name="psum", bufs=1) as psum,
+        tc.psum_pool(name="psum", bufs=2) as psum,
     ):
         offsets = held.tile([P, E * LIST_COLS], U16, name="offsets")
         tok_words = [held.tile([P, T], U32, name=f"tok_words{s}", align_bytes=64) for s in range(PASSES)]
@@ -57,22 +57,17 @@ def tile_moe_res_glu_gelu_kernel(tc, xT, xr, w1, w3, w2, gate, offs, out):
             chunks += [("w1", e, 0), ("w1", e, 1), ("w3", e, 0), ("w3", e, 1), ("w2", e, 0)]
         chunks += [("xr", 0, b) for b in range(BLOCKS)]
         pos = {chunk: i for i, chunk in enumerate(chunks)}
-        raws, weights, banks, gelus, ys, slots = {}, {}, {}, {}, {}, {}
-        first_layer_in = {"w1": w1, "w3": w3}
+        raws, banks, ys, slots = {}, {}, {}, {}
+        weights_in = {"w1": w1, "w3": w3, "w2": w2}
 
         def load(i):
             kind, e, s = chunks[i]
-            if kind == "w2":
-                raw = rawp.tile([P, 4, N], F32, name="raw2", tag="raw")
-                rows = w2[e].rearrange("(q u r v) n -> r q u (v n)", u=2, r=2, v=2)
-                for r in range(2):
-                    nc.sync.dma_start(raw[r:P:2].rearrange("p (u v) n -> p u (v n)", u=2), rows[r])
-            elif kind == "xr":
-                raw = rawp.tile([P, T], F32, name="xr_sb", tag="raw")
+            if kind == "xr":
+                raw = rawp.tile([P, T], F32, name="xr_sb", tag="raw", align_bytes=64)
                 nc.sync.dma_start(raw[:], xr[s * P : (s + 1) * P, :])
             else:
-                raw = rawp.tile([P, 4, H], F32, name="raw")
-                rows = first_layer_in[kind][e, s * PASS_K : (s + 1) * PASS_K, :]
+                rows = weights_in[kind][e, s * PASS_K : (s + 1) * PASS_K, :]
+                raw = rawp.tile([P, 4, rows.shape[1]], F32, name="raw", tag="raw", align_bytes=64)
                 nc.sync.dma_start(raw[:], rows.rearrange("(p j) i -> p j i", j=4))
             raws[chunks[i]] = raw
 
@@ -80,34 +75,31 @@ def tile_moe_res_glu_gelu_kernel(tc, xT, xr, w1, w3, w2, gate, offs, out):
             if pos[chunk] + LOOKAHEAD < len(chunks):
                 load(pos[chunk] + LOOKAHEAD)
 
-        def new_codes(chunk, width):
+        def shared_copy(dst, src, axis, cut):
+            size = dst.shape[axis]
+            head = (slice(None),) * axis
+            if cut > 0:
+                nc.vector.tensor_copy(dst[head + (slice(0, cut),)], src[head + (slice(0, cut),)])
+            if cut < size:
+                nc.scalar.copy(dst[head + (slice(cut, size),)], src[head + (slice(cut, size),)])
+
+        def quantize(name, grouped):
+            words, scales = new_codes(name, grouped.shape[1] // 4)
+            nc.vector.quantize_mx(out=words[:].bitcast(FP8X4), scales=scales[:], in_=grouped)
+            return words, scales
+
+        def new_codes(name, width):
+            words = codes.tile([P, width], U32, name=name + "_words", align_bytes=64)
+            scales = codes.tile([P, width], U8, name=name + "_scales", align_bytes=64)
+            return words, scales
+
+        def multiply(chunk, words, scales, tiles):
             kind, e, s = chunk
-            words = codes.tile([P, width], U32, name=f"{kind}_words{s}", align_bytes=64)[:]
-            scales = codes.tile([P, width], U8, name=f"{kind}_scales{s}", align_bytes=64)[:]
-            weights[chunk] = (words, scales)
-
-        def interleave(chunk, by_u, vector_q):
-            src = raws[chunk][:].rearrange("p j (q u r v) -> p u q j r v", u=2, r=2, v=2)
-            dst = [part.rearrange("p (v q r j) -> p q j r v", v=2, r=2, j=4) for part in by_u]
-            nc.scalar.copy(dst[0], src[:, 0])
-            if vector_q:
-                nc.vector.tensor_copy(dst[1][:, :vector_q], src[:, 1, :vector_q])
-            if vector_q < Q:
-                nc.scalar.copy(dst[1][:, vector_q:], src[:, 1, vector_q:])
-
-        def quantize(chunk, first_col, grouped):
-            words, scales = weights[chunk]
-            made = slice(first_col, first_col + grouped.shape[1] // 4)
-            nc.vector.quantize_mx(out=words[:, made].bitcast(FP8X4), scales=scales[:, made], in_=grouped)
-
-        def multiply(chunk, tiles, closing):
-            kind, e, s = chunk
-            words, scales = weights[chunk]
             for half in range(2):
                 if s == 0:
-                    banks[kind, half] = psum.tile([P, 4, SLOT_HALF], F32, name=f"bank_{kind}", bufs=BANK_BUFS)
+                    banks[kind, half] = psum.tile([P, 4, SLOT_HALF], F32, name=f"bank_{kind}", bufs=BANK_BUFS[kind])
                 moving = slice(half * SLOT_HALF, (half + 1) * SLOT_HALF)
-                for t in tiles:
+                for t in tiles[half]:
                     stationary = slice(t * P, (t + 1) * P)
                     nc.tensor.matmul_mx(
                         out=banks[kind, half][:, t, :],
@@ -116,27 +108,33 @@ def tile_moe_res_glu_gelu_kernel(tc, xT, xr, w1, w3, w2, gate, offs, out):
                         rhs=slots[s, e][:, moving].bitcast(FP8X4),
                         rhs_scale=slots["bytes", e][4 * s : P, moving],
                         start=(s, t) == (0, 0),
-                        stop=closing and (s, t) == (PASSES - 1, tiles[-1]),
+                        stop=(s, t) == (PASSES - 1, tiles[half][-1]),
                     )
 
-        def prepare(chunk):
+        def first_layer(chunk, vector_cols):
+            kind, e, s = chunk
             grouped = grp.tile([P, 4 * H], BF16, name="grouped", align_bytes=64)
-            interleave(chunk, (grouped[:, : 2 * H], grouped[:, 2 * H :]), 0)
+            dst = grouped[:].rearrange("p (u v m j) -> p m u j v", u=2, v=2, j=4)
+            src = raws[chunk][:].rearrange("p j (m u v) -> p m u j v", u=2, v=2)
+            shared_copy(dst, src, 1, vector_cols)
             load_ahead(chunk)
-            new_codes(chunk, H)
-            quantize(chunk, 0, grouped[:])
-            multiply(chunk, range(4), True)
+            words, scales = quantize(f"{kind}_{s}", grouped[:])
+            multiply(chunk, words, scales, (range(4), range(4)))
 
-        def prepare_last(e):
+        def last_chunk(e):
             chunk = ("w3", e, PASSES - 1)
-            by_u = [work.tile([P, 2 * H], BF16, name=f"last{u}", tag=f"last{u}", bufs=1, align_bytes=64)[:] for u in range(2)]
-            interleave(chunk, by_u, V_CLOSING if e == LAST else Q)
+            src = raws[chunk][:].rearrange("p j (m u v) -> p u m j v", u=2, v=2)
+            tags = ("last0" if e > 0 else "late_words", "last1")
+            by_u = [work.tile([P, 2 * H], BF16, name=f"last{u}", tag=tags[u], bufs=1, align_bytes=64) for u in range(2)]
+            dst = [part[:].rearrange("p (v m j) -> p m j v", v=2, j=4) for part in by_u]
+            nc.scalar.copy(dst[0], src[:, 0])
+            nc.vector.tensor_copy(dst[1], src[:, 1])
             load_ahead(chunk)
-            new_codes(chunk, H)
-            order = (0, 1) if e == LAST else (1, 0)
-            for u in order:
-                quantize(chunk, u * H // 2, by_u[u])
-                multiply(chunk, (2 * u, 2 * u + 1), u == order[1])
+            words, scales = new_codes("w3_1", H)
+            for u in (1, 0):
+                made = slice(u * H // 2, (u + 1) * H // 2)
+                nc.vector.quantize_mx(out=words[:, made].bitcast(FP8X4), scales=scales[:, made], in_=by_u[u][:])
+            multiply(chunk, words, scales, ((2, 3, 0, 1), (0, 1, 2, 3)))
 
         def load_tokens(s):
             raw = held.tile([P, 4, T], F32, name=f"tok_raw{s}")
@@ -149,9 +147,7 @@ def tile_moe_res_glu_gelu_kernel(tc, xT, xr, w1, w3, w2, gate, offs, out):
                 grouped = grp.tile([P, TOKEN_CHUNK * 4], BF16, name="grouped", align_bytes=64)
                 dst = grouped[:].rearrange("p (x pair j) -> p x j pair", pair=2, j=4)
                 src = raw[:, :, tokens].rearrange("p j (x pair) -> p x j pair", pair=2)
-                cut = dst.shape[1] * V_TOKENS // 64
-                nc.vector.tensor_copy(dst[:, :cut], src[:, :cut])
-                nc.scalar.copy(dst[:, cut:], src[:, cut:])
+                shared_copy(dst, src, 1, dst.shape[1] * V_TOKENS // 64)
                 nc.vector.quantize_mx(out=tok_words[s][:, tokens].bitcast(FP8X4), scales=tok_bytes[4 * s : P, tokens], in_=grouped[:])
 
         def gather(what, source, dtype, e0, e1, tag):
@@ -162,67 +158,81 @@ def tile_moe_res_glu_gelu_kernel(tc, xT, xr, w1, w3, w2, gate, offs, out):
 
         def spread_gate():
             make_identity(nc, identity[:])
-            turned = psum.tile([P, P], F32, name="gate_turned", tag="y", bufs=2)
+            turned = psum.tile([P, P], F32, name="gate_turned", tag="y", bufs=3)
             nc.tensor.transpose(turned[:], gate_rows[:], identity[:])
             nc.scalar.copy(gate_col[:], turned[:, :8])
             for c0 in (0, 4):
-                bank = psum.tile([P, 4, P], F32, name="gate_bank", tag="y", bufs=2)
+                bank = psum.tile([P, 4, P], F32, name="gate_bank", tag="y", bufs=3)
                 for c in range(c0, c0 + 4):
                     nc.tensor.transpose(bank[:, c - c0, :], gate_col[:, c : c + 1].to_broadcast([P, P]), identity[:])
                 nc.scalar.copy(gate_sb[:, c0 * P : (c0 + 4) * P], bank[:].rearrange("p c n -> p (c n)"))
 
-        def second_layer(e):
+        def gelu(e):
             spent = raws["w3", e, PASSES - 1]
-            gelus[0] = spent[:, 0:2, :].rearrange("p j (q u t) -> p j q u t", u=2, t=4)[:, :, :, 0, :]
-            gelus[1] = spent[:, 2, :].rearrange("p (j q t) -> p j q t", j=2, t=4)
+            values = [spent[:, 3 - half, :].rearrange("p (c t) -> p c t", t=4) for half in range(2)]
             for half in range(2):
-                nc.scalar.activation(gelus[half], banks["w1", half][:].rearrange("p t (j q) -> p j q t", j=2), GELU)
-            chunk = ("w2", e, 0)
-            grouped = work.tile([P, 4 * N], BF16, name="w2_grouped", tag="last1", bufs=1, align_bytes=64)[:]
-            dst = grouped.rearrange("p (n pair j) -> p n j pair", pair=2, j=4)
-            src = raws[chunk][:].rearrange("p j (n pair) -> p n j pair", pair=2)
-            cut = N // 4 if e == LAST else N // 2
-            nc.vector.tensor_copy(dst[:, :cut], src[:, :cut])
+                nc.scalar.activation(values[half], banks["w1", half][:].rearrange("p t c -> p c t"), GELU)
+            return values
+
+        def round_w2(engine_copy, e, cols, tag):
+            grouped = work.tile([P, 4 * (cols.stop - cols.start)], BF16, name="w2_grouped", tag=tag, bufs=1, align_bytes=64)[:]
+            engine_copy(
+                grouped.rearrange("p (n pair j) -> p n j pair", pair=2, j=4),
+                raws["w2", e, 0][:, :, cols].rearrange("p j (n pair) -> p n j pair", pair=2),
+            )
+            return grouped
+
+        def second_layer(e, values):
+            if e < LAST:
+                grouped = round_w2(nc.vector.tensor_copy, e, slice(0, N), "last0" if e > 0 else "late_bytes")
+            else:
+                grouped = round_w2(nc.vector.tensor_copy, e, slice(0, P), "last0")
+                grouped_late = round_w2(nc.scalar.copy, e, slice(P, N), "w2_late")
+            load_ahead(("w2", e, 0))
+            h = work.tile([P, 2, SLOT_HALF, 4], BF16, name="h", tag="h", bufs=1, align_bytes=64)[:]
+            for half in range(2):
+                nc.vector.tensor_tensor(h[:, half], banks["w3", half][:].rearrange("p t c -> p c t"), values[half], MULT)
+            words, scales = quantize("w2", grouped)
+            stationary = [(words[:, b * P : (b + 1) * P], scales[:, b * P : (b + 1) * P]) for b in range(words.shape[1] // P)]
+            h_words, h_scales = new_codes("h", C)
+            width = SLOT_HALF if e == LAST else C
+            pieces = [slice(c0, c0 + width) for c0 in range(0, C, width)]
+            flat = h.rearrange("p a c t -> p (a c) t")
+            for made in pieces:
+                nc.vector.quantize_mx(out=h_words[:, made].bitcast(FP8X4), scales=h_scales[:, made], in_=flat[:, made].rearrange("p c t -> p (c t)"))
             if e == LAST:
-                nc.scalar.copy(dst[:, cut:], src[:, cut:])
-            load_ahead(chunk)
-            if e == 0:
-                h = work.tile([P, C, 4], BF16, name="h_first", tag="late_words", bufs=1, align_bytes=64)
-            else:
-                h = work.tile([P, C, 4], BF16, name="h", align_bytes=64)
-            for half in range(2):
-                nc.vector.tensor_tensor(
-                    h[:, half * SLOT_HALF : (half + 1) * SLOT_HALF, :].rearrange("p (j q) t -> p j q t", j=2),
-                    banks["w3", half][:].rearrange("p t (j q) -> p j q t", j=2),
-                    gelus[half],
-                    MULT,
-                )
-            new_codes(chunk, N)
-            quantize(chunk, 0, grouped)
-            h_words = work.tile([P, C], U32, name="h_words", align_bytes=64)
-            if e == 0:
-                h_scales = work.tile([P, C], U8, name="h_scales_first", tag="late_bytes", bufs=1, align_bytes=64)
-            else:
-                h_scales = work.tile([P, C], U8, name="h_scales", align_bytes=64)
-            nc.vector.quantize_mx(out=h_words[:].bitcast(FP8X4), scales=h_scales[:], in_=h[:].rearrange("p c t -> p (c t)"))
-            words, scales = weights[chunk]
-            y = psum.tile([P, BLOCKS, C], F32, name="y", bufs=2)
-            for b in range(BLOCKS):
+                words, scales = quantize("w2_late", grouped_late)
+                stationary.append((words[:], scales[:]))
+
+            def product(y, b, made):
                 nc.tensor.matmul_mx(
-                    out=y[:, b, :],
-                    lhsT=words[:, b * P : (b + 1) * P].bitcast(FP8X4),
-                    lhsT_scale=scales[:, b * P : (b + 1) * P],
-                    rhs=h_words[:].bitcast(FP8X4),
-                    rhs_scale=h_scales[:],
+                    out=y[:, made],
+                    lhsT=stationary[b][0].bitcast(FP8X4),
+                    lhsT_scale=stationary[b][1],
+                    rhs=h_words[:, made].bitcast(FP8X4),
+                    rhs_scale=h_scales[:, made],
                     start=True,
                     stop=True,
                 )
-            ys[e] = y
+
+            if e < LAST:
+                y = psum.tile([P, BLOCKS, C], F32, name="y", tag="y", bufs=3)
+                ys[e] = y[:]
+                for b in range(BLOCKS):
+                    ys[e, b] = y[:, b, :]
+            else:
+                for b in range(BLOCKS):
+                    ys[e, b] = psum.tile([P, C], F32, name=f"y{b}", tag="y", bufs=3)[:]
+            for b in range(BLOCKS):
+                for made in pieces:
+                    product(ys[e, b], b, made)
+
+        def window(e, b):
+            return win[b][:].indirect(offsets[:, e * LIST_COLS : (e + 1) * LIST_COLS])
 
         def put_back(e, b, staged):
-            nc.scalar.copy(staged, ys[e][:, b, :])
-            window = win[b][:].indirect(offsets[:, e * LIST_COLS : (e + 1) * LIST_COLS])
-            nc.vector.tensor_tensor(window, staged, gate_sb[:, e * C : (e + 1) * C], MULT)
+            nc.vector.tensor_tensor(staged, ys[e, b], gate_sb[:, e * C : (e + 1) * C], MULT)
+            nc.scalar.activation(window(e, b), staged, COPY)
 
         def finish(b):
             xr_sb = raws["xr", 0, b]
@@ -241,26 +251,37 @@ def tile_moe_res_glu_gelu_kernel(tc, xT, xr, w1, w3, w2, gate, offs, out):
         for b in range(BLOCKS):
             nc.vector.memset(win[b][:], 0.0)
 
-        spread_gate()
         quantize_tokens(tok_raws[0], 0)
+        spread_gate()
         gather(0, tok_words[0], U32, 0, E, "words0")
         quantize_tokens(tok_raws[1], 1)
         gather(1, tok_words[1], U32, 0, EARLY, "words1")
         gather("bytes", tok_bytes, U8, 0, EARLY, "bytes")
         for e in range(E):
-            prepare(("w1", e, 0))
-            prepare(("w1", e, 1))
+            for chunk, share in zip(chunks[5 * e : 5 * e + 3], V_SHARES[min(e, 2)]):
+                first_layer(chunk, share)
+            last_chunk(e)
+            values = gelu(e)
             if e > 0:
-                put_back(e - 1, 0, raws["w1", e, 1][:, 0, :C])
-            prepare(("w3", e, 0))
-            prepare_last(e)
-            second_layer(e)
-            if e == 0:
-                gather(1, tok_words[1], U32, EARLY, E, "late_words")
-                gather("bytes", tok_bytes, U8, EARLY, E, "late_bytes")
+                staged = work.tile([P, BLOCKS, C], F32, name="staged_late", tag="last1", bufs=1, align_bytes=64)
+                if e < LAST:
+                    gates = gate_sb[:, (e - 1) * C : e * C].unsqueeze(1).to_broadcast([P, BLOCKS, C])
+                    nc.vector.tensor_tensor(staged[:], ys[e - 1], gates, MULT)
+                    for b in range(BLOCKS):
+                        nc.scalar.activation(window(e - 1, b), staged[:, b, :], COPY)
+                else:
+                    put_back(e - 1, 0, staged[:, 0, :])
             else:
-                put_back(e - 1, 1, raws["w3", e, PASSES - 1][:, 2 if e == LAST else 3, :C])
+                gather(1, tok_words[1], U32, EARLY, E, "late_words")
+            second_layer(e, values)
+            if e == LAST:
+                put_back(e - 1, 1, work.tile([P, C], F32, name="staged_last", tag="h", bufs=1, align_bytes=64)[:])
+            if e == 0:
+                gather("bytes", tok_bytes, U8, EARLY, E, "late_bytes")
+        staged = [work.tile([P, C], F32, name=f"staged{b}") for b in range(BLOCKS)]
         for b in range(BLOCKS):
-            put_back(LAST, b, raws["w1", LAST, 0][:, b, :C])
+            nc.vector.tensor_tensor(staged[b][:], ys[LAST, b], gate_sb[:, LAST * C :], MULT)
+        nc.vector.tensor_copy(window(LAST, 0), staged[0][:])
+        nc.scalar.activation(window(LAST, 1), staged[1][:], COPY)
         for b in range(BLOCKS):
             finish(b)

@@ -275,13 +275,12 @@ def tile_moe_res_glu_gelu_kernel(tc, xT, xr, w1, w3, w2, gate, offs, out):
                 gather(1, tok_words[1], U32, EARLY, E, "late_words")
             second_layer(e, values)
             if e == LAST:
+                plain = work.tile([P, C], F32, name="plain_y", bufs=1)
+                nc.scalar.copy(plain[:], ys[LAST, 0])
                 put_back(e - 1, 1, work.tile([P, C], F32, name="staged_last", tag="h", bufs=1, align_bytes=64)[:])
             if e == 0:
                 gather("bytes", tok_bytes, U8, EARLY, E, "late_bytes")
-        staged = [work.tile([P, C], F32, name=f"staged{b}") for b in range(BLOCKS)]
-        for b in range(BLOCKS):
-            nc.vector.tensor_tensor(staged[b][:], ys[LAST, b], gate_sb[:, LAST * C :], MULT)
-        nc.vector.tensor_copy(window(LAST, 0), staged[0][:])
-        nc.scalar.activation(window(LAST, 1), staged[1][:], COPY)
+        put_back(LAST, 1, work.tile([P, C], F32, name="staged", bufs=1)[:])
+        nc.vector.tensor_tensor(window(LAST, 0), plain[:], gate_sb[:, LAST * C :], MULT)
         for b in range(BLOCKS):
             finish(b)

@@ -30,6 +30,7 @@ RAW_BUFS = LOOKAHEAD + 2
 GROUPED_BUFS = 6
 BANK_BUFS = {"w1": 2, "w3": 3}
 EARLY = 2
+V_CLOSING = 32
 V_SHARES = ((0, 0, 64), (0, 32, 64), (128, 24, 48))
 
 
@@ -124,17 +125,22 @@ def tile_moe_res_glu_gelu_kernel(tc, xT, xr, w1, w3, w2, gate, offs, out):
         def last_chunk(e):
             chunk = ("w3", e, PASSES - 1)
             src = raws[chunk][:].rearrange("p j (m u v) -> p u m j v", u=2, v=2)
-            tags = ("last0" if e > 0 else "late_words", "last1")
+            first, second = (0, 1) if e == LAST else (1, 0)
+            tags = {first: "quantised_first", second: "quantised_second" if e > 0 else "late_words"}
             by_u = [work.tile([P, 2 * H], BF16, name=f"last{u}", tag=tags[u], bufs=1, align_bytes=64) for u in range(2)]
             dst = [part[:].rearrange("p (v m j) -> p m j v", v=2, j=4) for part in by_u]
-            nc.scalar.copy(dst[0], src[:, 0])
+            cut = V_CLOSING if e == LAST else 0
+            if cut:
+                nc.vector.tensor_copy(dst[0][:, :cut], src[:, 0, :cut])
+            nc.scalar.copy(dst[0][:, cut:], src[:, 0, cut:])
             nc.vector.tensor_copy(dst[1], src[:, 1])
             load_ahead(chunk)
             words, scales = new_codes("w3_1", H)
-            for u in (1, 0):
+            for u in (first, second):
                 made = slice(u * H // 2, (u + 1) * H // 2)
                 nc.vector.quantize_mx(out=words[:, made].bitcast(FP8X4), scales=scales[:, made], in_=by_u[u][:])
-            multiply(chunk, words, scales, ((2, 3, 0, 1), (0, 1, 2, 3)))
+            orders = ((0, 1, 2, 3), (2, 3, 0, 1))
+            multiply(chunk, words, scales, (orders[first], orders[second]))
 
         def load_tokens(s):
             raw = held.tile([P, 4, T], F32, name=f"tok_raw{s}")
@@ -184,9 +190,9 @@ def tile_moe_res_glu_gelu_kernel(tc, xT, xr, w1, w3, w2, gate, offs, out):
 
         def second_layer(e, values):
             if e < LAST:
-                grouped = round_w2(nc.vector.tensor_copy, e, slice(0, N), "last0" if e > 0 else "late_bytes")
+                grouped = round_w2(nc.vector.tensor_copy, e, slice(0, N), "quantised_second" if e > 0 else "late_bytes")
             else:
-                grouped = round_w2(nc.vector.tensor_copy, e, slice(0, P), "last0")
+                grouped = round_w2(nc.vector.tensor_copy, e, slice(0, P), "quantised_second")
                 grouped_late = round_w2(nc.scalar.copy, e, slice(P, N), "w2_late")
             load_ahead(("w2", e, 0))
             h = work.tile([P, 2, SLOT_HALF, 4], BF16, name="h", tag="h", bufs=1, align_bytes=64)[:]
@@ -263,7 +269,7 @@ def tile_moe_res_glu_gelu_kernel(tc, xT, xr, w1, w3, w2, gate, offs, out):
             last_chunk(e)
             values = gelu(e)
             if e > 0:
-                staged = work.tile([P, BLOCKS, C], F32, name="staged_late", tag="last1", bufs=1, align_bytes=64)
+                staged = work.tile([P, BLOCKS, C], F32, name="staged_late", tag="quantised_first", bufs=1, align_bytes=64)
                 if e < LAST:
                     gates = gate_sb[:, (e - 1) * C : e * C].unsqueeze(1).to_broadcast([P, BLOCKS, C])
                     nc.vector.tensor_tensor(staged[:], ys[e - 1], gates, MULT)

@@ -23,7 +23,7 @@ SLOT_HALF = 128
 LIST_COLS = C // 16
 LAST = E - 1
 TOKEN_CHUNK = 512
-V_TOKENS = 40
+V_TOKENS = (32, 40)
 CUTS = ((0, 128, 512, 1024, T), (0, 512, 1024, T))
 LOOKAHEAD = 8
 RAW_BUFS = LOOKAHEAD + 2
@@ -31,7 +31,7 @@ GROUPED_BUFS = 6
 BANK_BUFS = {"w1": 2, "w3": 3}
 EARLY = 2
 V_CLOSING = 32
-V_SHARES = ((0, 0, 64), (0, 32, 64), (128, 24, 48))
+V_SHARES = ((0, 0, 64), (0, 48, 64), (128, 40, 48))
 
 
 def tile_moe_res_glu_gelu_kernel(tc, xT, xr, w1, w3, w2, gate, offs, out):
@@ -153,7 +153,7 @@ def tile_moe_res_glu_gelu_kernel(tc, xT, xr, w1, w3, w2, gate, offs, out):
                 grouped = grp.tile([P, TOKEN_CHUNK * 4], BF16, name="grouped", align_bytes=64)
                 dst = grouped[:].rearrange("p (x pair j) -> p x j pair", pair=2, j=4)
                 src = raw[:, :, tokens].rearrange("p j (x pair) -> p x j pair", pair=2)
-                shared_copy(dst, src, 1, dst.shape[1] * V_TOKENS // 64)
+                shared_copy(dst, src, 1, dst.shape[1] * V_TOKENS[s] // 64)
                 nc.vector.quantize_mx(out=tok_words[s][:, tokens].bitcast(FP8X4), scales=tok_bytes[4 * s : P, tokens], in_=grouped[:])
 
         def gather(what, source, dtype, e0, e1, tag):
@@ -223,7 +223,6 @@ def tile_moe_res_glu_gelu_kernel(tc, xT, xr, w1, w3, w2, gate, offs, out):
 
             if e < LAST:
                 y = psum.tile([P, BLOCKS, C], F32, name="y", tag="y", bufs=3)
-                ys[e] = y[:]
                 for b in range(BLOCKS):
                     ys[e, b] = y[:, b, :]
             else:
@@ -270,13 +269,8 @@ def tile_moe_res_glu_gelu_kernel(tc, xT, xr, w1, w3, w2, gate, offs, out):
             values = gelu(e)
             if e > 0:
                 staged = work.tile([P, BLOCKS, C], F32, name="staged_late", tag="quantised_first", bufs=1, align_bytes=64)
-                if e < LAST:
-                    gates = gate_sb[:, (e - 1) * C : e * C].unsqueeze(1).to_broadcast([P, BLOCKS, C])
-                    nc.vector.tensor_tensor(staged[:], ys[e - 1], gates, MULT)
-                    for b in range(BLOCKS):
-                        nc.scalar.activation(window(e - 1, b), staged[:, b, :], COPY)
-                else:
-                    put_back(e - 1, 0, staged[:, 0, :])
+                for b in range(BLOCKS if e < LAST else 1):
+                    put_back(e - 1, b, staged[:, b, :])
             else:
                 gather(1, tok_words[1], U32, EARLY, E, "late_words")
             second_layer(e, values)

@@ -24,14 +24,15 @@ LIST_COLS = C // 16
 LAST = E - 1
 TOKEN_CHUNK = 512
 V_TOKENS = (32, 40)
-CUTS = ((0, 128, 512, 1024, T), (0, 512, 1024, T))
+CUTS = ((0, 256, 608, 1040, T), (0, 448, 960, T))
 LOOKAHEAD = 8
 RAW_BUFS = LOOKAHEAD + 2
 GROUPED_BUFS = 6
 BANK_BUFS = {"w1": 2, "w3": 3}
 EARLY = 2
-V_CLOSING = 32
-V_SHARES = ((0, 0, 64), (0, 48, 64), (128, 40, 48))
+HALF_M = P // 2
+V_CLOSING = (42, 42)
+V_SHARES = ((0, 0, 64), (0, 48, 64), (128, 40, 48), (128, 44, 52))
 
 
 def tile_moe_res_glu_gelu_kernel(tc, xT, xr, w1, w3, w2, gate, offs, out):
@@ -42,6 +43,7 @@ def tile_moe_res_glu_gelu_kernel(tc, xT, xr, w1, w3, w2, gate, offs, out):
         tc.tile_pool(name="grp", bufs=GROUPED_BUFS) as grp,
         tc.tile_pool(name="codes", bufs=2) as codes,
         tc.tile_pool(name="work", bufs=2) as work,
+        tc.tile_pool(name="tail", bufs=1) as tail,
         tc.psum_pool(name="psum", bufs=2) as psum,
     ):
         offsets = held.tile([P, E * LIST_COLS], U16, name="offsets")
@@ -55,7 +57,8 @@ def tile_moe_res_glu_gelu_kernel(tc, xT, xr, w1, w3, w2, gate, offs, out):
 
         chunks = []
         for e in range(E):
-            chunks += [("w1", e, 0), ("w1", e, 1), ("w3", e, 0), ("w3", e, 1), ("w2", e, 0)]
+            closing = [("w3", e, 1)] if e < LAST else [("closing", e, 0), ("closing", e, 1)]
+            chunks += [("w1", e, 0), ("w1", e, 1), ("w3", e, 0)] + closing + [("w2", e, 0)]
         chunks += [("xr", 0, b) for b in range(BLOCKS)]
         pos = {chunk: i for i, chunk in enumerate(chunks)}
         raws, banks, ys, slots = {}, {}, {}, {}
@@ -67,7 +70,10 @@ def tile_moe_res_glu_gelu_kernel(tc, xT, xr, w1, w3, w2, gate, offs, out):
                 raw = rawp.tile([P, T], F32, name="xr_sb", tag="raw", align_bytes=64)
                 nc.sync.dma_start(raw[:], xr[s * P : (s + 1) * P, :])
             else:
-                rows = weights_in[kind][e, s * PASS_K : (s + 1) * PASS_K, :]
+                if kind == "closing":
+                    rows = w3[e, PASS_K:, s * H // 2 : (s + 1) * H // 2]
+                else:
+                    rows = weights_in[kind][e, s * PASS_K : (s + 1) * PASS_K, :]
                 raw = rawp.tile([P, 4, rows.shape[1]], F32, name="raw", tag="raw", align_bytes=64)
                 nc.sync.dma_start(raw[:], rows.rearrange("(p j) i -> p j i", j=4))
             raws[chunks[i]] = raw
@@ -125,14 +131,11 @@ def tile_moe_res_glu_gelu_kernel(tc, xT, xr, w1, w3, w2, gate, offs, out):
         def last_chunk(e):
             chunk = ("w3", e, PASSES - 1)
             src = raws[chunk][:].rearrange("p j (m u v) -> p u m j v", u=2, v=2)
-            first, second = (0, 1) if e == LAST else (1, 0)
+            first, second = 1, 0
             tags = {first: "quantised_first", second: "quantised_second" if e > 0 else "late_words"}
             by_u = [work.tile([P, 2 * H], BF16, name=f"last{u}", tag=tags[u], bufs=1, align_bytes=64) for u in range(2)]
             dst = [part[:].rearrange("p (v m j) -> p m j v", v=2, j=4) for part in by_u]
-            cut = V_CLOSING if e == LAST else 0
-            if cut:
-                nc.vector.tensor_copy(dst[0][:, :cut], src[:, 0, :cut])
-            nc.scalar.copy(dst[0][:, cut:], src[:, 0, cut:])
+            nc.scalar.copy(dst[0], src[:, 0])
             nc.vector.tensor_copy(dst[1], src[:, 1])
             load_ahead(chunk)
             words, scales = new_codes("w3_1", H)
@@ -141,6 +144,28 @@ def tile_moe_res_glu_gelu_kernel(tc, xT, xr, w1, w3, w2, gate, offs, out):
                 nc.vector.quantize_mx(out=words[:, made].bitcast(FP8X4), scales=scales[:, made], in_=by_u[u][:])
             orders = ((0, 1, 2, 3), (2, 3, 0, 1))
             multiply(chunk, words, scales, (orders[first], orders[second]))
+
+        def closing_half(half, words, scales, grouped):
+            chunk = ("closing", LAST, half)
+            dst = grouped[:].rearrange("p (u v m j) -> p m u j v", u=2, v=2, j=4)
+            src = raws[chunk][:].rearrange("p j (m u v) -> p m u j v", u=2, v=2)
+            shared_copy(dst, src, 1, V_CLOSING[half])
+            for t in range(4):
+                made = slice(t * P + half * HALF_M, t * P + (half + 1) * HALF_M)
+                nc.vector.quantize_mx(
+                    out=words[:, made].bitcast(FP8X4), scales=scales[:, made], in_=grouped[:, 4 * t * HALF_M : 4 * (t + 1) * HALF_M]
+                )
+
+        def closing_chunk():
+            words, scales = new_codes("w3_1", H)
+            places = [raws["w3", LAST, 0][:, 3, :], raws["closing", LAST, 1][:, 2:, :].rearrange("p j i -> p (j i)")]
+            values = [place.rearrange("p (c t) -> p c t", t=4) for place in places]
+            nc.scalar.activation(values[0], banks["w1", 0][:].rearrange("p t c -> p c t"), GELU)
+            closing_half(0, words, scales, work.tile([P, 2 * H], BF16, name="closing0", tag="quantised_first", bufs=1, align_bytes=64))
+            closing_half(1, words, scales, tail.tile([P, 2 * H], BF16, name="closing1", align_bytes=64, offset=0))
+            nc.scalar.activation(values[1], banks["w1", 1][:].rearrange("p t c -> p c t"), GELU)
+            multiply(("w3", LAST, 1), words, scales, ((0, 1, 2, 3), (3, 0, 1, 2)))
+            return values
 
         def load_tokens(s):
             raw = held.tile([P, 4, T], F32, name=f"tok_raw{s}")
@@ -181,7 +206,10 @@ def tile_moe_res_glu_gelu_kernel(tc, xT, xr, w1, w3, w2, gate, offs, out):
             return values
 
         def round_w2(engine_copy, e, cols, tag):
-            grouped = work.tile([P, 4 * (cols.stop - cols.start)], BF16, name="w2_grouped", tag=tag, bufs=1, align_bytes=64)[:]
+            if tag is None:
+                grouped = tail.tile([P, 4 * P], BF16, name="w2_closing", align_bytes=64, offset=4 * C)[:]
+            else:
+                grouped = work.tile([P, 4 * (cols.stop - cols.start)], BF16, name="w2_grouped", tag=tag, bufs=1, align_bytes=64)[:]
             engine_copy(
                 grouped.rearrange("p (n pair j) -> p n j pair", pair=2, j=4),
                 raws["w2", e, 0][:, :, cols].rearrange("p j (n pair) -> p n j pair", pair=2),
@@ -192,8 +220,9 @@ def tile_moe_res_glu_gelu_kernel(tc, xT, xr, w1, w3, w2, gate, offs, out):
             if e < LAST:
                 grouped = round_w2(nc.vector.tensor_copy, e, slice(0, N), "quantised_second" if e > 0 else "late_bytes")
             else:
-                grouped = round_w2(nc.vector.tensor_copy, e, slice(0, P), "quantised_second")
                 grouped_late = round_w2(nc.scalar.copy, e, slice(P, N), "w2_late")
+                put_back(e - 1, 0, tail.tile([P, C], F32, name="staged_closing", align_bytes=64, offset=0)[:])
+                grouped = round_w2(nc.vector.tensor_copy, e, slice(0, P), None)
             load_ahead(("w2", e, 0))
             h = work.tile([P, 2, SLOT_HALF, 4], BF16, name="h", tag="h", bufs=1, align_bytes=64)[:]
             for half in range(2):
@@ -263,14 +292,18 @@ def tile_moe_res_glu_gelu_kernel(tc, xT, xr, w1, w3, w2, gate, offs, out):
         gather(1, tok_words[1], U32, 0, EARLY, "words1")
         gather("bytes", tok_bytes, U8, 0, EARLY, "bytes")
         for e in range(E):
-            for chunk, share in zip(chunks[5 * e : 5 * e + 3], V_SHARES[min(e, 2)]):
+            for chunk, share in zip(chunks[5 * e : 5 * e + 3], V_SHARES[e]):
                 first_layer(chunk, share)
-            last_chunk(e)
-            values = gelu(e)
+            if e < LAST:
+                last_chunk(e)
+                values = gelu(e)
+            else:
+                values = closing_chunk()
             if e > 0:
-                staged = work.tile([P, BLOCKS, C], F32, name="staged_late", tag="quantised_first", bufs=1, align_bytes=64)
-                for b in range(BLOCKS if e < LAST else 1):
-                    put_back(e - 1, b, staged[:, b, :])
+                if e < LAST:
+                    staged = work.tile([P, BLOCKS, C], F32, name="staged_late", tag="quantised_first", bufs=1, align_bytes=64)
+                    for b in range(BLOCKS):
+                        put_back(e - 1, b, staged[:, b, :])
             else:
                 gather(1, tok_words[1], U32, EARLY, E, "late_words")
             second_layer(e, values)

@@ -31,7 +31,7 @@ GROUPED_BUFS = 6
 BANK_BUFS = {"w1": 2, "w3": 3}
 EARLY = 2
 HALF_M = P // 2
-V_CLOSING = (42, 42)
+V_CLOSING = (42, 20)
 V_SHARES = ((0, 0, 64), (0, 48, 64), (128, 40, 48), (128, 44, 52))
 
 
@@ -145,24 +145,33 @@ def tile_moe_res_glu_gelu_kernel(tc, xT, xr, w1, w3, w2, gate, offs, out):
             orders = ((0, 1, 2, 3), (2, 3, 0, 1))
             multiply(chunk, words, scales, (orders[first], orders[second]))
 
-        def closing_half(half, words, scales, grouped):
-            chunk = ("closing", LAST, half)
-            dst = grouped[:].rearrange("p (u v m j) -> p m u j v", u=2, v=2, j=4)
-            src = raws[chunk][:].rearrange("p j (m u v) -> p m u j v", u=2, v=2)
-            shared_copy(dst, src, 1, V_CLOSING[half])
-            for t in range(4):
+        def quantize_half(half, words, scales, by_t):
+            for t, grouped in enumerate(by_t):
                 made = slice(t * P + half * HALF_M, t * P + (half + 1) * HALF_M)
-                nc.vector.quantize_mx(
-                    out=words[:, made].bitcast(FP8X4), scales=scales[:, made], in_=grouped[:, 4 * t * HALF_M : 4 * (t + 1) * HALF_M]
-                )
+                nc.vector.quantize_mx(out=words[:, made].bitcast(FP8X4), scales=scales[:, made], in_=grouped)
+
+        def closing_first(words, scales):
+            grouped = work.tile([P, 2 * H], BF16, name="closing0", tag="quantised_first", bufs=1, align_bytes=64)
+            dst = grouped[:].rearrange("p (u v m j) -> p m u j v", u=2, v=2, j=4)
+            src = raws["closing", LAST, 0][:].rearrange("p j (m u v) -> p m u j v", u=2, v=2)
+            shared_copy(dst, src, 1, V_CLOSING[0])
+            quantize_half(0, words, scales, [grouped[:, 4 * t * HALF_M : 4 * (t + 1) * HALF_M] for t in range(4)])
+
+        def closing_second(words, scales):
+            by_u = [tail.tile([P, H], BF16, name=f"closing1_{u}", align_bytes=64, offset=2 * H * u) for u in range(2)]
+            dst = [part[:].rearrange("p (v m j) -> p m j v", v=2, j=4) for part in by_u]
+            src = raws["closing", LAST, 1][:].rearrange("p j (m u v) -> p u m j v", u=2, v=2)
+            nc.vector.tensor_copy(dst[0], src[:, 0])
+            shared_copy(dst[1], src[:, 1], 1, V_CLOSING[1])
+            quantize_half(1, words, scales, [by_u[t // 2][:, 4 * (t % 2) * HALF_M : 4 * (t % 2 + 1) * HALF_M] for t in range(4)])
 
         def closing_chunk():
             words, scales = new_codes("w3_1", H)
             places = [raws["w3", LAST, 0][:, 3, :], raws["closing", LAST, 1][:, 2:, :].rearrange("p j i -> p (j i)")]
             values = [place.rearrange("p (c t) -> p c t", t=4) for place in places]
             nc.scalar.activation(values[0], banks["w1", 0][:].rearrange("p t c -> p c t"), GELU)
-            closing_half(0, words, scales, work.tile([P, 2 * H], BF16, name="closing0", tag="quantised_first", bufs=1, align_bytes=64))
-            closing_half(1, words, scales, tail.tile([P, 2 * H], BF16, name="closing1", align_bytes=64, offset=0))
+            closing_first(words, scales)
+            closing_second(words, scales)
             nc.scalar.activation(values[1], banks["w1", 1][:].rearrange("p t c -> p c t"), GELU)
             multiply(("w3", LAST, 1), words, scales, ((0, 1, 2, 3), (3, 0, 1, 2)))
             return values

@@ -32,7 +32,7 @@ BANK_BUFS = {"w1": 2, "w3": 3}
 EARLY = 2
 HALF_M = P // 2
 V_CLOSING = (42, 20)
-V_SHARES = ((0, 0, 64), (0, 48, 64), (128, 40, 48), (128, 44, 52))
+V_SHARES = ((0, 0, 64), (0, 48, 64), (128, 40, 48), (128, 52, 60))
 
 
 def tile_moe_res_glu_gelu_kernel(tc, xT, xr, w1, w3, w2, gate, offs, out):
@@ -216,7 +216,7 @@ def tile_moe_res_glu_gelu_kernel(tc, xT, xr, w1, w3, w2, gate, offs, out):
 
         def round_w2(engine_copy, e, cols, tag):
             if tag is None:
-                grouped = tail.tile([P, 4 * P], BF16, name="w2_closing", align_bytes=64, offset=4 * C)[:]
+                grouped = tail.tile([P, 4 * P], BF16, name="w2_closing", align_bytes=64, offset=3 * H)[:]
             else:
                 grouped = work.tile([P, 4 * (cols.stop - cols.start)], BF16, name="w2_grouped", tag=tag, bufs=1, align_bytes=64)[:]
             engine_copy(
@@ -230,7 +230,7 @@ def tile_moe_res_glu_gelu_kernel(tc, xT, xr, w1, w3, w2, gate, offs, out):
                 grouped = round_w2(nc.vector.tensor_copy, e, slice(0, N), "quantised_second" if e > 0 else "late_bytes")
             else:
                 grouped_late = round_w2(nc.scalar.copy, e, slice(P, N), "w2_late")
-                put_back(e - 1, 0, tail.tile([P, C], F32, name="staged_closing", align_bytes=64, offset=0)[:])
+                put_back(e - 1, 0, tail.tile([P, C], F32, name="staged_closing", align_bytes=64, offset=H)[:])
                 grouped = round_w2(nc.vector.tensor_copy, e, slice(0, P), None)
             load_ahead(("w2", e, 0))
             h = work.tile([P, 2, SLOT_HALF, 4], BF16, name="h", tag="h", bufs=1, align_bytes=64)[:]

@@ -58,7 +58,8 @@ def tile_moe_res_glu_gelu_kernel(tc, xT, xr, w1, w3, w2, gate, offs, out):
         chunks = []
         for e in range(E):
             closing = [("w3", e, 1)] if e < LAST else [("closing", e, 0), ("closing", e, 1)]
-            chunks += [("w1", e, 0), ("w1", e, 1), ("w3", e, 0)] + closing + [("w2", e, 0)]
+            second = [("w2", e, 0)] if e < LAST else [("w2_half", e, 0), ("w2_half", e, 1)]
+            chunks += [("w1", e, 0), ("w1", e, 1), ("w3", e, 0)] + closing + second
         chunks += [("xr", 0, b) for b in range(BLOCKS)]
         pos = {chunk: i for i, chunk in enumerate(chunks)}
         raws, banks, ys, slots = {}, {}, {}, {}
@@ -72,6 +73,8 @@ def tile_moe_res_glu_gelu_kernel(tc, xT, xr, w1, w3, w2, gate, offs, out):
             else:
                 if kind == "closing":
                     rows = w3[e, PASS_K:, s * H // 2 : (s + 1) * H // 2]
+                elif kind == "w2_half":
+                    rows = w2[e, :, s * P : (s + 1) * P]
                 else:
                     rows = weights_in[kind][e, s * PASS_K : (s + 1) * PASS_K, :]
                 raw = rawp.tile([P, 4, rows.shape[1]], F32, name="raw", tag="raw", align_bytes=64)
@@ -221,7 +224,7 @@ def tile_moe_res_glu_gelu_kernel(tc, xT, xr, w1, w3, w2, gate, offs, out):
                 grouped = work.tile([P, 4 * (cols.stop - cols.start)], BF16, name="w2_grouped", tag=tag, bufs=1, align_bytes=64)[:]
             engine_copy(
                 grouped.rearrange("p (n pair j) -> p n j pair", pair=2, j=4),
-                raws["w2", e, 0][:, :, cols].rearrange("p j (n pair) -> p n j pair", pair=2),
+                (raws["w2", e, 0] if e < LAST else raws["w2_half", e, cols.start // P])[:].rearrange("p j (n pair) -> p n j pair", pair=2),
             )
             return grouped
 
@@ -232,7 +235,8 @@ def tile_moe_res_glu_gelu_kernel(tc, xT, xr, w1, w3, w2, gate, offs, out):
                 grouped_late = round_w2(nc.scalar.copy, e, slice(P, N), "w2_late")
                 put_back(e - 1, 0, tail.tile([P, C], F32, name="staged_closing", align_bytes=64, offset=H)[:])
                 grouped = round_w2(nc.vector.tensor_copy, e, slice(0, P), None)
-            load_ahead(("w2", e, 0))
+            if e < LAST:
+                load_ahead(("w2", e, 0))
             h = work.tile([P, 2, SLOT_HALF, 4], BF16, name="h", tag="h", bufs=1, align_bytes=64)[:]
             for half in range(2):
                 nc.vector.tensor_tensor(h[:, half], banks["w3", half][:].rearrange("p t c -> p c t"), values[half], MULT)

@@ -24,7 +24,8 @@ LIST_COLS = C // 16
 LAST = E - 1
 TOKEN_CHUNK = 512
 V_TOKENS = (32, 40)
-CUTS = ((0, 256, 608, 1040, T), (0, 448, 960, T))
+CUTS = ((0, 256, 640, 1088, T), (0, 448, 960, T))
+DMA_ALIGN = 256
 LOOKAHEAD = 8
 RAW_BUFS = LOOKAHEAD + 2
 GROUPED_BUFS = 6
@@ -68,7 +69,7 @@ def tile_moe_res_glu_gelu_kernel(tc, xT, xr, w1, w3, w2, gate, offs, out):
         def load(i):
             kind, e, s = chunks[i]
             if kind == "xr":
-                raw = rawp.tile([P, T], F32, name="xr_sb", tag="raw", align_bytes=64)
+                raw = rawp.tile([P, T], F32, name="xr_sb", tag="raw", align_bytes=DMA_ALIGN)
                 nc.sync.dma_start(raw[:], xr[s * P : (s + 1) * P, :])
             else:
                 if kind == "closing":
@@ -77,7 +78,7 @@ def tile_moe_res_glu_gelu_kernel(tc, xT, xr, w1, w3, w2, gate, offs, out):
                     rows = w2[e, :, s * P : (s + 1) * P]
                 else:
                     rows = weights_in[kind][e, s * PASS_K : (s + 1) * PASS_K, :]
-                raw = rawp.tile([P, 4, rows.shape[1]], F32, name="raw", tag="raw", align_bytes=64)
+                raw = rawp.tile([P, 4, rows.shape[1]], F32, name="raw", tag="raw", align_bytes=DMA_ALIGN)
                 nc.sync.dma_start(raw[:], rows.rearrange("(p j) i -> p j i", j=4))
             raws[chunks[i]] = raw
 
@@ -180,7 +181,7 @@ def tile_moe_res_glu_gelu_kernel(tc, xT, xr, w1, w3, w2, gate, offs, out):
             return values
 
         def load_tokens(s):
-            raw = held.tile([P, 4, T], F32, name=f"tok_raw{s}")
+            raw = held.tile([P, 4, T], F32, name=f"tok_raw{s}", align_bytes=DMA_ALIGN)
             nc.sync.dma_start(raw[:], xT[s * PASS_K : (s + 1) * PASS_K, :].rearrange("(p j) x -> p j x", j=4))
             return raw
 

@@ -122,8 +122,23 @@ def tile_moe_res_glu_gelu_kernel(tc, xT, xr, w1, w3, w2, gate, offs, out):
                         stop=(s, t) == (PASSES - 1, tiles[half][-1]),
                     )
 
+        def vector_alone(chunk):
+            kind, e, s = chunk
+            src = raws[chunk][:].rearrange("p j (m u v) -> p u m j v", u=2, v=2)
+            by_u = [grp.tile([P, 2 * H], BF16, name="grouped", align_bytes=64) for u in range(2)]
+            for u in range(2):
+                nc.vector.tensor_copy(by_u[u][:].rearrange("p (v m j) -> p m j v", v=2, j=4), src[:, u])
+            load_ahead(chunk)
+            words, scales = new_codes(f"{kind}_{s}", H)
+            for u in range(2):
+                made = slice(u * H // 2, (u + 1) * H // 2)
+                nc.vector.quantize_mx(out=words[:, made].bitcast(FP8X4), scales=scales[:, made], in_=by_u[u][:])
+            multiply(chunk, words, scales, (range(4), range(4)))
+
         def first_layer(chunk, vector_cols):
             kind, e, s = chunk
+            if vector_cols == P:
+                return vector_alone(chunk)
             grouped = grp.tile([P, 4 * H], BF16, name="grouped", align_bytes=64)
             dst = grouped[:].rearrange("p (u v m j) -> p m u j v", u=2, v=2, j=4)
             src = raws[chunk][:].rearrange("p j (m u v) -> p m u j v", u=2, v=2)
@@ -234,7 +249,7 @@ def tile_moe_res_glu_gelu_kernel(tc, xT, xr, w1, w3, w2, gate, offs, out):
                 grouped = round_w2(nc.vector.tensor_copy, e, slice(0, N), "quantised_second" if e > 0 else "late_bytes")
             else:
                 grouped_late = round_w2(nc.scalar.copy, e, slice(P, N), "w2_late")
-                put_back(e - 1, 0, tail.tile([P, C], F32, name="staged_closing", align_bytes=64, offset=H)[:])
+                put_back(e - 1, 0, tail.tile([P, C], F32, name="staged_closing", align_bytes=64, offset=0)[:])
                 grouped = round_w2(nc.vector.tensor_copy, e, slice(0, P), None)
             if e < LAST:
                 load_ahead(("w2", e, 0))

@@ -1,3 +1,5 @@
+import math
+
 import concourse.mybir as mybir
 from concourse.masks import make_identity
 
@@ -26,22 +28,25 @@ TOKEN_CHUNK = 512
 V_TOKENS = (32, 40)
 CUTS = ((0, 256, 640, 1088, T), (0, 448, 960, T))
 DMA_ALIGN = 256
-LOOKAHEAD = 8
-RAW_BUFS = LOOKAHEAD + 2
-GROUPED_BUFS = 6
+RING_BYTES = 120 * 1024
+LINK = 2
+PROMPT = ((), (0,), ())
 BANK_BUFS = {"w1": 2, "w3": 3}
 EARLY = 2
 HALF_M = P // 2
 V_CLOSING = (42, 20)
-V_SHARES = ((0, 0, 64), (0, 48, 64), (128, 40, 48), (128, 52, 60))
+WHOLE = ((0, H),)
+HALVES = ((0, H // 2), (H // 2, H))
+IN_TURN = (range(4), range(4))
+V_SHARES = ((0, 0, 64), (0, 48, 64), (128, 128, 64), (80, 80, 60))
 
 
 def tile_moe_res_glu_gelu_kernel(tc, xT, xr, w1, w3, w2, gate, offs, out):
     nc = tc.nc
     with (
         tc.tile_pool(name="held", bufs=1) as held,
-        tc.tile_pool(name="rawp", bufs=RAW_BUFS) as rawp,
-        tc.tile_pool(name="grp", bufs=GROUPED_BUFS) as grp,
+        tc.tile_pool(name="rawp", bufs=1) as rawp,
+        tc.tile_pool(name="grp", bufs=2) as grp,
         tc.tile_pool(name="codes", bufs=2) as codes,
         tc.tile_pool(name="work", bufs=2) as work,
         tc.tile_pool(name="tail", bufs=1) as tail,
@@ -56,35 +61,38 @@ def tile_moe_res_glu_gelu_kernel(tc, xT, xr, w1, w3, w2, gate, offs, out):
         identity = held.tile([P, P], F32, name="identity")
         win = [held.tile([P, T], F32, name=f"win{b}") for b in range(BLOCKS)]
 
-        chunks = []
-        for e in range(E):
-            closing = [("w3", e, 1)] if e < LAST else [("closing", e, 0), ("closing", e, 1)]
-            second = [("w2", e, 0)] if e < LAST else [("w2_half", e, 0), ("w2_half", e, 1)]
-            chunks += [("w1", e, 0), ("w1", e, 1), ("w3", e, 0)] + closing + second
-        chunks += [("xr", 0, b) for b in range(BLOCKS)]
-        pos = {chunk: i for i, chunk in enumerate(chunks)}
         raws, banks, ys, slots = {}, {}, {}, {}
-        weights_in = {"w1": w1, "w3": w3, "w2": w2}
+        grouped = {}
+        ring = [0]
 
-        def load(i):
-            kind, e, s = chunks[i]
-            if kind == "xr":
-                raw = rawp.tile([P, T], F32, name="xr_sb", tag="raw", align_bytes=DMA_ALIGN)
-                nc.sync.dma_start(raw[:], xr[s * P : (s + 1) * P, :])
-            else:
-                if kind == "closing":
-                    rows = w3[e, PASS_K:, s * H // 2 : (s + 1) * H // 2]
-                elif kind == "w2_half":
-                    rows = w2[e, :, s * P : (s + 1) * P]
-                else:
-                    rows = weights_in[kind][e, s * PASS_K : (s + 1) * PASS_K, :]
-                raw = rawp.tile([P, 4, rows.shape[1]], F32, name="raw", tag="raw", align_bytes=DMA_ALIGN)
-                nc.sync.dma_start(raw[:], rows.rearrange("(p j) i -> p j i", j=4))
-            raws[chunks[i]] = raw
+        def staging(name, shape):
+            size = 4 * math.prod(shape[1:])
+            start = ring[0] if ring[0] + size <= RING_BYTES else 0
+            ring[0] = start + size
+            return rawp.tile(shape, F32, name=name, align_bytes=DMA_ALIGN, offset=start)
 
-        def load_ahead(chunk):
-            if pos[chunk] + LOOKAHEAD < len(chunks):
-                load(pos[chunk] + LOOKAHEAD)
+        def load(dst, rows):
+            nc.sync.dma_start(dst, rows.rearrange("(p j) i -> p j i", j=4))
+
+        def load_weights():
+            for e in range(E):
+                raws[e] = staging(f"raw{e}", [P, 4 if e < LAST else 3, 4, H])
+                load(raws[e][:, 0], w1[e, :PASS_K, :])
+                load(raws[e][:, 1], w1[e, PASS_K:, :])
+                load(raws[e][:, 2], w3[e, :PASS_K, :])
+                if e < LAST:
+                    load(raws[e][:, 3], w3[e, PASS_K:, :])
+                    raws["w2", e, 0] = staging(f"raw_w2_{e}", [P, 4, N])
+                    load(raws["w2", e, 0][:], w2[e])
+            for half in range(2):
+                raws["closing", half] = staging(f"raw_closing{half}", [P, 4, H // 2])
+                load(raws["closing", half][:], w3[LAST, PASS_K:, half * H // 2 : (half + 1) * H // 2])
+            for b in range(BLOCKS):
+                raws["w2_half", LAST, b] = staging(f"raw_w2_half{b}", [P, 4, P])
+                load(raws["w2_half", LAST, b][:], w2[LAST, :, b * P : (b + 1) * P])
+            for b in range(BLOCKS):
+                raws["xr", 0, b] = staging(f"xr{b}", [P, T])
+                nc.sync.dma_start(raws["xr", 0, b][:], xr[b * P : (b + 1) * P, :])
 
         def shared_copy(dst, src, axis, cut):
             size = dst.shape[axis]
@@ -94,9 +102,9 @@ def tile_moe_res_glu_gelu_kernel(tc, xT, xr, w1, w3, w2, gate, offs, out):
             if cut < size:
                 nc.scalar.copy(dst[head + (slice(cut, size),)], src[head + (slice(cut, size),)])
 
-        def quantize(name, grouped):
-            words, scales = new_codes(name, grouped.shape[1] // 4)
-            nc.vector.quantize_mx(out=words[:].bitcast(FP8X4), scales=scales[:], in_=grouped)
+        def quantize(name, rounded):
+            words, scales = new_codes(name, rounded.shape[1] // 4)
+            nc.vector.quantize_mx(out=words[:].bitcast(FP8X4), scales=scales[:], in_=rounded)
             return words, scales
 
         def new_codes(name, width):
@@ -122,92 +130,125 @@ def tile_moe_res_glu_gelu_kernel(tc, xT, xr, w1, w3, w2, gate, offs, out):
                         stop=(s, t) == (PASSES - 1, tiles[half][-1]),
                     )
 
-        def vector_alone(chunk):
-            kind, e, s = chunk
-            src = raws[chunk][:].rearrange("p j (m u v) -> p u m j v", u=2, v=2)
-            by_u = [grp.tile([P, 2 * H], BF16, name="grouped", align_bytes=64) for u in range(2)]
-            for u in range(2):
-                nc.vector.tensor_copy(by_u[u][:].rearrange("p (v m j) -> p m j v", v=2, j=4), src[:, u])
-            load_ahead(chunk)
+        def views(e, k, order):
+            dst = grouped[e][:, k].rearrange("p (u v m j) -> " + order, u=2, v=2, j=4)
+            return dst, raws[e][:, k].rearrange("p j (m u v) -> " + order, u=2, v=2)
+
+        def copy_range(engine_copy, e, k, m0, m1):
+            if m0 < m1:
+                dst, src = views(e, k, "p m u j v")
+                engine_copy(dst[:, m0:m1], src[:, m0:m1])
+
+        def copy_half(engine_copy, e, k, u, m0, m1):
+            dst, src = views(e, k, "p u m j v")
+            engine_copy(dst[:, u, m0:m1], src[:, u, m0:m1])
+
+        def link(e, k, m0):
+            dst = grouped[e][:, k : k + 2].rearrange("p s (t m j) -> p s m j t", t=4, j=4)
+            src = raws[e][:, k : k + 2].rearrange("p s j (m t) -> p s m j t", t=4)
+            nc.vector.tensor_copy(dst[:, :, m0 : m0 + LINK], src[:, :, m0 : m0 + LINK])
+
+        def products(e, k, pieces, tiles):
+            kind, s = ("w1", "w3")[k // 2], k % 2
             words, scales = new_codes(f"{kind}_{s}", H)
-            for u in range(2):
-                made = slice(u * H // 2, (u + 1) * H // 2)
-                nc.vector.quantize_mx(out=words[:, made].bitcast(FP8X4), scales=scales[:, made], in_=by_u[u][:])
-            multiply(chunk, words, scales, (range(4), range(4)))
+            for w0, w1_ in pieces:
+                nc.vector.quantize_mx(out=words[:, w0:w1_].bitcast(FP8X4), scales=scales[:, w0:w1_], in_=grouped[e][:, k, 4 * w0 : 4 * w1_])
+            multiply((kind, e, s), words, scales, tiles)
 
-        def first_layer(chunk, vector_cols):
-            kind, e, s = chunk
-            if vector_cols == P:
-                return vector_alone(chunk)
-            grouped = grp.tile([P, 4 * H], BF16, name="grouped", align_bytes=64)
-            dst = grouped[:].rearrange("p (u v m j) -> p m u j v", u=2, v=2, j=4)
-            src = raws[chunk][:].rearrange("p j (m u v) -> p m u j v", u=2, v=2)
-            shared_copy(dst, src, 1, vector_cols)
-            load_ahead(chunk)
-            words, scales = quantize(f"{kind}_{s}", grouped[:])
-            multiply(chunk, words, scales, (range(4), range(4)))
-
-        def last_chunk(e):
-            chunk = ("w3", e, PASSES - 1)
-            src = raws[chunk][:].rearrange("p j (m u v) -> p u m j v", u=2, v=2)
-            first, second = 1, 0
-            tags = {first: "quantised_first", second: "quantised_second" if e > 0 else "late_words"}
+        def first_expert():
+            for k, share in enumerate(V_SHARES[0]):
+                copy_range(nc.vector.tensor_copy, 0, k, 0, share)
+                copy_range(nc.scalar.copy, 0, k, share, P)
+                products(0, k, WHOLE, IN_TURN)
+            src = raws[0][:, 3].rearrange("p j (m u v) -> p u m j v", u=2, v=2)
+            tags = ("late_words", "last_half")
             by_u = [work.tile([P, 2 * H], BF16, name=f"last{u}", tag=tags[u], bufs=1, align_bytes=64) for u in range(2)]
             dst = [part[:].rearrange("p (v m j) -> p m j v", v=2, j=4) for part in by_u]
             nc.scalar.copy(dst[0], src[:, 0])
             nc.vector.tensor_copy(dst[1], src[:, 1])
-            load_ahead(chunk)
             words, scales = new_codes("w3_1", H)
-            for u in (first, second):
+            for u in (1, 0):
                 made = slice(u * H // 2, (u + 1) * H // 2)
                 nc.vector.quantize_mx(out=words[:, made].bitcast(FP8X4), scales=scales[:, made], in_=by_u[u][:])
-            orders = ((0, 1, 2, 3), (2, 3, 0, 1))
-            multiply(chunk, words, scales, (orders[first], orders[second]))
+            multiply(("w3", 0, 1), words, scales, ((2, 3, 0, 1), (0, 1, 2, 3)))
 
-        def quantize_half(half, words, scales, by_t):
-            for t, grouped in enumerate(by_t):
-                made = slice(t * P + half * HALF_M, t * P + (half + 1) * HALF_M)
-                nc.vector.quantize_mx(out=words[:, made].bitcast(FP8X4), scales=scales[:, made], in_=grouped)
+        def three_chunks(e):
+            first, second, third = V_SHARES[e]
+            if e == LAST:
+                copy_range(nc.vector.tensor_copy, e, 0, LINK, first)
+                copy_range(nc.scalar.copy, e, 0, first, P)
+                link(e, 0, 0)
+                copy_range(nc.vector.tensor_copy, e, 1, LINK, second)
+                copy_range(nc.scalar.copy, e, 1, second, P)
+                products(e, 0, WHOLE, IN_TURN)
+                products(e, 1, WHOLE, IN_TURN)
+                copy_range(nc.vector.tensor_copy, e, 2, 0, third)
+                copy_range(nc.scalar.copy, e, 2, third, P)
+                products(e, 2, WHOLE, IN_TURN)
+                return
+            if first == P:
+                for u in range(2):
+                    copy_half(nc.vector.tensor_copy, e, 0, u, 0, P)
+                prompt(e - 1)
+                products(e, 0, HALVES, IN_TURN)
+            else:
+                copy_range(nc.vector.tensor_copy, e, 0, 0, first)
+                copy_range(nc.scalar.copy, e, 0, first, P)
+                products(e, 0, WHOLE, IN_TURN)
+            copy_range(nc.vector.tensor_copy, e, 1, LINK, second)
+            copy_range(nc.scalar.copy, e, 1, second, P)
+            link(e, 1, 0)
+            copy_range(nc.vector.tensor_copy, e, 2, LINK, third)
+            copy_range(nc.scalar.copy, e, 2, third, P - LINK)
+            products(e, 1, WHOLE, IN_TURN)
+            link(e, 2, P - LINK)
 
-        def closing_first(words, scales):
-            grouped = work.tile([P, 2 * H], BF16, name="closing0", tag="quantised_first", bufs=1, align_bytes=64)
-            dst = grouped[:].rearrange("p (u v m j) -> p m u j v", u=2, v=2, j=4)
-            src = raws["closing", LAST, 0][:].rearrange("p j (m u v) -> p m u j v", u=2, v=2)
-            shared_copy(dst, src, 1, V_CLOSING[0])
-            quantize_half(0, words, scales, [grouped[:, 4 * t * HALF_M : 4 * (t + 1) * HALF_M] for t in range(4)])
-
-        def closing_second(words, scales):
-            by_u = [tail.tile([P, H], BF16, name=f"closing1_{u}", align_bytes=64, offset=2 * H * u) for u in range(2)]
-            dst = [part[:].rearrange("p (v m j) -> p m j v", v=2, j=4) for part in by_u]
-            src = raws["closing", LAST, 1][:].rearrange("p j (m u v) -> p u m j v", u=2, v=2)
-            nc.vector.tensor_copy(dst[0], src[:, 0])
-            shared_copy(dst[1], src[:, 1], 1, V_CLOSING[1])
-            quantize_half(1, words, scales, [by_u[t // 2][:, 4 * (t % 2) * HALF_M : 4 * (t % 2 + 1) * HALF_M] for t in range(4)])
+        def last_chunk(e):
+            copy_half(nc.scalar.copy, e, 3, 0, 0, P - LINK)
+            copy_half(nc.vector.tensor_copy, e, 3, 1, 0, P - LINK)
+            products(e, 2, WHOLE, IN_TURN)
+            products(e, 3, HALVES[::-1], ((2, 3, 0, 1), (0, 1, 2, 3)))
 
         def closing_chunk():
+            places = [raws[LAST][:, 2, 3, :], raws["closing", 1][:, 2:, :].rearrange("p j i -> p (j i)")]
+            values = [place.rearrange("p (a c t) -> p a c t", a=2, t=4) for place in places]
+            nc.scalar.activation(values[0], sums("w1", 0), GELU)
             words, scales = new_codes("w3_1", H)
-            places = [raws["w3", LAST, 0][:, 3, :], raws["closing", LAST, 1][:, 2:, :].rearrange("p j i -> p (j i)")]
-            values = [place.rearrange("p (c t) -> p c t", t=4) for place in places]
-            nc.scalar.activation(values[0], banks["w1", 0][:].rearrange("p t c -> p c t"), GELU)
-            closing_first(words, scales)
-            closing_second(words, scales)
-            nc.scalar.activation(values[1], banks["w1", 1][:].rearrange("p t c -> p c t"), GELU)
+            first = grouped[LAST][:, 3, : 2 * H]
+            dst = first.rearrange("p (u v m j) -> p m u j v", u=2, v=2, j=4)
+            shared_copy(dst, raws["closing", 0][:].rearrange("p j (m u v) -> p m u j v", u=2, v=2), 1, V_CLOSING[0])
+            by_u = [tail.tile([P, H], BF16, name=f"closing1_{u}", align_bytes=64, offset=2 * H * u) for u in range(2)]
+            dst = [part[:].rearrange("p (v m j) -> p m j v", v=2, j=4) for part in by_u]
+            src = raws["closing", 1][:].rearrange("p j (m u v) -> p u m j v", u=2, v=2)
+            for t in range(4):
+                made = slice(t * P, t * P + HALF_M)
+                nc.vector.quantize_mx(out=words[:, made].bitcast(FP8X4), scales=scales[:, made], in_=first[:, t * C : (t + 1) * C])
+            nc.vector.tensor_copy(dst[0], src[:, 0])
+            shared_copy(dst[1], src[:, 1], 1, V_CLOSING[1])
+            for t in range(4):
+                made = slice(t * P + HALF_M, (t + 1) * P)
+                nc.vector.quantize_mx(out=words[:, made].bitcast(FP8X4), scales=scales[:, made], in_=by_u[t // 2][:, (t % 2) * C : (t % 2 + 1) * C])
+            nc.scalar.activation(values[1], sums("w1", 1), GELU)
             multiply(("w3", LAST, 1), words, scales, ((0, 1, 2, 3), (3, 0, 1, 2)))
             return values
 
+        def sums(kind, half):
+            return banks[kind, half][:].rearrange("p t (a c) -> p a c t", a=2)
+
         def load_tokens(s):
-            raw = held.tile([P, 4, T], F32, name=f"tok_raw{s}", align_bytes=DMA_ALIGN)
-            nc.sync.dma_start(raw[:], xT[s * PASS_K : (s + 1) * PASS_K, :].rearrange("(p j) x -> p j x", j=4))
+            raw = staging(f"tok_raw{s}", [P, 4, T])
+            load(raw[:], xT[s * PASS_K : (s + 1) * PASS_K, :])
             return raw
 
         def quantize_tokens(raw, s):
+            rounded = grp.tile([P, T // TOKEN_CHUNK, TOKEN_CHUNK * 4], BF16, name="rounded", tag="grouped", align_bytes=64)
             for x0 in range(0, T, TOKEN_CHUNK):
                 tokens = slice(x0, x0 + TOKEN_CHUNK)
-                grouped = grp.tile([P, TOKEN_CHUNK * 4], BF16, name="grouped", align_bytes=64)
-                dst = grouped[:].rearrange("p (x pair j) -> p x j pair", pair=2, j=4)
+                piece = rounded[:, x0 // TOKEN_CHUNK]
+                dst = piece.rearrange("p (x pair j) -> p x j pair", pair=2, j=4)
                 src = raw[:, :, tokens].rearrange("p j (x pair) -> p x j pair", pair=2)
                 shared_copy(dst, src, 1, dst.shape[1] * V_TOKENS[s] // 64)
-                nc.vector.quantize_mx(out=tok_words[s][:, tokens].bitcast(FP8X4), scales=tok_bytes[4 * s : P, tokens], in_=grouped[:])
+                nc.vector.quantize_mx(out=tok_words[s][:, tokens].bitcast(FP8X4), scales=tok_bytes[4 * s : P, tokens], in_=piece)
 
         def gather(what, source, dtype, e0, e1, tag):
             got = work.tile([P, (e1 - e0) * C], dtype, name=f"slot_{what}_{e0}", tag=tag, bufs=1, align_bytes=64)
@@ -227,36 +268,31 @@ def tile_moe_res_glu_gelu_kernel(tc, xT, xr, w1, w3, w2, gate, offs, out):
                 nc.scalar.copy(gate_sb[:, c0 * P : (c0 + 4) * P], bank[:].rearrange("p c n -> p (c n)"))
 
         def gelu(e):
-            spent = raws["w3", e, PASSES - 1]
-            values = [spent[:, 3 - half, :].rearrange("p (c t) -> p c t", t=4) for half in range(2)]
+            values = [raws[e][:, 3, 3 - half, :].rearrange("p (a c t) -> p a c t", a=2, t=4) for half in range(2)]
             for half in range(2):
-                nc.scalar.activation(values[half], banks["w1", half][:].rearrange("p t c -> p c t"), GELU)
+                nc.scalar.activation(values[half], sums("w1", half), GELU)
             return values
 
-        def round_w2(engine_copy, e, cols, tag):
-            if tag is None:
-                grouped = tail.tile([P, 4 * P], BF16, name="w2_closing", align_bytes=64, offset=3 * H)[:]
-            else:
-                grouped = work.tile([P, 4 * (cols.stop - cols.start)], BF16, name="w2_grouped", tag=tag, bufs=1, align_bytes=64)[:]
-            engine_copy(
-                grouped.rearrange("p (n pair j) -> p n j pair", pair=2, j=4),
-                (raws["w2", e, 0] if e < LAST else raws["w2_half", e, cols.start // P])[:].rearrange("p j (n pair) -> p n j pair", pair=2),
-            )
-            return grouped
+        def round_w2(engine_copy, rounded, raw):
+            engine_copy(rounded.rearrange("p (n pair j) -> p n j pair", pair=2, j=4), raw[:].rearrange("p j (n pair) -> p n j pair", pair=2))
 
         def second_layer(e, values):
-            if e < LAST:
-                grouped = round_w2(nc.vector.tensor_copy, e, slice(0, N), "quantised_second" if e > 0 else "late_bytes")
+            if e == 0:
+                rounded = work.tile([P, 4 * N], BF16, name="w2_grouped", tag="late_bytes", bufs=1, align_bytes=64)[:]
+                round_w2(nc.vector.tensor_copy, rounded, raws["w2", e, 0])
+            elif e < LAST:
+                rounded = grouped[e][:, 3, : 2 * H]
+                round_w2(nc.vector.tensor_copy, rounded, raws["w2", e, 0])
             else:
-                grouped_late = round_w2(nc.scalar.copy, e, slice(P, N), "w2_late")
+                grouped_late = work.tile([P, 4 * P], BF16, name="w2_late", bufs=1, align_bytes=64)[:]
+                round_w2(nc.scalar.copy, grouped_late, raws["w2_half", e, 1])
                 put_back(e - 1, 0, tail.tile([P, C], F32, name="staged_closing", align_bytes=64, offset=0)[:])
-                grouped = round_w2(nc.vector.tensor_copy, e, slice(0, P), None)
-            if e < LAST:
-                load_ahead(("w2", e, 0))
+                rounded = tail.tile([P, 4 * P], BF16, name="w2_closing", align_bytes=64, offset=3 * H)[:]
+                round_w2(nc.vector.tensor_copy, rounded, raws["w2_half", e, 0])
             h = work.tile([P, 2, SLOT_HALF, 4], BF16, name="h", tag="h", bufs=1, align_bytes=64)[:]
             for half in range(2):
-                nc.vector.tensor_tensor(h[:, half], banks["w3", half][:].rearrange("p t c -> p c t"), values[half], MULT)
-            words, scales = quantize("w2", grouped)
+                nc.vector.tensor_tensor(h[:, half].rearrange("p (a c) t -> p a c t", a=2), sums("w3", half), values[half], MULT)
+            words, scales = quantize("w2", rounded)
             stationary = [(words[:, b * P : (b + 1) * P], scales[:, b * P : (b + 1) * P]) for b in range(words.shape[1] // P)]
             h_words, h_scales = new_codes("h", C)
             width = SLOT_HALF if e == LAST else C
@@ -297,6 +333,10 @@ def tile_moe_res_glu_gelu_kernel(tc, xT, xr, w1, w3, w2, gate, offs, out):
             nc.vector.tensor_tensor(staged, ys[e, b], gate_sb[:, e * C : (e + 1) * C], MULT)
             nc.scalar.activation(window(e, b), staged, COPY)
 
+        def prompt(e):
+            for b in PROMPT[e]:
+                put_back(e, b, work.tile([P, C], F32, name="prompt", bufs=2)[:])
+
         def finish(b):
             xr_sb = raws["xr", 0, b]
             for x0, x1 in zip(CUTS[b], CUTS[b][1:]):
@@ -308,8 +348,7 @@ def tile_moe_res_glu_gelu_kernel(tc, xT, xr, w1, w3, w2, gate, offs, out):
         nc.sync.dma_start(offsets[:], offs)
         nc.sync.dma_start(gate_rows[0:8, :], gate[0].rearrange("(c n) -> c n", c=8))
         tok_raws.append(load_tokens(1))
-        for i in range(LOOKAHEAD):
-            load(i)
+        load_weights()
         nc.gpsimd.memset(tok_bytes[:], 0)
         for b in range(BLOCKS):
             nc.vector.memset(win[b][:], 0.0)
@@ -321,20 +360,21 @@ def tile_moe_res_glu_gelu_kernel(tc, xT, xr, w1, w3, w2, gate, offs, out):
         gather(1, tok_words[1], U32, 0, EARLY, "words1")
         gather("bytes", tok_bytes, U8, 0, EARLY, "bytes")
         for e in range(E):
-            for chunk, share in zip(chunks[5 * e : 5 * e + 3], V_SHARES[e]):
-                first_layer(chunk, share)
-            if e < LAST:
+            grouped[e] = grp.tile([P, 4, 4 * H], BF16, name=f"grouped{e}", tag="grouped", align_bytes=64)
+            if e == 0:
+                first_expert()
+                values = gelu(e)
+                gather(1, tok_words[1], U32, EARLY, E, "late_words")
+            elif e < LAST:
+                three_chunks(e)
                 last_chunk(e)
                 values = gelu(e)
+                staged = grouped[e][:, 3, 2 * H :].bitcast(F32)
+                for b in range(len(PROMPT[e - 1]), BLOCKS):
+                    put_back(e - 1, b, staged[:, b * C : (b + 1) * C])
             else:
+                three_chunks(e)
                 values = closing_chunk()
-            if e > 0:
-                if e < LAST:
-                    staged = work.tile([P, BLOCKS, C], F32, name="staged_late", tag="quantised_first", bufs=1, align_bytes=64)
-                    for b in range(BLOCKS):
-                        put_back(e - 1, b, staged[:, b, :])
-            else:
-                gather(1, tok_words[1], U32, EARLY, E, "late_words")
             second_layer(e, values)
             if e == LAST:
                 plain = work.tile([P, C], F32, name="plain_y", bufs=1)

@@ -38,7 +38,7 @@ V_CLOSING = (42, 20)
 WHOLE = ((0, H),)
 HALVES = ((0, H // 2), (H // 2, H))
 IN_TURN = (range(4), range(4))
-V_SHARES = ((0, 0, 64), (0, 48, 64), (128, 128, 64), (80, 80, 60))
+V_SHARES = ((0, 0, 64), (48, 48, 64), (128, 128, 20), (80, 80, 60))
 
 
 def tile_moe_res_glu_gelu_kernel(tc, xT, xr, w1, w3, w2, gate, offs, out):
@@ -77,8 +77,11 @@ def tile_moe_res_glu_gelu_kernel(tc, xT, xr, w1, w3, w2, gate, offs, out):
         def load_weights():
             for e in range(E):
                 raws[e] = staging(f"raw{e}", [P, 4 if e < LAST else 3, 4, H])
-                load(raws[e][:, 0], w1[e, :PASS_K, :])
-                load(raws[e][:, 1], w1[e, PASS_K:, :])
+                if e < LAST:
+                    nc.sync.dma_start(raws[e][:, 0:2], w1[e].rearrange("(s p j) i -> p s j i", s=PASSES, j=4))
+                else:
+                    load(raws[e][:, 0], w1[e, :PASS_K, :])
+                    load(raws[e][:, 1], w1[e, PASS_K:, :])
                 load(raws[e][:, 2], w3[e, :PASS_K, :])
                 if e < LAST:
                     load(raws[e][:, 3], w3[e, PASS_K:, :])
@@ -195,12 +198,19 @@ def tile_moe_res_glu_gelu_kernel(tc, xT, xr, w1, w3, w2, gate, offs, out):
                 copy_range(nc.vector.tensor_copy, e, 0, 0, first)
                 copy_range(nc.scalar.copy, e, 0, first, P)
                 products(e, 0, WHOLE, IN_TURN)
-            copy_range(nc.vector.tensor_copy, e, 1, LINK, second)
-            copy_range(nc.scalar.copy, e, 1, second, P)
-            link(e, 1, 0)
-            copy_range(nc.vector.tensor_copy, e, 2, LINK, third)
-            copy_range(nc.scalar.copy, e, 2, third, P - LINK)
-            products(e, 1, WHOLE, IN_TURN)
+            if second == P:
+                for u in range(2):
+                    copy_half(nc.vector.tensor_copy, e, 1, u, 0, P)
+                products(e, 1, HALVES, IN_TURN)
+                copy_range(nc.vector.tensor_copy, e, 2, 0, third)
+                copy_range(nc.scalar.copy, e, 2, third, P - LINK)
+            else:
+                copy_range(nc.vector.tensor_copy, e, 1, LINK, second)
+                copy_range(nc.scalar.copy, e, 1, second, P)
+                link(e, 1, 0)
+                copy_range(nc.vector.tensor_copy, e, 2, LINK, third)
+                copy_range(nc.scalar.copy, e, 2, third, P - LINK)
+                products(e, 1, WHOLE, IN_TURN)
             link(e, 2, P - LINK)
 
         def last_chunk(e):

@@ -33,12 +33,11 @@ LINK = 2
 PROMPT = ((), (0,), ())
 BANK_BUFS = {"w1": 2, "w3": 3}
 EARLY = 2
-HALF_M = P // 2
-V_CLOSING = (42, 20)
+V_CLOSING = 84
 WHOLE = ((0, H),)
 HALVES = ((0, H // 2), (H // 2, H))
 IN_TURN = (range(4), range(4))
-V_SHARES = ((0, 0, 64), (48, 48, 64), (128, 128, 20), (80, 80, 60))
+V_SHARES = ((0, 0, 64), (48, 48, 64), (128, 128, 20), (80, 80, 88))
 
 
 def tile_moe_res_glu_gelu_kernel(tc, xT, xr, w1, w3, w2, gate, offs, out):
@@ -49,7 +48,6 @@ def tile_moe_res_glu_gelu_kernel(tc, xT, xr, w1, w3, w2, gate, offs, out):
         tc.tile_pool(name="grp", bufs=2) as grp,
         tc.tile_pool(name="codes", bufs=2) as codes,
         tc.tile_pool(name="work", bufs=2) as work,
-        tc.tile_pool(name="tail", bufs=1) as tail,
         tc.psum_pool(name="psum", bufs=2) as psum,
     ):
         offsets = held.tile([P, E * LIST_COLS], U16, name="offsets")
@@ -76,20 +74,17 @@ def tile_moe_res_glu_gelu_kernel(tc, xT, xr, w1, w3, w2, gate, offs, out):
 
         def load_weights():
             for e in range(E):
-                raws[e] = staging(f"raw{e}", [P, 4 if e < LAST else 3, 4, H])
+                raws[e] = staging(f"raw{e}", [P, 4, 4, H])
                 if e < LAST:
                     nc.sync.dma_start(raws[e][:, 0:2], w1[e].rearrange("(s p j) i -> p s j i", s=PASSES, j=4))
                 else:
                     load(raws[e][:, 0], w1[e, :PASS_K, :])
                     load(raws[e][:, 1], w1[e, PASS_K:, :])
                 load(raws[e][:, 2], w3[e, :PASS_K, :])
+                load(raws[e][:, 3], w3[e, PASS_K:, :])
                 if e < LAST:
-                    load(raws[e][:, 3], w3[e, PASS_K:, :])
                     raws["w2", e, 0] = staging(f"raw_w2_{e}", [P, 4, N])
                     load(raws["w2", e, 0][:], w2[e])
-            for half in range(2):
-                raws["closing", half] = staging(f"raw_closing{half}", [P, 4, H // 2])
-                load(raws["closing", half][:], w3[LAST, PASS_K:, half * H // 2 : (half + 1) * H // 2])
             for b in range(BLOCKS):
                 raws["w2_half", LAST, b] = staging(f"raw_w2_half{b}", [P, 4, P])
                 load(raws["w2_half", LAST, b][:], w2[LAST, :, b * P : (b + 1) * P])
@@ -220,26 +215,13 @@ def tile_moe_res_glu_gelu_kernel(tc, xT, xr, w1, w3, w2, gate, offs, out):
             products(e, 3, HALVES[::-1], ((2, 3, 0, 1), (0, 1, 2, 3)))
 
         def closing_chunk():
-            places = [raws[LAST][:, 2, 3, :], raws["closing", 1][:, 2:, :].rearrange("p j i -> p (j i)")]
-            values = [place.rearrange("p (a c t) -> p a c t", a=2, t=4) for place in places]
+            values = [raws[LAST][:, 2 + half, 3, :].rearrange("p (a c t) -> p a c t", a=2, t=4) for half in range(2)]
             nc.scalar.activation(values[0], sums("w1", 0), GELU)
-            words, scales = new_codes("w3_1", H)
-            first = grouped[LAST][:, 3, : 2 * H]
-            dst = first.rearrange("p (u v m j) -> p m u j v", u=2, v=2, j=4)
-            shared_copy(dst, raws["closing", 0][:].rearrange("p j (m u v) -> p m u j v", u=2, v=2), 1, V_CLOSING[0])
-            by_u = [tail.tile([P, H], BF16, name=f"closing1_{u}", align_bytes=64, offset=2 * H * u) for u in range(2)]
-            dst = [part[:].rearrange("p (v m j) -> p m j v", v=2, j=4) for part in by_u]
-            src = raws["closing", 1][:].rearrange("p j (m u v) -> p u m j v", u=2, v=2)
-            for t in range(4):
-                made = slice(t * P, t * P + HALF_M)
-                nc.vector.quantize_mx(out=words[:, made].bitcast(FP8X4), scales=scales[:, made], in_=first[:, t * C : (t + 1) * C])
-            nc.vector.tensor_copy(dst[0], src[:, 0])
-            shared_copy(dst[1], src[:, 1], 1, V_CLOSING[1])
-            for t in range(4):
-                made = slice(t * P + HALF_M, (t + 1) * P)
-                nc.vector.quantize_mx(out=words[:, made].bitcast(FP8X4), scales=scales[:, made], in_=by_u[t // 2][:, (t % 2) * C : (t % 2 + 1) * C])
+            for u in range(2):
+                copy_half(nc.vector.tensor_copy, LAST, 3, u, 0, V_CLOSING)
+                copy_half(nc.scalar.copy, LAST, 3, u, V_CLOSING, P)
             nc.scalar.activation(values[1], sums("w1", 1), GELU)
-            multiply(("w3", LAST, 1), words, scales, ((0, 1, 2, 3), (3, 0, 1, 2)))
+            products(LAST, 3, ((0, 2 * P), (2 * P, 3 * P), (3 * P, H)), ((0, 1, 2, 3), (3, 0, 1, 2)))
             return values
 
         def sums(kind, half):
@@ -277,8 +259,8 @@ def tile_moe_res_glu_gelu_kernel(tc, xT, xr, w1, w3, w2, gate, offs, out):
                     nc.tensor.transpose(bank[:, c - c0, :], gate_col[:, c : c + 1].to_broadcast([P, P]), identity[:])
                 nc.scalar.copy(gate_sb[:, c0 * P : (c0 + 4) * P], bank[:].rearrange("p c n -> p (c n)"))
 
-        def gelu(e):
-            values = [raws[e][:, 3, 3 - half, :].rearrange("p (a c t) -> p a c t", a=2, t=4) for half in range(2)]
+        def gelu(e, k):
+            values = [raws[e][:, k, 3 - half, :].rearrange("p (a c t) -> p a c t", a=2, t=4) for half in range(2)]
             for half in range(2):
                 nc.scalar.activation(values[half], sums("w1", half), GELU)
             return values
@@ -296,8 +278,8 @@ def tile_moe_res_glu_gelu_kernel(tc, xT, xr, w1, w3, w2, gate, offs, out):
             else:
                 grouped_late = work.tile([P, 4 * P], BF16, name="w2_late", bufs=1, align_bytes=64)[:]
                 round_w2(nc.scalar.copy, grouped_late, raws["w2_half", e, 1])
-                put_back(e - 1, 0, tail.tile([P, C], F32, name="staged_closing", align_bytes=64, offset=0)[:])
-                rounded = tail.tile([P, 4 * P], BF16, name="w2_closing", align_bytes=64, offset=3 * H)[:]
+                put_back(e - 1, 0, grouped[e][:, 3, H : 2 * H].bitcast(F32))
+                rounded = grouped[e][:, 3, 3 * H :]
                 round_w2(nc.vector.tensor_copy, rounded, raws["w2_half", e, 0])
             h = work.tile([P, 2, SLOT_HALF, 4], BF16, name="h", tag="h", bufs=1, align_bytes=64)[:]
             for half in range(2):
@@ -373,12 +355,12 @@ def tile_moe_res_glu_gelu_kernel(tc, xT, xr, w1, w3, w2, gate, offs, out):
             grouped[e] = grp.tile([P, 4, 4 * H], BF16, name=f"grouped{e}", tag="grouped", align_bytes=64)
             if e == 0:
                 first_expert()
-                values = gelu(e)
+                values = gelu(e, 3)
                 gather(1, tok_words[1], U32, EARLY, E, "late_words")
             elif e < LAST:
                 three_chunks(e)
                 last_chunk(e)
-                values = gelu(e)
+                values = gelu(e, 3)
                 staged = grouped[e][:, 3, 2 * H :].bitcast(F32)
                 for b in range(len(PROMPT[e - 1]), BLOCKS):
                     put_back(e - 1, b, staged[:, b * C : (b + 1) * C])

import math

import concourse.mybir as mybir
from concourse.masks import make_identity

K, T, E, C, H, N = 1024, 1536, 4, 256, 512, 256
FLOPS = 2 * E * C * (2 * K * H + H * N)
BYTES = 4 * (K * T + N * T + 2 * E * K * H + E * H * N + E * C + N * T) + 2 * 128 * E * C // 16

F32 = mybir.dt.float32
BF16 = mybir.dt.bfloat16
U32 = mybir.dt.uint32
U16 = mybir.dt.uint16
U8 = mybir.dt.uint8
FP8X4 = mybir.dt.float8_e4m3fn_x4
MULT, ADD = mybir.AluOpType.mult, mybir.AluOpType.add
GELU = mybir.ActivationFunctionType.Gelu_apprx_tanh
COPY = mybir.ActivationFunctionType.Copy

P = 128
PASS_K = 512
PASSES = K // PASS_K
BLOCKS = N // P
SLOT_HALF = 128
LIST_COLS = C // 16
LAST = E - 1
TOKEN_CHUNK = 512
V_TOKENS = (32, 40)
CUTS = ((0, 256, 640, 1088, T), (0, 448, 960, T))
DMA_ALIGN = 256
RING_BYTES = 120 * 1024
LINK = 2
PROMPT = ((), (0,), ())
BANK_BUFS = {"w1": 2, "w3": 3}
EARLY = 2
V_CLOSING = 84
WHOLE = ((0, H),)
HALVES = ((0, H // 2), (H // 2, H))
IN_TURN = (range(4), range(4))
V_SHARES = ((0, 0, 64), (48, 48, 64), (128, 128, 20), (80, 80, 88))


def tile_moe_res_glu_gelu_kernel(tc, xT, xr, w1, w3, w2, gate, offs, out):
    nc = tc.nc
    with (
        tc.tile_pool(name="held", bufs=1) as held,
        tc.tile_pool(name="rawp", bufs=1) as rawp,
        tc.tile_pool(name="grp", bufs=2) as grp,
        tc.tile_pool(name="codes", bufs=2) as codes,
        tc.tile_pool(name="work", bufs=2) as work,
        tc.psum_pool(name="psum", bufs=2) as psum,
    ):
        offsets = held.tile([P, E * LIST_COLS], U16, name="offsets")
        tok_words = [held.tile([P, T], U32, name=f"tok_words{s}", align_bytes=64) for s in range(PASSES)]
        tok_bytes = held.tile([P, T], U8, name="tok_bytes", align_bytes=64)
        gate_sb = held.tile([P, E * C], F32, name="gate_sb")
        gate_rows = held.tile([P, P], F32, name="gate_rows")
        gate_col = held.tile([P, 8], F32, name="gate_col")
        identity = held.tile([P, P], F32, name="identity")
        win = [held.tile([P, T], F32, name=f"win{b}") for b in range(BLOCKS)]

        raws, banks, ys, slots = {}, {}, {}, {}
        grouped = {}
        ring = [0]

        def staging(name, shape):
            size = 4 * math.prod(shape[1:])
            start = ring[0] if ring[0] + size <= RING_BYTES else 0
            ring[0] = start + size
            return rawp.tile(shape, F32, name=name, align_bytes=DMA_ALIGN, offset=start)

        def load(dst, rows):
            nc.sync.dma_start(dst, rows.rearrange("(p j) i -> p j i", j=4))

        def load_weights():
            for e in range(E):
                raws[e] = staging(f"raw{e}", [P, 4, 4, H])
                if e < LAST:
                    nc.sync.dma_start(raws[e][:, 0:2], w1[e].rearrange("(s p j) i -> p s j i", s=PASSES, j=4))
                else:
                    load(raws[e][:, 0], w1[e, :PASS_K, :])
                    load(raws[e][:, 1], w1[e, PASS_K:, :])
                load(raws[e][:, 2], w3[e, :PASS_K, :])
                load(raws[e][:, 3], w3[e, PASS_K:, :])
                if e < LAST:
                    raws["w2", e, 0] = staging(f"raw_w2_{e}", [P, 4, N])
                    load(raws["w2", e, 0][:], w2[e])
            for b in range(BLOCKS):
                raws["w2_half", LAST, b] = staging(f"raw_w2_half{b}", [P, 4, P])
                load(raws["w2_half", LAST, b][:], w2[LAST, :, b * P : (b + 1) * P])
            for b in range(BLOCKS):
                raws["xr", 0, b] = staging(f"xr{b}", [P, T])
                nc.sync.dma_start(raws["xr", 0, b][:], xr[b * P : (b + 1) * P, :])

        def shared_copy(dst, src, axis, cut):
            size = dst.shape[axis]
            head = (slice(None),) * axis
            if cut > 0:
                nc.vector.tensor_copy(dst[head + (slice(0, cut),)], src[head + (slice(0, cut),)])
            if cut < size:
                nc.scalar.copy(dst[head + (slice(cut, size),)], src[head + (slice(cut, size),)])

        def quantize(name, rounded):
            words, scales = new_codes(name, rounded.shape[1] // 4)
            nc.vector.quantize_mx(out=words[:].bitcast(FP8X4), scales=scales[:], in_=rounded)
            return words, scales

        def new_codes(name, width):
            words = codes.tile([P, width], U32, name=name + "_words", align_bytes=64)
            scales = codes.tile([P, width], U8, name=name + "_scales", align_bytes=64)
            return words, scales

        def multiply(chunk, words, scales, tiles):
            kind, e, s = chunk
            for half in range(2):
                if s == 0:
                    banks[kind, half] = psum.tile([P, 4, SLOT_HALF], F32, name=f"bank_{kind}", bufs=BANK_BUFS[kind])
                moving = slice(half * SLOT_HALF, (half + 1) * SLOT_HALF)
                for t in tiles[half]:
                    stationary = slice(t * P, (t + 1) * P)
                    nc.tensor.matmul_mx(
                        out=banks[kind, half][:, t, :],
                        lhsT=words[:, stationary].bitcast(FP8X4),
                        lhsT_scale=scales[:, stationary],
                        rhs=slots[s, e][:, moving].bitcast(FP8X4),
                        rhs_scale=slots["bytes", e][4 * s : P, moving],
                        start=(s, t) == (0, 0),
                        stop=(s, t) == (PASSES - 1, tiles[half][-1]),
                    )

        def views(e, k, order):
            dst = grouped[e][:, k].rearrange("p (u v m j) -> " + order, u=2, v=2, j=4)
            return dst, raws[e][:, k].rearrange("p j (m u v) -> " + order, u=2, v=2)

        def copy_range(engine_copy, e, k, m0, m1):
            if m0 < m1:
                dst, src = views(e, k, "p m u j v")
                engine_copy(dst[:, m0:m1], src[:, m0:m1])

        def copy_half(engine_copy, e, k, u, m0, m1):
            dst, src = views(e, k, "p u m j v")
            engine_copy(dst[:, u, m0:m1], src[:, u, m0:m1])

        def link(e, k, m0):
            dst = grouped[e][:, k : k + 2].rearrange("p s (t m j) -> p s m j t", t=4, j=4)
            src = raws[e][:, k : k + 2].rearrange("p s j (m t) -> p s m j t", t=4)
            nc.vector.tensor_copy(dst[:, :, m0 : m0 + LINK], src[:, :, m0 : m0 + LINK])

        def products(e, k, pieces, tiles):
            kind, s = ("w1", "w3")[k // 2], k % 2
            words, scales = new_codes(f"{kind}_{s}", H)
            for w0, w1_ in pieces:
                nc.vector.quantize_mx(out=words[:, w0:w1_].bitcast(FP8X4), scales=scales[:, w0:w1_], in_=grouped[e][:, k, 4 * w0 : 4 * w1_])
            multiply((kind, e, s), words, scales, tiles)

        def first_expert():
            for k, share in enumerate(V_SHARES[0]):
                copy_range(nc.vector.tensor_copy, 0, k, 0, share)
                copy_range(nc.scalar.copy, 0, k, share, P)
                products(0, k, WHOLE, IN_TURN)
            src = raws[0][:, 3].rearrange("p j (m u v) -> p u m j v", u=2, v=2)
            tags = ("late_words", "last_half")
            by_u = [work.tile([P, 2 * H], BF16, name=f"last{u}", tag=tags[u], bufs=1, align_bytes=64) for u in range(2)]
            dst = [part[:].rearrange("p (v m j) -> p m j v", v=2, j=4) for part in by_u]
            nc.scalar.copy(dst[0], src[:, 0])
            nc.vector.tensor_copy(dst[1], src[:, 1])
            words, scales = new_codes("w3_1", H)
            for u in (1, 0):
                made = slice(u * H // 2, (u + 1) * H // 2)
                nc.vector.quantize_mx(out=words[:, made].bitcast(FP8X4), scales=scales[:, made], in_=by_u[u][:])
            multiply(("w3", 0, 1), words, scales, ((2, 3, 0, 1), (0, 1, 2, 3)))

        def three_chunks(e):
            first, second, third = V_SHARES[e]
            if e == LAST:
                copy_range(nc.vector.tensor_copy, e, 0, LINK, first)
                copy_range(nc.scalar.copy, e, 0, first, P)
                link(e, 0, 0)
                copy_range(nc.vector.tensor_copy, e, 1, LINK, second)
                copy_range(nc.scalar.copy, e, 1, second, P)
                products(e, 0, WHOLE, IN_TURN)
                products(e, 1, WHOLE, IN_TURN)
                copy_range(nc.vector.tensor_copy, e, 2, 0, third)
                copy_range(nc.scalar.copy, e, 2, third, P)
                products(e, 2, WHOLE, IN_TURN)
                return
            if first == P:
                for u in range(2):
                    copy_half(nc.vector.tensor_copy, e, 0, u, 0, P)
                prompt(e - 1)
                products(e, 0, HALVES, IN_TURN)
            else:
                copy_range(nc.vector.tensor_copy, e, 0, 0, first)
                copy_range(nc.scalar.copy, e, 0, first, P)
                products(e, 0, WHOLE, IN_TURN)
            if second == P:
                for u in range(2):
                    copy_half(nc.vector.tensor_copy, e, 1, u, 0, P)
                products(e, 1, HALVES, IN_TURN)
                copy_range(nc.vector.tensor_copy, e, 2, 0, third)
                copy_range(nc.scalar.copy, e, 2, third, P - LINK)
            else:
                copy_range(nc.vector.tensor_copy, e, 1, LINK, second)
                copy_range(nc.scalar.copy, e, 1, second, P)
                link(e, 1, 0)
                copy_range(nc.vector.tensor_copy, e, 2, LINK, third)
                copy_range(nc.scalar.copy, e, 2, third, P - LINK)
                products(e, 1, WHOLE, IN_TURN)
            link(e, 2, P - LINK)

        def last_chunk(e):
            copy_half(nc.scalar.copy, e, 3, 0, 0, P - LINK)
            copy_half(nc.vector.tensor_copy, e, 3, 1, 0, P - LINK)
            products(e, 2, WHOLE, IN_TURN)
            products(e, 3, HALVES[::-1], ((2, 3, 0, 1), (0, 1, 2, 3)))

        def closing_chunk():
            values = [raws[LAST][:, 2 + half, 3, :].rearrange("p (a c t) -> p a c t", a=2, t=4) for half in range(2)]
            nc.scalar.activation(values[0], sums("w1", 0), GELU)
            for u in range(2):
                copy_half(nc.vector.tensor_copy, LAST, 3, u, 0, V_CLOSING)
                copy_half(nc.scalar.copy, LAST, 3, u, V_CLOSING, P)
            nc.scalar.activation(values[1], sums("w1", 1), GELU)
            products(LAST, 3, ((0, 2 * P), (2 * P, 3 * P), (3 * P, H)), ((0, 1, 2, 3), (3, 0, 1, 2)))
            return values

        def sums(kind, half):
            return banks[kind, half][:].rearrange("p t (a c) -> p a c t", a=2)

        def load_tokens(s):
            raw = staging(f"tok_raw{s}", [P, 4, T])
            load(raw[:], xT[s * PASS_K : (s + 1) * PASS_K, :])
            return raw

        def quantize_tokens(raw, s):
            rounded = grp.tile([P, T // TOKEN_CHUNK, TOKEN_CHUNK * 4], BF16, name="rounded", tag="grouped", align_bytes=64)
            for x0 in range(0, T, TOKEN_CHUNK):
                tokens = slice(x0, x0 + TOKEN_CHUNK)
                piece = rounded[:, x0 // TOKEN_CHUNK]
                dst = piece.rearrange("p (x pair j) -> p x j pair", pair=2, j=4)
                src = raw[:, :, tokens].rearrange("p j (x pair) -> p x j pair", pair=2)
                shared_copy(dst, src, 1, dst.shape[1] * V_TOKENS[s] // 64)
                nc.vector.quantize_mx(out=tok_words[s][:, tokens].bitcast(FP8X4), scales=tok_bytes[4 * s : P, tokens], in_=piece)

        def gather(what, source, dtype, e0, e1, tag):
            got = work.tile([P, (e1 - e0) * C], dtype, name=f"slot_{what}_{e0}", tag=tag, bufs=1, align_bytes=64)
            nc.vector.tensor_copy(got[:], source[:].indirect(offsets[:, e0 * LIST_COLS : e1 * LIST_COLS]))
            for e in range(e0, e1):
                slots[what, e] = got[:, (e - e0) * C : (e - e0 + 1) * C]

        def spread_gate():
            make_identity(nc, identity[:])
            turned = psum.tile([P, P], F32, name="gate_turned", tag="y", bufs=3)
            nc.tensor.transpose(turned[:], gate_rows[:], identity[:])
            nc.scalar.copy(gate_col[:], turned[:, :8])
            for c0 in (0, 4):
                bank = psum.tile([P, 4, P], F32, name="gate_bank", tag="y", bufs=3)
                for c in range(c0, c0 + 4):
                    nc.tensor.transpose(bank[:, c - c0, :], gate_col[:, c : c + 1].to_broadcast([P, P]), identity[:])
                nc.scalar.copy(gate_sb[:, c0 * P : (c0 + 4) * P], bank[:].rearrange("p c n -> p (c n)"))

        def gelu(e, k):
            values = [raws[e][:, k, 3 - half, :].rearrange("p (a c t) -> p a c t", a=2, t=4) for half in range(2)]
            for half in range(2):
                nc.scalar.activation(values[half], sums("w1", half), GELU)
            return values

        def round_w2(engine_copy, rounded, raw):
            engine_copy(rounded.rearrange("p (n pair j) -> p n j pair", pair=2, j=4), raw[:].rearrange("p j (n pair) -> p n j pair", pair=2))

        def second_layer(e, values):
            if e == 0:
                rounded = work.tile([P, 4 * N], BF16, name="w2_grouped", tag="late_bytes", bufs=1, align_bytes=64)[:]
                round_w2(nc.vector.tensor_copy, rounded, raws["w2", e, 0])
            elif e < LAST:
                rounded = grouped[e][:, 3, : 2 * H]
                round_w2(nc.vector.tensor_copy, rounded, raws["w2", e, 0])
            else:
                grouped_late = work.tile([P, 4 * P], BF16, name="w2_late", bufs=1, align_bytes=64)[:]
                round_w2(nc.scalar.copy, grouped_late, raws["w2_half", e, 1])
                put_back(e - 1, 0, grouped[e][:, 3, H : 2 * H].bitcast(F32))
                rounded = grouped[e][:, 3, 3 * H :]
                round_w2(nc.vector.tensor_copy, rounded, raws["w2_half", e, 0])
            h = work.tile([P, 2, SLOT_HALF, 4], BF16, name="h", tag="h", bufs=1, align_bytes=64)[:]
            for half in range(2):
                nc.vector.tensor_tensor(h[:, half].rearrange("p (a c) t -> p a c t", a=2), sums("w3", half), values[half], MULT)
            words, scales = quantize("w2", rounded)
            stationary = [(words[:, b * P : (b + 1) * P], scales[:, b * P : (b + 1) * P]) for b in range(words.shape[1] // P)]
            h_words, h_scales = new_codes("h", C)
            width = SLOT_HALF if e == LAST else C
            pieces = [slice(c0, c0 + width) for c0 in range(0, C, width)]
            flat = h.rearrange("p a c t -> p (a c) t")
            for made in pieces:
                nc.vector.quantize_mx(out=h_words[:, made].bitcast(FP8X4), scales=h_scales[:, made], in_=flat[:, made].rearrange("p c t -> p (c t)"))
            if e == LAST:
                words, scales = quantize("w2_late", grouped_late)
                stationary.append((words[:], scales[:]))

            def product(y, b, made):
                nc.tensor.matmul_mx(
                    out=y[:, made],
                    lhsT=stationary[b][0].bitcast(FP8X4),
                    lhsT_scale=stationary[b][1],
                    rhs=h_words[:, made].bitcast(FP8X4),
                    rhs_scale=h_scales[:, made],
                    start=True,
                    stop=True,
                )

            if e < LAST:
                y = psum.tile([P, BLOCKS, C], F32, name="y", tag="y", bufs=3)
                for b in range(BLOCKS):
                    ys[e, b] = y[:, b, :]
            else:
                for b in range(BLOCKS):
                    ys[e, b] = psum.tile([P, C], F32, name=f"y{b}", tag="y", bufs=3)[:]
            for b in range(BLOCKS):
                for made in pieces:
                    product(ys[e, b], b, made)

        def window(e, b):
            return win[b][:].indirect(offsets[:, e * LIST_COLS : (e + 1) * LIST_COLS])

        def put_back(e, b, staged):
            nc.vector.tensor_tensor(staged, ys[e, b], gate_sb[:, e * C : (e + 1) * C], MULT)
            nc.scalar.activation(window(e, b), staged, COPY)

        def prompt(e):
            for b in PROMPT[e]:
                put_back(e, b, work.tile([P, C], F32, name="prompt", bufs=2)[:])

        def finish(b):
            xr_sb = raws["xr", 0, b]
            for x0, x1 in zip(CUTS[b], CUTS[b][1:]):
                nc.vector.tensor_tensor(xr_sb[:, x0:x1], win[b][:, x0:x1], xr_sb[:, x0:x1], ADD)
                nc.sync.dma_start(out[b * P : (b + 1) * P, x0:x1], xr_sb[:, x0:x1])

        nc.vector.memset(gate_rows[:], 0.0)
        tok_raws = [load_tokens(0)]
        nc.sync.dma_start(offsets[:], offs)
        nc.sync.dma_start(gate_rows[0:8, :], gate[0].rearrange("(c n) -> c n", c=8))
        tok_raws.append(load_tokens(1))
        load_weights()
        nc.gpsimd.memset(tok_bytes[:], 0)
        for b in range(BLOCKS):
            nc.vector.memset(win[b][:], 0.0)

        quantize_tokens(tok_raws[0], 0)
        spread_gate()
        gather(0, tok_words[0], U32, 0, E, "words0")
        quantize_tokens(tok_raws[1], 1)
        gather(1, tok_words[1], U32, 0, EARLY, "words1")
        gather("bytes", tok_bytes, U8, 0, EARLY, "bytes")
        for e in range(E):
            grouped[e] = grp.tile([P, 4, 4 * H], BF16, name=f"grouped{e}", tag="grouped", align_bytes=64)
            if e == 0:
                first_expert()
                values = gelu(e, 3)
                gather(1, tok_words[1], U32, EARLY, E, "late_words")
            elif e < LAST:
                three_chunks(e)
                last_chunk(e)
                values = gelu(e, 3)
                staged = grouped[e][:, 3, 2 * H :].bitcast(F32)
                for b in range(len(PROMPT[e - 1]), BLOCKS):
                    put_back(e - 1, b, staged[:, b * C : (b + 1) * C])
            else:
                three_chunks(e)
                values = closing_chunk()
            second_layer(e, values)
            if e == LAST:
                plain = work.tile([P, C], F32, name="plain_y", bufs=1)
                nc.scalar.copy(plain[:], ys[LAST, 0])
                put_back(e - 1, 1, work.tile([P, C], F32, name="staged_last", tag="h", bufs=1, align_bytes=64)[:])
            if e == 0:
                gather("bytes", tok_bytes, U8, EARLY, E, "late_bytes")
        put_back(LAST, 1, work.tile([P, C], F32, name="staged", bufs=1)[:])
        nc.vector.tensor_tensor(window(LAST, 0), plain[:], gate_sb[:, LAST * C :], MULT)
        for b in range(BLOCKS):
            finish(b)
